import numpy as np
import ml_dtypes


def mxq(x, axis, fmt="e4m3"):
    dtype, down = {"e4m3": (ml_dtypes.float8_e4m3fn, 7), "e5m2": (ml_dtypes.float8_e5m2, 14)}[fmt]
    v = np.moveaxis(np.asarray(x, np.float32).astype(ml_dtypes.bfloat16).astype(np.float64), axis, -1)
    blocks = v.reshape(v.shape[:-1] + (-1, 32))
    amax = np.abs(blocks).max(-1, keepdims=True)
    byte = np.maximum(np.where(amax > 0, np.frexp(amax)[1] - 1 + 127, 0) - down, 1)
    scale = np.exp2(byte - 127.0)
    codes = (blocks / scale).astype(np.float32).astype(dtype).astype(np.float64)
    return np.moveaxis((codes * scale).reshape(v.shape), -1, axis)


WIDE = False


def mx_kscale(k):
    if not WIDE:
        return np.ones(k)
    levels = np.array([10, -10, 5, -5, 0])
    if k % 512:
        return np.exp2(np.random.permutation(np.resize(levels, k // 32))).repeat(32)
    a = np.empty((k // 512, 16))
    for p in range(k // 512):
        a[p, :8] = np.random.permutation(np.resize(levels, 8))
        for g in range(8):
            far = levels[np.abs(levels - a[p, g]) >= 10]
            a[p, g + 8] = far[np.random.randint(len(far))]
    return np.exp2(a.ravel()).repeat(32)


def f64(x):
    return np.asarray(x).astype(np.float64)


def striped(idx):
    return np.tile(idx.reshape(-1, 16).T, (8, 1)).astype(np.uint16)


def unstriped(offs):
    return offs[:16].T.reshape(-1).astype(np.int64)


E2M1 = np.array([0.0, 0.5, 1.0, 1.5, 2.0, 3.0, 4.0, 6.0, -0.0, -0.5, -1.0, -1.5, -2.0, -3.0, -4.0, -6.0])


def pack_weight(w, fmt):
    k, n = w.shape
    w = f64(np.asarray(w, np.float32).astype(ml_dtypes.bfloat16)).reshape(k // 32, 32, n)
    amax = np.abs(w).max(1)
    if fmt == "e4m3":
        byte = np.frexp(amax)[1] - 1 + 127 - 7
    else:
        mant, ex = np.frexp(amax / 6.0)
        byte = np.where(mant > 0.5, ex, ex - 1) + 127
    byte = np.clip(np.where(amax > 0, byte, 1), 1, 254)
    scaled = (w * np.exp2(127.0 - byte)[:, None, :]).reshape(k, n).astype(np.float32)
    by_word = np.ascontiguousarray(scaled.reshape(k // 512, 128, 4, n).transpose(0, 1, 3, 2))
    if fmt == "e4m3":
        words = by_word.astype(ml_dtypes.float8_e4m3fn).view(np.uint8)
    else:
        c = by_word.astype(ml_dtypes.float4_e2m1fn).view(np.uint8) & 0xF
        words = (c[..., 0::2] | (c[..., 1::2] << 4)).reshape(k // 512, 128, 2 * n)
    return np.ascontiguousarray(words), np.ascontiguousarray(byte.astype(np.uint8).reshape(k // 512, 16, n))


def unpack_weight(words, scales, fmt):
    g, _, n = scales.shape
    words = np.ascontiguousarray(words).reshape(g, 128, n, -1)
    if fmt == "e4m3":
        vals = words.view(ml_dtypes.float8_e4m3fn).astype(np.float64)
    else:
        nib = np.empty((g, 128, n, 4), np.uint8)
        nib[..., 0::2] = words & 0xF
        nib[..., 1::2] = words >> 4
        vals = E2M1[nib]
    vals = vals * np.repeat(np.exp2(scales.astype(np.float64) - 127.0), 8, axis=1)[..., None]
    return vals.transpose(0, 1, 3, 2).reshape(g * 512, n)


def silu(v):
    return v / (1.0 + np.exp(-np.maximum(v, -700.0)))


K, T, E, C, H, N = 512, 1024, 4, 256, 512, 512


def by_expert(wq, xq):
    return np.concatenate([wq[e].T @ xq[:, e * C:(e + 1) * C] for e in range(E)], axis=1)


def setup_inputs():
    n = np.random.standard_normal
    s = mx_kscale(K)
    u = mx_kscale(H)
    slot_token = np.random.permutation(T)[:E * C]
    x = pack_weight(n((K, T)) * s[:, None], "e4m3")
    w = pack_weight(n((K, N)) / np.sqrt(K) / s[:, None], "e2m1")
    wa = [pack_weight(m, "e4m3") for m in n((E, K, H)) / np.sqrt(K) / s[None, :, None] * u]
    wb = [pack_weight(m, "e4m3") for m in n((E, H, N)) / np.sqrt(H) / u[None, :, None]]
    return {
        "x_words": x[0],
        "x_scales": x[1],
        "w_words": w[0],
        "w_scales": w[1],
        "wa_words": np.stack([m[0] for m in wa]),
        "wa_scales": np.stack([m[1] for m in wa]),
        "wb_words": np.stack([m[0] for m in wb]),
        "wb_scales": np.stack([m[1] for m in wb]),
        "gate": np.tile(np.random.uniform(0.2, 1.0, E * C), (128, 1)).astype(np.float32),
        "offs": striped(slot_token),
    }


def reference(x_words, x_scales, w_words, w_scales, wa_words, wa_scales, wb_words, wb_scales, gate, offs):
    w = unpack_weight(w_words, w_scales, "e2m1")
    wa = np.stack([unpack_weight(wa_words[e], wa_scales[e], "e4m3") for e in range(E)])
    wb = np.stack([unpack_weight(wb_words[e], wb_scales[e], "e4m3") for e in range(E)])
    idx = unstriped(offs)
    x = unpack_weight(x_words, x_scales, "e4m3")
    base = w.T @ x
    h = silu(by_expert(wa, x[:, idx]))
    y = by_expert(wb, mxq(h, 0, "e4m3"))
    c = np.zeros((N, T))
    c[:, idx] = f64(gate[:1]) * y
    return base + c

@@ -1,0 +1,238 @@
+from contextlib import ExitStack
+
+import concourse.mybir as mybir
+from concourse.masks import make_identity
+
+K, T, E, C, H, N = 512, 1024, 4, 256, 512, 512
+FLOPS = 2 * K * N * T + 2 * K * H * E * C + 2 * H * N * E * C
+
+F32 = mybir.dt.float32
+BF16 = mybir.dt.bfloat16
+I32 = mybir.dt.int32
+U32 = mybir.dt.uint32
+U16 = mybir.dt.uint16
+U8 = mybir.dt.uint8
+FP8X4 = mybir.dt.float8_e4m3fn_x4
+FP4X4 = mybir.dt.float4_e2m1fn_x4
+ACT = mybir.ActivationFunctionType
+ALU = mybir.AluOpType
+
+P = 128
+BANK = 512
+NB = N // P
+LIST_COLS = C // 16
+
+
+def tile_moe_adp_silu_kernel(
+    tc, x_words, x_scales, w_words, w_scales, wa_words, wa_scales, wb_words, wb_scales, gate, offs, out
+):
+    nc = tc.nc
+    with ExitStack() as ctx:
+        keep = ctx.enter_context(tc.tile_pool(name="keep", bufs=1))
+        ring = ctx.enter_context(tc.tile_pool(name="ring", bufs=2))
+        psum = ctx.enter_context(tc.psum_pool(name="psum", bufs=1))
+
+        def held(shape, dtype, name):
+            return keep.tile(shape, dtype, name=name, align_bytes=64)
+
+        offsets = keep.tile([P, E * C // 16], U16, name="offsets")
+        nc.sync.dma_start(offsets[:], offs)
+
+        xs = held([P, T], U8, "xs")
+        was = held([P, H], U8, "was")
+        wbs = held([P, N], U8, "wbs")
+        ws = held([P, N], U8, "ws")
+        nc.vector.memset(was[:].bitcast(I32), 0)
+        nc.vector.memset(wbs[:].bitcast(I32), 0)
+        nc.vector.memset(ws[:].bitcast(I32), 0)
+
+        ident = held([P, P], F32, "ident")
+        make_identity(nc, ident[:])
+        warm = held([P, 1], F32, "warm")
+        nc.scalar.activation(warm[:], ident[:, 0:1], ACT.Silu)
+
+        def load_plane(plane, rows):
+            for q in range(4):
+                four = rows[4 * q : 4 * q + 4, :].bitcast(I32)
+                nc.sync.dma_start(
+                    plane[32 * q : 32 * q + 32, :].bitcast(I32),
+                    four.unsqueeze(0).broadcast_to([8, 4, four.shape[1]]),
+                )
+
+        def load_packed(plane, scales):
+            for q in range(4):
+                nc.sync.dma_start(
+                    plane[32 * q : 32 * q + 16, :].bitcast(I32), scales[:, 0, 4 * q : 4 * q + 4, :].bitcast(I32)
+                )
+
+        def load_words(src, name):
+            words = held([P, src.shape[1]], I32, name)
+            nc.sync.dma_start(words[:], src.rearrange("p c d -> p (c d)").bitcast(I32))
+            return words
+
+        load_plane(xs, x_scales[0])
+        xw = load_words(x_words[0], "xw")
+        load_packed(was, wa_scales)
+        wa0 = load_words(wa_words[0, 0], "wa0")
+        wa1 = load_words(wa_words[1, 0], "wa1")
+        load_packed(wbs, wb_scales)
+        wb0 = load_words(wb_words[0, 0], "wb0")
+        g0 = held([P, C], F32, "g0")
+        nc.sync.dma_start(g0[:], gate[:, 0:C])
+        wa_rest = held([P, E - 2, H], I32, "wa_rest")
+        nc.sync.dma_start(wa_rest[:], wa_words[2:E, 0].rearrange("e p c d -> p e (c d)").bitcast(I32))
+        wb_rest = held([P, E - 1, N], I32, "wb_rest")
+        nc.sync.dma_start(wb_rest[:], wb_words[1:E, 0].rearrange("e p c d -> p e (c d)").bitcast(I32))
+        g1 = held([P, (E - 1) * C], F32, "g1")
+        nc.sync.dma_start(g1[:], gate[:, C : E * C])
+        wa = [wa0[:], wa1[:]] + [wa_rest[:, e, :] for e in range(E - 2)]
+        wb = [wb0[:]] + [wb_rest[:, e, :] for e in range(E - 1)]
+        ww = held([P, 2 * N], U8, "ww")
+        nc.sync.dma_start(ww[:].bitcast(I32), w_words[0].bitcast(I32))
+        for r in range(4):
+            nc.sync.dma_start(ws[r:P:32, :].bitcast(I32), w_scales[0, r:16:4, :].bitcast(I32))
+
+        def entries(e0, e1):
+            return offsets[:, e0 * LIST_COLS : e1 * LIST_COLS]
+
+        def after(e, shape, dtype, name):
+            return keep.tile(shape, dtype, name=name, tag="hcol%d" % e, align_bytes=64)
+
+        banks = [psum.tile([P, BANK], F32, name="bank%d" % b) for b in range(8)]
+        xg, xsg, hq, hs, win = {}, {}, {}, {}, {}
+
+        def gather_scales(e0, tile):
+            nc.vector.tensor_copy(tile[:], xs[:].indirect(entries(e0, e0 + 2)))
+            xsg[e0], xsg[e0 + 1] = tile[:, 0:C], tile[:, C : 2 * C]
+
+        def gather_words(e):
+            xg[e] = held([P, C], U32, "xg%d" % e)
+            nc.vector.tensor_copy(xg[e][:], xw[:].bitcast(U32).indirect(entries(e, e + 1)))
+
+        def hidden(e):
+            hcol = after(e, [P, 4 * C], BF16, "hcol%d" % e)
+            for c in range(2):
+                cols = slice(c * P, (c + 1) * P)
+                pre = banks[4 + c if e == 2 else c]
+                nc.tensor.matmul_mx(
+                    pre[:], lhsT=xg[e][:, cols].bitcast(FP8X4), lhsT_scale=xsg[e][:, cols],
+                    rhs=wa[e].bitcast(FP8X4), rhs_scale=was[4 * e : P, :], start=True, stop=True,
+                )
+                hrow = ring.tile([P, H], BF16, tag="hrow", name="hrow", align_bytes=64)
+                nc.scalar.activation(
+                    hrow[:].rearrange("s (u p b) -> s u p b", u=2, b=2),
+                    pre[:].rearrange("s (p u b) -> s u p b", u=2, b=2),
+                    ACT.Silu,
+                )
+                pairs = hrow[:].bitcast(F32)
+                turned = banks[2 + c][:, 0 : 2 * P].rearrange("p (u s) -> p u s", u=2)
+                for u in range(2):
+                    nc.tensor.transpose(turned[:, u, :], pairs[:, u * P : (u + 1) * P], ident[:])
+                nc.scalar.copy(
+                    hcol[:].bitcast(F32)[:, c * 2 * P : (c + 1) * 2 * P].rearrange("p (s u) -> p s u", u=2),
+                    turned.rearrange("p u s -> p s u"),
+                )
+            hq[e] = held([P, C], U32, "hq%d" % e)
+            hs[e] = held([P, C], U8, "hs%d" % e)
+            nc.vector.quantize_mx(hq[e][:].bitcast(FP8X4), hs[e][:], hcol[:])
+
+        def second(bank, pairs, dst):
+            for j, (e, nb) in enumerate(pairs):
+                cols = slice(nb * P, (nb + 1) * P)
+                nc.tensor.matmul_mx(
+                    bank[:, j * C : (j + 1) * C], lhsT=wb[e][:, cols].bitcast(FP8X4), lhsT_scale=wbs[4 * e : P, cols],
+                    rhs=hq[e][:].bitcast(FP8X4), rhs_scale=hs[e][:], start=True, stop=True,
+                )
+            nc.scalar.copy(dst, bank[:, 0 : len(pairs) * C].rearrange("p (j s) -> p j s", s=C))
+
+        def scatter(nb, e0, e1, src):
+            nc.vector.tensor_tensor(win[nb][:].indirect(entries(e0, e1)), src, g1[:] if e0 else g0[:], ALU.mult)
+
+        def frozen(nb, th, base):
+            cols = slice(th * BANK, (th + 1) * BANK)
+            nc.tensor.matmul_mx(
+                base[:], lhsT=ww[:, 2 * nb * P : 2 * (nb + 1) * P].bitcast(FP4X4),
+                lhsT_scale=ws[:, nb * P : (nb + 1) * P],
+                rhs=xw[:, cols].bitcast(FP8X4), rhs_scale=xs[:, cols], start=True, stop=True,
+            )
+            return base
+
+        def frozen_to_sbuf(nb):
+            halves = []
+            for th in range(2):
+                base = frozen(nb, th, banks[4 + th])
+                sb = held([P, BANK], F32, "base%d_%d" % (nb, th))
+                nc.scalar.copy(sb[:], base[:])
+                halves.append(sb)
+            return halves
+
+        def finish_on_tensor(nb, halves, first, second_pair):
+            for th in range(2):
+                summed = banks[first[th]][:].rearrange("p (j n) -> p j n", j=4)
+                for j in range(4):
+                    t0 = th * BANK + j * P
+                    nc.tensor.matmul(summed[:, j, :], halves[th][:, j * P : (j + 1) * P], ident[:],
+                                     start=True, stop=False, is_transpose=True)
+                    nc.tensor.matmul(summed[:, j, :], win[nb][:, t0 : t0 + P], ident[:],
+                                     start=False, stop=True, is_transpose=True)
+                flipped = ring.tile([P, 4, P], F32, tag="flipped", name="flipped")
+                nc.scalar.copy(flipped[:], summed)
+                back = banks[second_pair[th]][:].rearrange("p (j t) -> p j t", j=4)
+                for j in range(4):
+                    nc.tensor.transpose(back[:, j, :], flipped[:, j, :], ident[:])
+                res = held([P, BANK], F32, "res%d_%d" % (nb, th))
+                nc.scalar.copy(res[:], banks[second_pair[th]][:])
+                nc.sync.dma_start(out[nb * P : (nb + 1) * P, th * BANK : (th + 1) * BANK], res[:])
+
+        def finish_on_vector(nb, pair):
+            for th in range(2):
+                base = frozen(nb, th, banks[pair[th]])
+                for j in range(2):
+                    t0 = th * BANK + j * C
+                    res = held([P, C], F32, "last%d_%d" % (th, j))
+                    nc.vector.tensor_tensor(res[:], base[:, j * C : (j + 1) * C], win[nb][:, t0 : t0 + C], ALU.add)
+                    nc.sync.dma_start(out[nb * P : (nb + 1) * P, t0 : t0 + C], res[:])
+
+        y0 = held([P, NB, C], F32, "y0")
+        yr = [held([P, 2, (E - 1) * C], F32, "yr%d" % h) for h in range(2)]
+
+        def rest(nb):
+            return yr[nb // 2][:, nb % 2, :]
+
+        def second_12(nb, bank):
+            second(bank, [(1, nb), (2, nb)], rest(nb)[:, 0 : 2 * C].rearrange("p (j s) -> p j s", s=C))
+
+        def second_3(h, bank):
+            second(bank, [(3, 2 * h), (3, 2 * h + 1)], yr[h][:, :, 2 * C : 3 * C])
+
+        gather_scales(0, held([P, 2 * C], U8, "xsg01"))
+        for e in range(E):
+            gather_words(e)
+        hidden(0)
+        gather_scales(2, after(0, [P, 2 * C], U8, "xsg23"))
+        second(banks[4], [(0, 0)], y0[:, 0:1, :])
+        win[0] = held([P, 2 * T], F32, "win0")
+        scatter(0, 0, 1, y0[:, 0, :])
+        second(banks[5], [(0, 1)], y0[:, 1:2, :])
+        hidden(1)
+        second(banks[6], [(0, 2), (0, 3)], y0[:, 2:4, :])
+        for nb in range(1, NB):
+            win[nb] = after(nb, [P, 2 * T], F32, "win%d" % nb)
+            scatter(nb, 0, 1, y0[:, nb, :])
+            if nb + 1 < E:
+                hidden(nb + 1)
+        second_12(0, banks[7])
+        second_3(0, banks[6])
+        scatter(0, 1, E, rest(0))
+        second_12(1, banks[5])
+        scatter(1, 1, E, rest(1))
+        second_12(2, banks[4])
+        second_3(1, banks[7])
+        second_12(3, banks[6])
+        bases = [frozen_to_sbuf(nb) for nb in range(NB - 1)]
+        finish_on_tensor(0, bases[0], (0, 1), (2, 3))
+        scatter(2, 1, E, rest(2))
+        finish_on_tensor(1, bases[1], (3, 2), (0, 1))
+        scatter(3, 1, E, rest(3))
+        finish_on_tensor(2, bases[2], (1, 0), (3, 2))
+        finish_on_vector(3, (2, 3))

@@ -59,8 +59,8 @@ def tile_moe_adp_silu_kernel(
                     four.unsqueeze(0).broadcast_to([8, 4, four.shape[1]]),
                 )
 
-        def load_packed(plane, scales):
-            for q in range(4):
+        def load_packed(plane, scales, quadrants):
+            for q in quadrants:
                 nc.sync.dma_start(
                     plane[32 * q : 32 * q + 16, :].bitcast(I32), scales[:, 0, 4 * q : 4 * q + 4, :].bitcast(I32)
                 )
@@ -71,20 +71,20 @@ def tile_moe_adp_silu_kernel(
             return words
 
         load_plane(xs, x_scales[0])
+        load_packed(was, wa_scales, (0, 1))
         xw = load_words(x_words[0], "xw")
-        load_packed(was, wa_scales)
+        load_packed(was, wa_scales, (2, 3))
         wa0 = load_words(wa_words[0, 0], "wa0")
         wa1 = load_words(wa_words[1, 0], "wa1")
-        load_packed(wbs, wb_scales)
+        load_packed(wbs, wb_scales, range(4))
         wb0 = load_words(wb_words[0, 0], "wb0")
-        g0 = held([P, C], F32, "g0")
-        nc.sync.dma_start(g0[:], gate[:, 0:C])
+        g = held([P, E * C], F32, "g")
+        nc.sync.dma_start(g[:, 0:C], gate[:, 0:C])
         wa_rest = held([P, E - 2, H], I32, "wa_rest")
         nc.sync.dma_start(wa_rest[:], wa_words[2:E, 0].rearrange("e p c d -> p e (c d)").bitcast(I32))
         wb_rest = held([P, E - 1, N], I32, "wb_rest")
         nc.sync.dma_start(wb_rest[:], wb_words[1:E, 0].rearrange("e p c d -> p e (c d)").bitcast(I32))
-        g1 = held([P, (E - 1) * C], F32, "g1")
-        nc.sync.dma_start(g1[:], gate[:, C : E * C])
+        nc.sync.dma_start(g[:, C : E * C], gate[:, C : E * C])
         wa = [wa0[:], wa1[:]] + [wa_rest[:, e, :] for e in range(E - 2)]
         wb = [wb0[:]] + [wb_rest[:, e, :] for e in range(E - 1)]
         ww = held([P, 2 * N], U8, "ww")
@@ -101,19 +101,20 @@ def tile_moe_adp_silu_kernel(
         banks = [psum.tile([P, BANK], F32, name="bank%d" % b) for b in range(8)]
         xg, xsg, hq, hs, win = {}, {}, {}, {}, {}
 
-        def gather_scales(e0, tile):
-            nc.vector.tensor_copy(tile[:], xs[:].indirect(entries(e0, e0 + 2)))
-            xsg[e0], xsg[e0 + 1] = tile[:, 0:C], tile[:, C : 2 * C]
+        def gather_scales(e0, e1, tile):
+            nc.vector.tensor_copy(tile[:], xs[:].indirect(entries(e0, e1)))
+            for e in range(e0, e1):
+                xsg[e] = tile[:, (e - e0) * C : (e - e0 + 1) * C]
 
         def gather_words(e):
-            xg[e] = held([P, C], U32, "xg%d" % e)
+            xg[e] = keep.tile([P, C], U32, name="xg%d" % e, tag="xg%d" % e, align_bytes=64)
             nc.vector.tensor_copy(xg[e][:], xw[:].bitcast(U32).indirect(entries(e, e + 1)))
 
-        def hidden(e):
+        def hidden(e, pre_banks):
             hcol = after(e, [P, 4 * C], BF16, "hcol%d" % e)
             for c in range(2):
                 cols = slice(c * P, (c + 1) * P)
-                pre = banks[4 + c if e == 2 else c]
+                pre = banks[pre_banks[c]]
                 nc.tensor.matmul_mx(
                     pre[:], lhsT=xg[e][:, cols].bitcast(FP8X4), lhsT_scale=xsg[e][:, cols],
                     rhs=wa[e].bitcast(FP8X4), rhs_scale=was[4 * e : P, :], start=True, stop=True,
@@ -128,7 +129,8 @@ def tile_moe_adp_silu_kernel(
                 turned = banks[2 + c][:, 0 : 2 * P].rearrange("p (u s) -> p u s", u=2)
                 for u in range(2):
                     nc.tensor.transpose(turned[:, u, :], pairs[:, u * P : (u + 1) * P], ident[:])
-                nc.scalar.copy(
+                copy = nc.vector.tensor_copy if e == 0 else nc.scalar.copy
+                copy(
                     hcol[:].bitcast(F32)[:, c * 2 * P : (c + 1) * 2 * P].rearrange("p (s u) -> p s u", u=2),
                     turned.rearrange("p u s -> p s u"),
                 )
@@ -136,17 +138,20 @@ def tile_moe_adp_silu_kernel(
             hs[e] = held([P, C], U8, "hs%d" % e)
             nc.vector.quantize_mx(hq[e][:].bitcast(FP8X4), hs[e][:], hcol[:])
 
-        def second(bank, pairs, dst):
+        def second(bank, pairs, dst, copy=nc.scalar.copy):
             for j, (e, nb) in enumerate(pairs):
                 cols = slice(nb * P, (nb + 1) * P)
                 nc.tensor.matmul_mx(
                     bank[:, j * C : (j + 1) * C], lhsT=wb[e][:, cols].bitcast(FP8X4), lhsT_scale=wbs[4 * e : P, cols],
                     rhs=hq[e][:].bitcast(FP8X4), rhs_scale=hs[e][:], start=True, stop=True,
                 )
-            nc.scalar.copy(dst, bank[:, 0 : len(pairs) * C].rearrange("p (j s) -> p j s", s=C))
+            copy(dst, bank[:, 0 : len(pairs) * C].rearrange("p (j s) -> p j s", s=C))
 
-        def scatter(nb, e0, e1, src):
-            nc.vector.tensor_tensor(win[nb][:].indirect(entries(e0, e1)), src, g1[:] if e0 else g0[:], ALU.mult)
+        def scatter(nb, e0, e1):
+            cols = slice(e0 * C, e1 * C)
+            nc.vector.tensor_tensor(
+                win[nb][:].indirect(entries(e0, e1)), y[nb // 2][:, nb % 2, cols], g[:, cols], ALU.mult
+            )
 
         def frozen(nb, th, base):
             cols = slice(th * BANK, (th + 1) * BANK)
@@ -193,46 +198,46 @@ def tile_moe_adp_silu_kernel(
                     nc.vector.tensor_tensor(res[:], base[:, j * C : (j + 1) * C], win[nb][:, t0 : t0 + C], ALU.add)
                     nc.sync.dma_start(out[nb * P : (nb + 1) * P, t0 : t0 + C], res[:])
 
-        y0 = held([P, NB, C], F32, "y0")
-        yr = [held([P, 2, (E - 1) * C], F32, "yr%d" % h) for h in range(2)]
-
-        def rest(nb):
-            return yr[nb // 2][:, nb % 2, :]
+        y = [held([P, 2, E * C], F32, "y%d" % h) for h in range(2)]
 
         def second_12(nb, bank):
-            second(bank, [(1, nb), (2, nb)], rest(nb)[:, 0 : 2 * C].rearrange("p (j s) -> p j s", s=C))
+            second(bank, [(1, nb), (2, nb)], y[nb // 2][:, nb % 2, C : 3 * C].rearrange("p (j s) -> p j s", s=C))
 
-        def second_3(h, bank):
-            second(bank, [(3, 2 * h), (3, 2 * h + 1)], yr[h][:, :, 2 * C : 3 * C])
+        def second_pair(e, h, bank):
+            second(bank, [(e, 2 * h), (e, 2 * h + 1)], y[h][:, :, e * C : (e + 1) * C])
 
-        gather_scales(0, held([P, 2 * C], U8, "xsg01"))
+        gather_scales(0, 2, held([P, 2 * C], U8, "xsg01"))
         for e in range(E):
             gather_words(e)
-        hidden(0)
-        gather_scales(2, after(0, [P, 2 * C], U8, "xsg23"))
-        second(banks[4], [(0, 0)], y0[:, 0:1, :])
+        hidden(0, (0, 1))
+        gather_scales(2, 3, keep.tile([P, C], U8, name="xsg2", tag="xg0", align_bytes=64))
+        gather_scales(3, 4, after(0, [P, C], U8, "xsg3"))
+        second(banks[4], [(0, 0)], y[0][:, 0:1, 0:C], nc.vector.tensor_copy)
         win[0] = held([P, 2 * T], F32, "win0")
-        scatter(0, 0, 1, y0[:, 0, :])
-        second(banks[5], [(0, 1)], y0[:, 1:2, :])
-        hidden(1)
-        second(banks[6], [(0, 2), (0, 3)], y0[:, 2:4, :])
-        for nb in range(1, NB):
-            win[nb] = after(nb, [P, 2 * T], F32, "win%d" % nb)
-            scatter(nb, 0, 1, y0[:, nb, :])
-            if nb + 1 < E:
-                hidden(nb + 1)
-        second_12(0, banks[7])
-        second_3(0, banks[6])
-        scatter(0, 1, E, rest(0))
-        second_12(1, banks[5])
-        scatter(1, 1, E, rest(1))
+        scatter(0, 0, 1)
+        second(banks[5], [(0, 1)], y[0][:, 1:2, 0:C])
+        hidden(1, (0, 1))
+        win[1] = after(1, [P, 2 * T], F32, "win1")
+        scatter(1, 0, 1)
+        second_pair(0, 1, banks[6])
+        hidden(2, (5, 1))
+        win[2] = after(2, [P, 2 * T], F32, "win2")
+        scatter(2, 0, 1)
+        hidden(3, (0, 1))
+        second_12(0, banks[2])
+        scatter(0, 1, 3)
+        second_pair(3, 0, banks[7])
+        scatter(0, 3, 4)
+        second_12(1, banks[3])
+        scatter(1, 1, E)
         second_12(2, banks[4])
-        second_3(1, banks[7])
+        second_pair(3, 1, banks[5])
         second_12(3, banks[6])
         bases = [frozen_to_sbuf(nb) for nb in range(NB - 1)]
         finish_on_tensor(0, bases[0], (0, 1), (2, 3))
-        scatter(2, 1, E, rest(2))
-        finish_on_tensor(1, bases[1], (3, 2), (0, 1))
-        scatter(3, 1, E, rest(3))
-        finish_on_tensor(2, bases[2], (1, 0), (3, 2))
-        finish_on_vector(3, (2, 3))
+        scatter(2, 1, E)
+        finish_on_tensor(1, bases[1], (1, 0), (2, 3))
+        win[3] = held([P, 2 * T], F32, "win3")
+        scatter(3, 0, E)
+        finish_on_tensor(2, bases[2], (0, 1), (2, 3))
+        finish_on_vector(3, (3, 2))

@@ -19,8 +19,9 @@ ALU = mybir.AluOpType
 
 P = 128
 BANK = 512
-NB = N // P
-LIST_COLS = C // 16
+ROW_BLOCKS = N // P
+CHUNKS = E * C // P
+LIST_COLS = P // 16
 
 
 def tile_moe_adp_silu_kernel(
@@ -46,22 +47,9 @@ def tile_moe_adp_silu_kernel(
         nc.vector.memset(wbs[:].bitcast(I32), 0)
         nc.vector.memset(ws[:].bitcast(I32), 0)
 
-        ident = held([P, P], F32, "ident")
-        make_identity(nc, ident[:])
-        warm = held([P, 1], F32, "warm")
-        nc.scalar.activation(warm[:], ident[:, 0:1], ACT.Silu)
-
-        def load_plane(plane, rows):
-            for q in range(4):
-                four = rows[4 * q : 4 * q + 4, :].bitcast(I32)
-                nc.sync.dma_start(
-                    plane[32 * q : 32 * q + 32, :].bitcast(I32),
-                    four.unsqueeze(0).broadcast_to([8, 4, four.shape[1]]),
-                )
-
-        def load_packed(plane, scales, quadrants):
+        def load_adapter_planes(plane, scales, quadrants, queue):
             for q in quadrants:
-                nc.sync.dma_start(
+                queue.dma_start(
                     plane[32 * q : 32 * q + 16, :].bitcast(I32), scales[:, 0, 4 * q : 4 * q + 4, :].bitcast(I32)
                 )
 
@@ -70,13 +58,18 @@ def tile_moe_adp_silu_kernel(
             nc.sync.dma_start(words[:], src.rearrange("p c d -> p (c d)").bitcast(I32))
             return words
 
-        load_plane(xs, x_scales[0])
-        load_packed(was, wa_scales, (0, 1))
+        for q in range(4):
+            four_rows = x_scales[0][4 * q : 4 * q + 4, :].bitcast(I32)
+            (nc.scalar if q % 2 else nc.sync).dma_start(
+                xs[32 * q : 32 * q + 32, :].bitcast(I32),
+                four_rows.unsqueeze(0).broadcast_to([8, 4, T // 4]),
+            )
+        load_adapter_planes(was, wa_scales, (0, 1), nc.scalar)
         xw = load_words(x_words[0], "xw")
-        load_packed(was, wa_scales, (2, 3))
+        load_adapter_planes(was, wa_scales, (2, 3), nc.sync)
         wa0 = load_words(wa_words[0, 0], "wa0")
         wa1 = load_words(wa_words[1, 0], "wa1")
-        load_packed(wbs, wb_scales, range(4))
+        load_adapter_planes(wbs, wb_scales, range(4), nc.sync)
         wb0 = load_words(wb_words[0, 0], "wb0")
         g = held([P, E * C], F32, "g")
         nc.sync.dma_start(g[:, 0:C], gate[:, 0:C])
@@ -92,152 +85,187 @@ def tile_moe_adp_silu_kernel(
         for r in range(4):
             nc.sync.dma_start(ws[r:P:32, :].bitcast(I32), w_scales[0, r:16:4, :].bitcast(I32))
 
-        def entries(e0, e1):
-            return offsets[:, e0 * LIST_COLS : e1 * LIST_COLS]
+        ident = held([P, P], F32, "ident")
+        make_identity(nc, ident[:])
 
-        def after(e, shape, dtype, name):
+        def entries(c0, c1):
+            return offsets[:, c0 * LIST_COLS : c1 * LIST_COLS]
+
+        def in_h_buffer(e, shape, dtype, name):
             return keep.tile(shape, dtype, name=name, tag="hcol%d" % e, align_bytes=64)
 
         banks = [psum.tile([P, BANK], F32, name="bank%d" % b) for b in range(8)]
         xg, xsg, hq, hs, win = {}, {}, {}, {}, {}
 
         def gather_scales(e0, e1, tile):
-            nc.vector.tensor_copy(tile[:], xs[:].indirect(entries(e0, e1)))
+            nc.vector.tensor_copy(tile[:], xs[:].indirect(entries(2 * e0, 2 * e1)))
             for e in range(e0, e1):
                 xsg[e] = tile[:, (e - e0) * C : (e - e0 + 1) * C]
 
-        def gather_words(e):
-            xg[e] = keep.tile([P, C], U32, name="xg%d" % e, tag="xg%d" % e, align_bytes=64)
-            nc.vector.tensor_copy(xg[e][:], xw[:].bitcast(U32).indirect(entries(e, e + 1)))
+        def gather_words(c0, c1):
+            tile = held([P, (c1 - c0) * P], U32, "xg%d_%d" % divmod(c0, 2))
+            nc.vector.tensor_copy(tile[:], xw[:].bitcast(U32).indirect(entries(c0, c1)))
+            for c in range(c0, c1):
+                xg[c] = tile[:, (c - c0) * P : (c - c0 + 1) * P]
+
+        def turn_hidden_chunk(e, half, pre, turned):
+            nc.tensor.matmul_mx(
+                pre[:], lhsT=xg[2 * e + half].bitcast(FP8X4), lhsT_scale=xsg[e][:, half * P : (half + 1) * P],
+                rhs=wa[e].bitcast(FP8X4), rhs_scale=was[4 * e : P, :], start=True, stop=True,
+            )
+            hrow = ring.tile([P, H], BF16, tag="hrow", name="hrow", align_bytes=64)
+            nc.scalar.activation(
+                hrow[:].rearrange("s (u p b) -> s u p b", u=2, b=2),
+                pre[:].rearrange("s (p u b) -> s u p b", u=2, b=2),
+                ACT.Silu,
+            )
+            pairs = hrow[:].bitcast(F32)
+            for u in range(2):
+                nc.tensor.transpose(turned[:, u, :], pairs[:, u * P : (u + 1) * P], ident[:])
+
+        def hidden_first_adapter():
+            hq[0] = held([P, C], U32, "hq0")
+            hs[0] = held([P, C], U8, "hs0")
+            for half in range(2):
+                cols = slice(half * P, (half + 1) * P)
+                turned = banks[2 + half][:, 0 : 2 * P].rearrange("p (u s) -> p u s", u=2)
+                turn_hidden_chunk(0, half, banks[half], turned)
+                hcol = held([P, 4 * P], BF16, "half1") if half else in_h_buffer(0, [P, 4 * P], BF16, "half0")
+                nc.scalar.copy(
+                    hcol[:].bitcast(F32).rearrange("p (s u) -> p s u", u=2), turned.rearrange("p u s -> p s u")
+                )
+                nc.vector.quantize_mx(hq[0][:, cols].bitcast(FP8X4), hs[0][:, cols], hcol[:])
 
         def hidden(e, pre_banks):
-            hcol = after(e, [P, 4 * C], BF16, "hcol%d" % e)
-            for c in range(2):
-                cols = slice(c * P, (c + 1) * P)
-                pre = banks[pre_banks[c]]
-                nc.tensor.matmul_mx(
-                    pre[:], lhsT=xg[e][:, cols].bitcast(FP8X4), lhsT_scale=xsg[e][:, cols],
-                    rhs=wa[e].bitcast(FP8X4), rhs_scale=was[4 * e : P, :], start=True, stop=True,
-                )
-                hrow = ring.tile([P, H], BF16, tag="hrow", name="hrow", align_bytes=64)
-                nc.scalar.activation(
-                    hrow[:].rearrange("s (u p b) -> s u p b", u=2, b=2),
-                    pre[:].rearrange("s (p u b) -> s u p b", u=2, b=2),
-                    ACT.Silu,
-                )
-                pairs = hrow[:].bitcast(F32)
-                turned = banks[2 + c][:, 0 : 2 * P].rearrange("p (u s) -> p u s", u=2)
-                for u in range(2):
-                    nc.tensor.transpose(turned[:, u, :], pairs[:, u * P : (u + 1) * P], ident[:])
-                copy = nc.vector.tensor_copy if e == 0 else nc.scalar.copy
-                copy(
-                    hcol[:].bitcast(F32)[:, c * 2 * P : (c + 1) * 2 * P].rearrange("p (s u) -> p s u", u=2),
-                    turned.rearrange("p u s -> p s u"),
-                )
+            hcol = in_h_buffer(e, [P, 4 * C], BF16, "hcol%d" % e)
             hq[e] = held([P, C], U32, "hq%d" % e)
             hs[e] = held([P, C], U8, "hs%d" % e)
+            bank = banks[2 + e % 2]
+            for half in range(2):
+                turned = bank[:, half * 2 * P : (half + 1) * 2 * P].rearrange("p (u s) -> p u s", u=2)
+                turn_hidden_chunk(e, half, banks[pre_banks[half]], turned)
+            nc.scalar.copy(
+                hcol[:].bitcast(F32).rearrange("p (c s u) -> p c s u", c=2, u=2),
+                bank[:].rearrange("p (c u s) -> p c s u", c=2, u=2),
+            )
             nc.vector.quantize_mx(hq[e][:].bitcast(FP8X4), hs[e][:], hcol[:])
 
-        def second(bank, pairs, dst, copy=nc.scalar.copy):
-            for j, (e, nb) in enumerate(pairs):
+        def second_layer(bank, pieces, dst):
+            for j, (e, nb) in enumerate(pieces):
                 cols = slice(nb * P, (nb + 1) * P)
                 nc.tensor.matmul_mx(
                     bank[:, j * C : (j + 1) * C], lhsT=wb[e][:, cols].bitcast(FP8X4), lhsT_scale=wbs[4 * e : P, cols],
                     rhs=hq[e][:].bitcast(FP8X4), rhs_scale=hs[e][:], start=True, stop=True,
                 )
-            copy(dst, bank[:, 0 : len(pairs) * C].rearrange("p (j s) -> p j s", s=C))
+            nc.scalar.copy(dst, bank[:, 0 : len(pieces) * C].rearrange("p (j s) -> p j s", s=C))
 
-        def scatter(nb, e0, e1):
-            cols = slice(e0 * C, e1 * C)
+        def first_scatter(half, bank):
+            cols = slice(half * P, (half + 1) * P)
+            nc.tensor.matmul_mx(
+                bank[:, 0:P], lhsT=wb[0][:, 0:P].bitcast(FP8X4), lhsT_scale=wbs[:, 0:P],
+                rhs=hq[0][:, cols].bitcast(FP8X4), rhs_scale=hs[0][:, cols], start=True, stop=True,
+            )
+            nc.scalar.copy(y[0][:, 0, cols], bank[:, 0:P])
+            scatter(0, half, half + 1)
+
+        def scatter(nb, c0, c1):
+            cols = slice(c0 * P, c1 * P)
             nc.vector.tensor_tensor(
-                win[nb][:].indirect(entries(e0, e1)), y[nb // 2][:, nb % 2, cols], g[:, cols], ALU.mult
+                win[nb][:].indirect(entries(c0, c1)), y[nb // 2][:, nb % 2, cols], g[:, cols], ALU.mult
             )
 
-        def frozen(nb, th, base):
+        def frozen(nb, th, bank):
             cols = slice(th * BANK, (th + 1) * BANK)
             nc.tensor.matmul_mx(
-                base[:], lhsT=ww[:, 2 * nb * P : 2 * (nb + 1) * P].bitcast(FP4X4),
+                bank[:], lhsT=ww[:, 2 * nb * P : 2 * (nb + 1) * P].bitcast(FP4X4),
                 lhsT_scale=ws[:, nb * P : (nb + 1) * P],
                 rhs=xw[:, cols].bitcast(FP8X4), rhs_scale=xs[:, cols], start=True, stop=True,
             )
-            return base
 
         def frozen_to_sbuf(nb):
             halves = []
             for th in range(2):
-                base = frozen(nb, th, banks[4 + th])
-                sb = held([P, BANK], F32, "base%d_%d" % (nb, th))
-                nc.scalar.copy(sb[:], base[:])
-                halves.append(sb)
+                frozen(nb, th, banks[4 + th])
+                base = held([P, BANK], F32, "base%d_%d" % (nb, th))
+                nc.scalar.copy(base[:], banks[4 + th][:])
+                halves.append(base)
             return halves
 
-        def finish_on_tensor(nb, halves, first, second_pair):
+        def finish_on_tensor(nb, base_halves, sum_banks):
             for th in range(2):
-                summed = banks[first[th]][:].rearrange("p (j n) -> p j n", j=4)
+                summed = banks[sum_banks[th]][:].rearrange("p (j n) -> p j n", j=4)
                 for j in range(4):
                     t0 = th * BANK + j * P
-                    nc.tensor.matmul(summed[:, j, :], halves[th][:, j * P : (j + 1) * P], ident[:],
+                    nc.tensor.matmul(summed[:, j, :], base_halves[th][:, j * P : (j + 1) * P], ident[:],
                                      start=True, stop=False, is_transpose=True)
                     nc.tensor.matmul(summed[:, j, :], win[nb][:, t0 : t0 + P], ident[:],
                                      start=False, stop=True, is_transpose=True)
                 flipped = ring.tile([P, 4, P], F32, tag="flipped", name="flipped")
                 nc.scalar.copy(flipped[:], summed)
-                back = banks[second_pair[th]][:].rearrange("p (j t) -> p j t", j=4)
+                back = banks[2 + th][:].rearrange("p (j t) -> p j t", j=4)
                 for j in range(4):
                     nc.tensor.transpose(back[:, j, :], flipped[:, j, :], ident[:])
                 res = held([P, BANK], F32, "res%d_%d" % (nb, th))
-                nc.scalar.copy(res[:], banks[second_pair[th]][:])
-                nc.sync.dma_start(out[nb * P : (nb + 1) * P, th * BANK : (th + 1) * BANK], res[:])
+                nc.scalar.copy(res[:], banks[2 + th][:])
+                nc.scalar.dma_start(out[nb * P : (nb + 1) * P, th * BANK : (th + 1) * BANK], res[:])
 
-        def finish_on_vector(nb, pair):
+        def finish_on_vector(nb):
             for th in range(2):
-                base = frozen(nb, th, banks[pair[th]])
-                for j in range(2):
-                    t0 = th * BANK + j * C
-                    res = held([P, C], F32, "last%d_%d" % (th, j))
-                    nc.vector.tensor_tensor(res[:], base[:, j * C : (j + 1) * C], win[nb][:, t0 : t0 + C], ALU.add)
-                    nc.sync.dma_start(out[nb * P : (nb + 1) * P, t0 : t0 + C], res[:])
+                frozen(nb, th, banks[th])
+                width = BANK // 2 if th else BANK
+                for col in range(0, BANK, width):
+                    t0 = th * BANK + col
+                    res = held([P, width], F32, "last%d" % t0)
+                    nc.vector.tensor_tensor(
+                        res[:], banks[th][:, col : col + width], win[nb][:, t0 : t0 + width], ALU.add
+                    )
+                    nc.sync.dma_start(out[nb * P : (nb + 1) * P, t0 : t0 + width], res[:])
 
         y = [held([P, 2, E * C], F32, "y%d" % h) for h in range(2)]
 
-        def second_12(nb, bank):
-            second(bank, [(1, nb), (2, nb)], y[nb // 2][:, nb % 2, C : 3 * C].rearrange("p (j s) -> p j s", s=C))
+        def second_layer_middle_adapters(nb, bank):
+            dst = y[nb // 2][:, nb % 2, C : 3 * C].rearrange("p (j s) -> p j s", s=C)
+            second_layer(bank, [(1, nb), (2, nb)], dst)
 
-        def second_pair(e, h, bank):
-            second(bank, [(e, 2 * h), (e, 2 * h + 1)], y[h][:, :, e * C : (e + 1) * C])
+        def second_layer_last_adapter(h, bank):
+            second_layer(bank, [(3, 2 * h), (3, 2 * h + 1)], y[h][:, :, 3 * C : 4 * C])
 
-        gather_scales(0, 2, held([P, 2 * C], U8, "xsg01"))
-        for e in range(E):
-            gather_words(e)
-        hidden(0, (0, 1))
-        gather_scales(2, 3, keep.tile([P, C], U8, name="xsg2", tag="xg0", align_bytes=64))
-        gather_scales(3, 4, after(0, [P, C], U8, "xsg3"))
-        second(banks[4], [(0, 0)], y[0][:, 0:1, 0:C], nc.vector.tensor_copy)
-        win[0] = held([P, 2 * T], F32, "win0")
-        scatter(0, 0, 1)
-        second(banks[5], [(0, 1)], y[0][:, 1:2, 0:C])
+        gather_scales(0, 3, held([P, 3 * C], U8, "xsg012"))
+        gather_words(0, 1)
+        gather_words(1, 2)
+        for e in range(1, E):
+            gather_words(2 * e, 2 * e + 2)
+
+        hidden_first_adapter()
+        gather_scales(3, 4, in_h_buffer(0, [P, C], U8, "xsg3"))
+        win[0] = held([P, T], F32, "win0")
+        first_scatter(0, banks[4])
+        first_scatter(1, banks[6])
+        second_layer(banks[5], [(0, 1)], y[0][:, 1:2, 0:C])
         hidden(1, (0, 1))
-        win[1] = after(1, [P, 2 * T], F32, "win1")
-        scatter(1, 0, 1)
-        second_pair(0, 1, banks[6])
+        win[1] = in_h_buffer(1, [P, 2 * T], F32, "win1")
+        scatter(1, 0, 2)
+        second_layer(banks[7], [(0, 2)], y[1][:, 0:1, 0:C])
         hidden(2, (5, 1))
-        win[2] = after(2, [P, 2 * T], F32, "win2")
-        scatter(2, 0, 1)
+        win[2] = in_h_buffer(2, [P, 2 * T], F32, "win2")
+        scatter(2, 0, 2)
         hidden(3, (0, 1))
-        second_12(0, banks[2])
-        scatter(0, 1, 3)
-        second_pair(3, 0, banks[7])
-        scatter(0, 3, 4)
-        second_12(1, banks[3])
-        scatter(1, 1, E)
-        second_12(2, banks[4])
-        second_pair(3, 1, banks[5])
-        second_12(3, banks[6])
-        bases = [frozen_to_sbuf(nb) for nb in range(NB - 1)]
-        finish_on_tensor(0, bases[0], (0, 1), (2, 3))
-        scatter(2, 1, E)
-        finish_on_tensor(1, bases[1], (1, 0), (2, 3))
+
+        second_layer_middle_adapters(0, banks[1])
+        scatter(0, 2, 6)
+        second_layer_last_adapter(0, banks[6])
+        scatter(0, 6, CHUNKS)
+        second_layer_middle_adapters(1, banks[2])
+        scatter(1, 2, CHUNKS)
+        second_layer_middle_adapters(2, banks[4])
+        second_layer_last_adapter(1, banks[5])
+        second_layer_middle_adapters(3, banks[7])
+        second_layer(banks[6], [(0, 3)], y[1][:, 1:2, 0:C])
+        bases = [frozen_to_sbuf(nb) for nb in range(ROW_BLOCKS - 1)]
+        finish_on_tensor(0, bases[0], (0, 1))
+        scatter(2, 2, CHUNKS)
+        finish_on_tensor(1, bases[1], (1, 0))
         win[3] = held([P, 2 * T], F32, "win3")
-        scatter(3, 0, E)
-        finish_on_tensor(2, bases[2], (0, 1), (2, 3))
-        finish_on_vector(3, (3, 2))
+        scatter(3, 0, CHUNKS)
+        finish_on_tensor(2, bases[2], (0, 1))
+        finish_on_vector(3)

@@ -43,7 +43,7 @@ def tile_moe_adp_silu_kernel(
         was = held([P, H], U8, "was")
         wbs = held([P, N], U8, "wbs")
         ws = held([P, N], U8, "ws")
-        nc.vector.memset(was[:].bitcast(I32), 0)
+        nc.gpsimd.memset(was[:].bitcast(I32), 0)
         nc.vector.memset(wbs[:].bitcast(I32), 0)
         nc.vector.memset(ws[:].bitcast(I32), 0)
 
@@ -64,13 +64,12 @@ def tile_moe_adp_silu_kernel(
                 xs[32 * q : 32 * q + 32, :].bitcast(I32),
                 four_rows.unsqueeze(0).broadcast_to([8, 4, T // 4]),
             )
-        load_adapter_planes(was, wa_scales, (0, 1), nc.scalar)
         xw = load_words(x_words[0], "xw")
-        load_adapter_planes(was, wa_scales, (2, 3), nc.sync)
         wa0 = load_words(wa_words[0, 0], "wa0")
+        load_adapter_planes(was, wa_scales, range(4), nc.sync)
         wa1 = load_words(wa_words[1, 0], "wa1")
-        load_adapter_planes(wbs, wb_scales, range(4), nc.sync)
         wb0 = load_words(wb_words[0, 0], "wb0")
+        load_adapter_planes(wbs, wb_scales, range(4), nc.sync)
         g = held([P, E * C], F32, "g")
         nc.sync.dma_start(g[:, 0:C], gate[:, 0:C])
         wa_rest = held([P, E - 2, H], I32, "wa_rest")
@@ -95,7 +94,10 @@ def tile_moe_adp_silu_kernel(
             return keep.tile(shape, dtype, name=name, tag="hcol%d" % e, align_bytes=64)
 
         banks = [psum.tile([P, BANK], F32, name="bank%d" % b) for b in range(8)]
-        xg, xsg, hq, hs, win = {}, {}, {}, {}, {}
+        xg, xsg, base = {}, {}, {}
+        hq = [held([P, C], U32, "hq%d" % e) for e in range(E)]
+        hs = [held([P, C], U8, "hs%d" % e) for e in range(E)]
+        win = [held([P, T if nb < 2 else 2 * T], F32, "win%d" % nb) for nb in range(ROW_BLOCKS)]
 
         def gather_scales(e0, e1, tile):
             nc.vector.tensor_copy(tile[:], xs[:].indirect(entries(2 * e0, 2 * e1)))
@@ -103,7 +105,7 @@ def tile_moe_adp_silu_kernel(
                 xsg[e] = tile[:, (e - e0) * C : (e - e0 + 1) * C]
 
         def gather_words(c0, c1):
-            tile = held([P, (c1 - c0) * P], U32, "xg%d_%d" % divmod(c0, 2))
+            tile = keep.tile([P, (c1 - c0) * P], U32, name="xg%d" % c0, tag="xg%d" % c0, align_bytes=64)
             nc.vector.tensor_copy(tile[:], xw[:].bitcast(U32).indirect(entries(c0, c1)))
             for c in range(c0, c1):
                 xg[c] = tile[:, (c - c0) * P : (c - c0 + 1) * P]
@@ -123,30 +125,25 @@ def tile_moe_adp_silu_kernel(
             for u in range(2):
                 nc.tensor.transpose(turned[:, u, :], pairs[:, u * P : (u + 1) * P], ident[:])
 
-        def hidden_first_adapter():
-            hq[0] = held([P, C], U32, "hq0")
-            hs[0] = held([P, C], U8, "hs0")
-            for half in range(2):
-                cols = slice(half * P, (half + 1) * P)
-                turned = banks[2 + half][:, 0 : 2 * P].rearrange("p (u s) -> p u s", u=2)
-                turn_hidden_chunk(0, half, banks[half], turned)
-                hcol = held([P, 4 * P], BF16, "half1") if half else in_h_buffer(0, [P, 4 * P], BF16, "half0")
-                nc.scalar.copy(
-                    hcol[:].bitcast(F32).rearrange("p (s u) -> p s u", u=2), turned.rearrange("p u s -> p s u")
-                )
-                nc.vector.quantize_mx(hq[0][:, cols].bitcast(FP8X4), hs[0][:, cols], hcol[:])
+        def quantise_first_chunk(half):
+            cols = slice(half * P, (half + 1) * P)
+            turned = banks[2 + half][:, 0 : 2 * P].rearrange("p (u s) -> p u s", u=2)
+            hcol = held([P, 4 * P], BF16, "half1") if half else in_h_buffer(0, [P, 4 * P], BF16, "half0")
+            nc.scalar.copy(
+                hcol[:].bitcast(F32).rearrange("p (s u) -> p s u", u=2), turned.rearrange("p u s -> p s u")
+            )
+            nc.vector.quantize_mx(hq[0][:, cols].bitcast(FP8X4), hs[0][:, cols], hcol[:])
 
-        def hidden(e, pre_banks):
-            hcol = in_h_buffer(e, [P, 4 * C], BF16, "hcol%d" % e)
-            hq[e] = held([P, C], U32, "hq%d" % e)
-            hs[e] = held([P, C], U8, "hs%d" % e)
-            bank = banks[2 + e % 2]
-            for half in range(2):
-                turned = bank[:, half * 2 * P : (half + 1) * 2 * P].rearrange("p (u s) -> p u s", u=2)
-                turn_hidden_chunk(e, half, banks[pre_banks[half]], turned)
+        def turn(e, half, pre_bank, turn_bank):
+            off = half * 2 * P if e else 0
+            turned = banks[turn_bank][:, off : off + 2 * P].rearrange("p (u s) -> p u s", u=2)
+            turn_hidden_chunk(e, half, banks[pre_bank], turned)
+
+        def quantise(e, turn_bank):
+            hcol = held([P, 4 * C], BF16, "hcol%d_" % e)
             nc.scalar.copy(
                 hcol[:].bitcast(F32).rearrange("p (c s u) -> p c s u", c=2, u=2),
-                bank[:].rearrange("p (c u s) -> p c s u", c=2, u=2),
+                banks[turn_bank][:].rearrange("p (c u s) -> p c s u", c=2, u=2),
             )
             nc.vector.quantize_mx(hq[e][:].bitcast(FP8X4), hs[e][:], hcol[:])
 
@@ -159,14 +156,18 @@ def tile_moe_adp_silu_kernel(
                 )
             nc.scalar.copy(dst, bank[:, 0 : len(pieces) * C].rearrange("p (j s) -> p j s", s=C))
 
-        def first_scatter(half, bank):
+        def second_layer_chunk(half, blocks, bank):
             cols = slice(half * P, (half + 1) * P)
-            nc.tensor.matmul_mx(
-                bank[:, 0:P], lhsT=wb[0][:, 0:P].bitcast(FP8X4), lhsT_scale=wbs[:, 0:P],
-                rhs=hq[0][:, cols].bitcast(FP8X4), rhs_scale=hs[0][:, cols], start=True, stop=True,
+            for j, nb in enumerate(blocks):
+                rows = slice(nb * P, (nb + 1) * P)
+                nc.tensor.matmul_mx(
+                    bank[:, j * P : (j + 1) * P], lhsT=wb[0][:, rows].bitcast(FP8X4), lhsT_scale=wbs[:, rows],
+                    rhs=hq[0][:, cols].bitcast(FP8X4), rhs_scale=hs[0][:, cols], start=True, stop=True,
+                )
+            nc.scalar.copy(
+                y[0][:, blocks[0] : blocks[-1] + 1, cols],
+                bank[:, 0 : len(blocks) * P].rearrange("p (j s) -> p j s", s=P),
             )
-            nc.scalar.copy(y[0][:, 0, cols], bank[:, 0:P])
-            scatter(0, half, half + 1)
 
         def scatter(nb, c0, c1):
             cols = slice(c0 * P, c1 * P)
@@ -182,31 +183,27 @@ def tile_moe_adp_silu_kernel(
                 rhs=xw[:, cols].bitcast(FP8X4), rhs_scale=xs[:, cols], start=True, stop=True,
             )
 
-        def frozen_to_sbuf(nb):
-            halves = []
-            for th in range(2):
-                frozen(nb, th, banks[4 + th])
-                base = held([P, BANK], F32, "base%d_%d" % (nb, th))
-                nc.scalar.copy(base[:], banks[4 + th][:])
-                halves.append(base)
-            return halves
+        def frozen_to_sbuf(nb, th, bank):
+            frozen(nb, th, bank)
+            base[nb, th] = held([P, BANK], F32, "base%d_%d" % (nb, th))
+            nc.scalar.copy(base[nb, th][:], bank[:])
 
-        def finish_on_tensor(nb, base_halves, sum_banks):
+        def finish_on_tensor(nb, sum_banks, back_banks):
             for th in range(2):
                 summed = banks[sum_banks[th]][:].rearrange("p (j n) -> p j n", j=4)
                 for j in range(4):
                     t0 = th * BANK + j * P
-                    nc.tensor.matmul(summed[:, j, :], base_halves[th][:, j * P : (j + 1) * P], ident[:],
+                    nc.tensor.matmul(summed[:, j, :], base[nb, th][:, j * P : (j + 1) * P], ident[:],
                                      start=True, stop=False, is_transpose=True)
                     nc.tensor.matmul(summed[:, j, :], win[nb][:, t0 : t0 + P], ident[:],
                                      start=False, stop=True, is_transpose=True)
                 flipped = ring.tile([P, 4, P], F32, tag="flipped", name="flipped")
                 nc.scalar.copy(flipped[:], summed)
-                back = banks[2 + th][:].rearrange("p (j t) -> p j t", j=4)
+                back = banks[back_banks[th]][:].rearrange("p (j t) -> p j t", j=4)
                 for j in range(4):
                     nc.tensor.transpose(back[:, j, :], flipped[:, j, :], ident[:])
                 res = held([P, BANK], F32, "res%d_%d" % (nb, th))
-                nc.scalar.copy(res[:], banks[2 + th][:])
+                nc.scalar.copy(res[:], banks[back_banks[th]][:])
                 nc.scalar.dma_start(out[nb * P : (nb + 1) * P, th * BANK : (th + 1) * BANK], res[:])
 
         def finish_on_vector(nb):
@@ -223,49 +220,65 @@ def tile_moe_adp_silu_kernel(
 
         y = [held([P, 2, E * C], F32, "y%d" % h) for h in range(2)]
 
-        def second_layer_middle_adapters(nb, bank):
-            dst = y[nb // 2][:, nb % 2, C : 3 * C].rearrange("p (j s) -> p j s", s=C)
-            second_layer(bank, [(1, nb), (2, nb)], dst)
+        def second_layer_one(e, nb, bank):
+            second_layer(bank, [(e, nb)], y[nb // 2][:, nb % 2 : nb % 2 + 1, e * C : (e + 1) * C])
 
-        def second_layer_last_adapter(h, bank):
-            second_layer(bank, [(3, 2 * h), (3, 2 * h + 1)], y[h][:, :, 3 * C : 4 * C])
+        def second_layer_last_two(nb, bank):
+            dst = y[nb // 2][:, nb % 2, 2 * C : 4 * C].rearrange("p (j s) -> p j s", s=C)
+            second_layer(bank, [(2, nb), (3, nb)], dst)
 
-        gather_scales(0, 3, held([P, 3 * C], U8, "xsg012"))
+        gather_scales(0, 2, held([P, 2 * C], U8, "xsg01"))
         gather_words(0, 1)
         gather_words(1, 2)
         for e in range(1, E):
             gather_words(2 * e, 2 * e + 2)
 
-        hidden_first_adapter()
+        turn(0, 0, 0, 2)
+        gather_scales(2, 3, keep.tile([P, C], U8, name="xsg2", tag="xg0", align_bytes=64))
+        turn(0, 1, 1, 3)
+        quantise_first_chunk(0)
         gather_scales(3, 4, in_h_buffer(0, [P, C], U8, "xsg3"))
-        win[0] = held([P, T], F32, "win0")
-        first_scatter(0, banks[4])
-        first_scatter(1, banks[6])
-        second_layer(banks[5], [(0, 1)], y[0][:, 1:2, 0:C])
-        hidden(1, (0, 1))
-        win[1] = in_h_buffer(1, [P, 2 * T], F32, "win1")
-        scatter(1, 0, 2)
-        second_layer(banks[7], [(0, 2)], y[1][:, 0:1, 0:C])
-        hidden(2, (5, 1))
-        win[2] = in_h_buffer(2, [P, 2 * T], F32, "win2")
+        quantise_first_chunk(1)
+        turn(1, 0, 0, 2)
+        second_layer_chunk(0, [0], banks[4])
+        scatter(0, 0, 1)
+        second_layer_chunk(0, [1], banks[5])
+        scatter(1, 0, 1)
+        second_layer_chunk(1, [0, 1], banks[6])
+        scatter(0, 1, 2)
+        scatter(1, 1, 2)
+        turn(1, 1, 4, 2)
+        second_layer_one(0, 2, banks[7])
         scatter(2, 0, 2)
-        hidden(3, (0, 1))
-
-        second_layer_middle_adapters(0, banks[1])
-        scatter(0, 2, 6)
-        second_layer_last_adapter(0, banks[6])
-        scatter(0, 6, CHUNKS)
-        second_layer_middle_adapters(1, banks[2])
-        scatter(1, 2, CHUNKS)
-        second_layer_middle_adapters(2, banks[4])
-        second_layer_last_adapter(1, banks[5])
-        second_layer_middle_adapters(3, banks[7])
-        second_layer(banks[6], [(0, 3)], y[1][:, 1:2, 0:C])
-        bases = [frozen_to_sbuf(nb) for nb in range(ROW_BLOCKS - 1)]
-        finish_on_tensor(0, bases[0], (0, 1))
+        quantise(1, 2)
+        second_layer_one(0, 3, banks[4])
+        scatter(3, 0, 2)
+        turn(2, 0, 5, 3)
+        turn(2, 1, 6, 3)
+        quantise(2, 3)
+        turn(3, 0, 7, 2)
+        turn(3, 1, 4, 2)
+        second_layer_one(1, 0, banks[7])
+        scatter(0, 2, 4)
+        quantise(3, 2)
+        second_layer_one(1, 1, banks[4])
+        scatter(1, 2, 4)
+        frozen_to_sbuf(0, 0, banks[5])
+        frozen_to_sbuf(0, 1, banks[6])
+        frozen_to_sbuf(1, 0, banks[3])
+        frozen_to_sbuf(1, 1, banks[7])
+        second_layer_last_two(0, banks[5])
+        scatter(0, 4, CHUNKS)
+        second_layer_last_two(1, banks[6])
+        scatter(1, 4, CHUNKS)
+        second_layer(banks[3], [(1, 2), (1, 3)], y[1][:, :, C : 2 * C])
+        second_layer_last_two(2, banks[7])
         scatter(2, 2, CHUNKS)
-        finish_on_tensor(1, bases[1], (1, 0))
-        win[3] = held([P, 2 * T], F32, "win3")
-        scatter(3, 0, CHUNKS)
-        finish_on_tensor(2, bases[2], (0, 1))
+        second_layer_last_two(3, banks[2])
+        scatter(3, 2, CHUNKS)
+        frozen_to_sbuf(2, 0, banks[4])
+        frozen_to_sbuf(2, 1, banks[5])
+        finish_on_tensor(0, (4, 5), (0, 1))
+        finish_on_tensor(1, (5, 0), (1, 4))
+        finish_on_tensor(2, (0, 1), (4, 5))
         finish_on_vector(3)

@@ -64,9 +64,9 @@ def tile_moe_adp_silu_kernel(
                 xs[32 * q : 32 * q + 32, :].bitcast(I32),
                 four_rows.unsqueeze(0).broadcast_to([8, 4, T // 4]),
             )
+        load_adapter_planes(was, wa_scales, range(4), nc.scalar)
         xw = load_words(x_words[0], "xw")
         wa0 = load_words(wa_words[0, 0], "wa0")
-        load_adapter_planes(was, wa_scales, range(4), nc.sync)
         wa1 = load_words(wa_words[1, 0], "wa1")
         wb0 = load_words(wb_words[0, 0], "wb0")
         load_adapter_planes(wbs, wb_scales, range(4), nc.sync)
@@ -185,7 +185,7 @@ def tile_moe_adp_silu_kernel(
 
         def frozen_to_sbuf(nb, th, bank):
             frozen(nb, th, bank)
-            base[nb, th] = held([P, BANK], F32, "base%d_%d" % (nb, th))
+            base[nb, th] = keep.tile([P, BANK], F32, name="base%d_%d" % (nb, th), tag="base%d_%d" % (nb, th), align_bytes=64)
             nc.scalar.copy(base[nb, th][:], bank[:])
 
         def finish_on_tensor(nb, sum_banks, back_banks):
@@ -206,17 +206,16 @@ def tile_moe_adp_silu_kernel(
                 nc.scalar.copy(res[:], banks[back_banks[th]][:])
                 nc.scalar.dma_start(out[nb * P : (nb + 1) * P, th * BANK : (th + 1) * BANK], res[:])
 
-        def finish_on_vector(nb):
+        def finish_on_vector(nb, base_banks):
+            res = keep.tile([P, T], F32, name="last", tag="base1_1", align_bytes=64)
             for th in range(2):
-                frozen(nb, th, banks[th])
                 width = BANK // 2 if th else BANK
                 for col in range(0, BANK, width):
-                    t0 = th * BANK + col
-                    res = held([P, width], F32, "last%d" % t0)
+                    cols = slice(th * BANK + col, th * BANK + col + width)
                     nc.vector.tensor_tensor(
-                        res[:], banks[th][:, col : col + width], win[nb][:, t0 : t0 + width], ALU.add
+                        res[:, cols], banks[base_banks[th]][:, col : col + width], win[nb][:, cols], ALU.add
                     )
-                    nc.sync.dma_start(out[nb * P : (nb + 1) * P, t0 : t0 + width], res[:])
+                    nc.sync.dma_start(out[nb * P : (nb + 1) * P, cols], res[:, cols])
 
         y = [held([P, 2, E * C], F32, "y%d" % h) for h in range(2)]
 
@@ -278,7 +277,9 @@ def tile_moe_adp_silu_kernel(
         scatter(3, 2, CHUNKS)
         frozen_to_sbuf(2, 0, banks[4])
         frozen_to_sbuf(2, 1, banks[5])
+        frozen(3, 0, banks[6])
+        frozen(3, 1, banks[3])
         finish_on_tensor(0, (4, 5), (0, 1))
         finish_on_tensor(1, (5, 0), (1, 4))
         finish_on_tensor(2, (0, 1), (4, 5))
-        finish_on_vector(3)
+        finish_on_vector(3, (6, 3))

@@ -21,6 +21,8 @@ P = 128
 BANK = 512
 ROW_BLOCKS = N // P
 CHUNKS = E * C // P
+QUARTER = T // 4
+GPSIMD_COLS = QUARTER
 LIST_COLS = P // 16
 
 
@@ -67,9 +69,9 @@ def tile_moe_adp_silu_kernel(
         load_adapter_planes(was, wa_scales, range(4), nc.scalar)
         xw = load_words(x_words[0], "xw")
         wa0 = load_words(wa_words[0, 0], "wa0")
-        wa1 = load_words(wa_words[1, 0], "wa1")
         wb0 = load_words(wb_words[0, 0], "wb0")
         load_adapter_planes(wbs, wb_scales, range(4), nc.sync)
+        wa1 = load_words(wa_words[1, 0], "wa1")
         g = held([P, E * C], F32, "g")
         nc.sync.dma_start(g[:, 0:C], gate[:, 0:C])
         wa_rest = held([P, E - 2, H], I32, "wa_rest")
@@ -156,7 +158,7 @@ def tile_moe_adp_silu_kernel(
                 )
             nc.scalar.copy(dst, bank[:, 0 : len(pieces) * C].rearrange("p (j s) -> p j s", s=C))
 
-        def second_layer_chunk(half, blocks, bank):
+        def second_layer_chunk(half, blocks, bank, copy):
             cols = slice(half * P, (half + 1) * P)
             for j, nb in enumerate(blocks):
                 rows = slice(nb * P, (nb + 1) * P)
@@ -164,7 +166,7 @@ def tile_moe_adp_silu_kernel(
                     bank[:, j * P : (j + 1) * P], lhsT=wb[0][:, rows].bitcast(FP8X4), lhsT_scale=wbs[:, rows],
                     rhs=hq[0][:, cols].bitcast(FP8X4), rhs_scale=hs[0][:, cols], start=True, stop=True,
                 )
-            nc.scalar.copy(
+            copy(
                 y[0][:, blocks[0] : blocks[-1] + 1, cols],
                 bank[:, 0 : len(blocks) * P].rearrange("p (j s) -> p j s", s=P),
             )
@@ -208,29 +210,31 @@ def tile_moe_adp_silu_kernel(
 
         def finish_on_vector(nb, base_banks):
             res = keep.tile([P, T], F32, name="last", tag="base1_1", align_bytes=64)
-            for th in range(2):
-                width = BANK // 2 if th else BANK
-                for col in range(0, BANK, width):
-                    cols = slice(th * BANK + col, th * BANK + col + width)
-                    nc.vector.tensor_tensor(
-                        res[:, cols], banks[base_banks[th]][:, col : col + width], win[nb][:, cols], ALU.add
-                    )
-                    nc.sync.dma_start(out[nb * P : (nb + 1) * P, cols], res[:, cols])
+            for col, end in ((0, P), (P, BANK), (BANK, T - GPSIMD_COLS)):
+                th, off = divmod(col, BANK)
+                cols = slice(col, end)
+                nc.vector.tensor_tensor(
+                    res[:, cols], banks[base_banks[th]][:, off : off + end - col], win[nb][:, cols], ALU.add
+                )
+                nc.sync.dma_start(out[nb * P : (nb + 1) * P, cols], res[:, cols])
+            cols = slice(T - GPSIMD_COLS, T)
+            nc.gpsimd.tensor_tensor(res[:, cols], base_tail[:], win[nb][:, cols], ALU.add)
+            nc.sync.dma_start(out[nb * P : (nb + 1) * P, cols], res[:, cols])
 
         y = [held([P, 2, E * C], F32, "y%d" % h) for h in range(2)]
 
         def second_layer_one(e, nb, bank):
             second_layer(bank, [(e, nb)], y[nb // 2][:, nb % 2 : nb % 2 + 1, e * C : (e + 1) * C])
 
-        def second_layer_last_two(nb, bank):
-            dst = y[nb // 2][:, nb % 2, 2 * C : 4 * C].rearrange("p (j s) -> p j s", s=C)
-            second_layer(bank, [(2, nb), (3, nb)], dst)
+        def second_layer_pair(e, nb, bank):
+            dst = y[nb // 2][:, nb % 2, e * C : (e + 2) * C].rearrange("p (j s) -> p j s", s=C)
+            second_layer(bank, [(e, nb), (e + 1, nb)], dst)
 
         gather_scales(0, 2, held([P, 2 * C], U8, "xsg01"))
         gather_words(0, 1)
         gather_words(1, 2)
-        for e in range(1, E):
-            gather_words(2 * e, 2 * e + 2)
+        gather_words(2, 4)
+        gather_words(4, CHUNKS)
 
         turn(0, 0, 0, 2)
         gather_scales(2, 3, keep.tile([P, C], U8, name="xsg2", tag="xg0", align_bytes=64))
@@ -239,47 +243,47 @@ def tile_moe_adp_silu_kernel(
         gather_scales(3, 4, in_h_buffer(0, [P, C], U8, "xsg3"))
         quantise_first_chunk(1)
         turn(1, 0, 0, 2)
-        second_layer_chunk(0, [0], banks[4])
+        turn(1, 1, 1, 2)
+        second_layer_chunk(0, [0], banks[4], nc.vector.tensor_copy)
         scatter(0, 0, 1)
-        second_layer_chunk(0, [1], banks[5])
-        scatter(1, 0, 1)
-        second_layer_chunk(1, [0, 1], banks[6])
+        second_layer_one(0, 1, banks[5])
+        scatter(1, 0, 2)
+        second_layer_chunk(1, [0], banks[6], nc.scalar.copy)
         scatter(0, 1, 2)
-        scatter(1, 1, 2)
-        turn(1, 1, 4, 2)
-        second_layer_one(0, 2, banks[7])
-        scatter(2, 0, 2)
         quantise(1, 2)
-        second_layer_one(0, 3, banks[4])
-        scatter(3, 0, 2)
+        second_layer_one(0, 2, banks[1])
+        scatter(2, 0, 2)
         turn(2, 0, 5, 3)
         turn(2, 1, 6, 3)
         quantise(2, 3)
         turn(3, 0, 7, 2)
-        turn(3, 1, 4, 2)
-        second_layer_one(1, 0, banks[7])
+        second_layer_one(1, 0, banks[6])
         scatter(0, 2, 4)
+        turn(3, 1, 1, 2)
         quantise(3, 2)
-        second_layer_one(1, 1, banks[4])
+        second_layer_one(1, 1, banks[1])
         scatter(1, 2, 4)
         frozen_to_sbuf(0, 0, banks[5])
-        frozen_to_sbuf(0, 1, banks[6])
-        frozen_to_sbuf(1, 0, banks[3])
-        frozen_to_sbuf(1, 1, banks[7])
-        second_layer_last_two(0, banks[5])
+        frozen_to_sbuf(0, 1, banks[3])
+        second_layer_pair(2, 0, banks[6])
         scatter(0, 4, CHUNKS)
-        second_layer_last_two(1, banks[6])
+        frozen_to_sbuf(1, 0, banks[7])
+        frozen_to_sbuf(1, 1, banks[0])
+        second_layer_pair(2, 1, banks[2])
         scatter(1, 4, CHUNKS)
-        second_layer(banks[3], [(1, 2), (1, 3)], y[1][:, :, C : 2 * C])
-        second_layer_last_two(2, banks[7])
+        second_layer_pair(0, 3, banks[5])
+        second_layer_one(1, 2, banks[3])
+        second_layer_pair(2, 2, banks[6])
         scatter(2, 2, CHUNKS)
-        second_layer_last_two(3, banks[2])
-        scatter(3, 2, CHUNKS)
-        frozen_to_sbuf(2, 0, banks[4])
-        frozen_to_sbuf(2, 1, banks[5])
-        frozen(3, 0, banks[6])
-        frozen(3, 1, banks[3])
-        finish_on_tensor(0, (4, 5), (0, 1))
-        finish_on_tensor(1, (5, 0), (1, 4))
-        finish_on_tensor(2, (0, 1), (4, 5))
-        finish_on_vector(3, (6, 3))
+        second_layer_pair(2, 3, banks[7])
+        scatter(3, 0, CHUNKS)
+        frozen(3, 0, banks[2])
+        frozen(3, 1, banks[5])
+        finish_on_tensor(0, (7, 6), (3, 0))
+        frozen_to_sbuf(2, 0, banks[1])
+        frozen_to_sbuf(2, 1, banks[4])
+        base_tail = held([P, GPSIMD_COLS], F32, "base_tail")
+        nc.scalar.copy(base_tail[:], banks[5][:, BANK - GPSIMD_COLS : BANK])
+        finish_on_tensor(1, (6, 3), (0, 7))
+        finish_on_tensor(2, (3, 0), (7, 6))
+        finish_on_vector(3, (2, 5))

@@ -73,14 +73,14 @@ def tile_moe_adp_silu_kernel(
         load_adapter_planes(wbs, wb_scales, range(4), nc.sync)
         wa1 = load_words(wa_words[1, 0], "wa1")
         g = held([P, E * C], F32, "g")
-        nc.sync.dma_start(g[:, 0:C], gate[:, 0:C])
+        nc.sync.dma_start(g[:], gate)
+        wb1 = load_words(wb_words[1, 0], "wb1")
         wa_rest = held([P, E - 2, H], I32, "wa_rest")
         nc.sync.dma_start(wa_rest[:], wa_words[2:E, 0].rearrange("e p c d -> p e (c d)").bitcast(I32))
-        wb_rest = held([P, E - 1, N], I32, "wb_rest")
-        nc.sync.dma_start(wb_rest[:], wb_words[1:E, 0].rearrange("e p c d -> p e (c d)").bitcast(I32))
-        nc.sync.dma_start(g[:, C : E * C], gate[:, C : E * C])
+        wb_rest = held([P, E - 2, N], I32, "wb_rest")
+        nc.sync.dma_start(wb_rest[:], wb_words[2:E, 0].rearrange("e p c d -> p e (c d)").bitcast(I32))
         wa = [wa0[:], wa1[:]] + [wa_rest[:, e, :] for e in range(E - 2)]
-        wb = [wb0[:]] + [wb_rest[:, e, :] for e in range(E - 1)]
+        wb = [wb0[:], wb1[:]] + [wb_rest[:, e, :] for e in range(E - 2)]
         ww = held([P, 2 * N], U8, "ww")
         nc.sync.dma_start(ww[:].bitcast(I32), w_words[0].bitcast(I32))
         for r in range(4):
@@ -106,23 +106,28 @@ def tile_moe_adp_silu_kernel(
             for e in range(e0, e1):
                 xsg[e] = tile[:, (e - e0) * C : (e - e0 + 1) * C]
 
-        def gather_words(c0, c1):
-            tile = keep.tile([P, (c1 - c0) * P], U32, name="xg%d" % c0, tag="xg%d" % c0, align_bytes=64)
+        def gather_words(c0, c1, buffer):
+            tile = keep.tile([P, (c1 - c0) * P], U32, name="xg%d" % c0, tag=buffer, align_bytes=64)
             nc.vector.tensor_copy(tile[:], xw[:].bitcast(U32).indirect(entries(c0, c1)))
             for c in range(c0, c1):
                 xg[c] = tile[:, (c - c0) * P : (c - c0 + 1) * P]
 
         def turn_hidden_chunk(e, half, pre, turned):
-            nc.tensor.matmul_mx(
-                pre[:], lhsT=xg[2 * e + half].bitcast(FP8X4), lhsT_scale=xsg[e][:, half * P : (half + 1) * P],
-                rhs=wa[e].bitcast(FP8X4), rhs_scale=was[4 * e : P, :], start=True, stop=True,
-            )
             hrow = ring.tile([P, H], BF16, tag="hrow", name="hrow", align_bytes=64)
-            nc.scalar.activation(
-                hrow[:].rearrange("s (u p b) -> s u p b", u=2, b=2),
-                pre[:].rearrange("s (p u b) -> s u p b", u=2, b=2),
-                ACT.Silu,
-            )
+            width = H // len(pre)
+            for part, bank in enumerate(pre):
+                cols = slice(part * width, (part + 1) * width)
+                nc.tensor.matmul_mx(
+                    bank[:, 0:width], lhsT=xg[2 * e + half].bitcast(FP8X4),
+                    lhsT_scale=xsg[e][:, half * P : (half + 1) * P],
+                    rhs=wa[e][:, cols].bitcast(FP8X4), rhs_scale=was[4 * e : P, cols], start=True, stop=True,
+                )
+                p0, p1 = cols.start // 4, cols.stop // 4
+                nc.scalar.activation(
+                    hrow[:].rearrange("s (u p b) -> s u p b", u=2, b=2)[:, :, p0:p1, :],
+                    bank[:, 0:width].rearrange("s (p u b) -> s u p b", u=2, b=2),
+                    ACT.Silu,
+                )
             pairs = hrow[:].bitcast(F32)
             for u in range(2):
                 nc.tensor.transpose(turned[:, u, :], pairs[:, u * P : (u + 1) * P], ident[:])
@@ -136,10 +141,10 @@ def tile_moe_adp_silu_kernel(
             )
             nc.vector.quantize_mx(hq[0][:, cols].bitcast(FP8X4), hs[0][:, cols], hcol[:])
 
-        def turn(e, half, pre_bank, turn_bank):
+        def turn(e, half, pre_banks, turn_bank):
             off = half * 2 * P if e else 0
             turned = banks[turn_bank][:, off : off + 2 * P].rearrange("p (u s) -> p u s", u=2)
-            turn_hidden_chunk(e, half, banks[pre_bank], turned)
+            turn_hidden_chunk(e, half, [banks[b] for b in pre_banks], turned)
 
         def quantise(e, turn_bank):
             hcol = held([P, 4 * C], BF16, "hcol%d_" % e)
@@ -230,20 +235,20 @@ def tile_moe_adp_silu_kernel(
             dst = y[nb // 2][:, nb % 2, e * C : (e + 2) * C].rearrange("p (j s) -> p j s", s=C)
             second_layer(bank, [(e, nb), (e + 1, nb)], dst)
 
-        gather_scales(0, 2, held([P, 2 * C], U8, "xsg01"))
-        gather_words(0, 1)
-        gather_words(1, 2)
-        gather_words(2, 4)
-        gather_words(4, CHUNKS)
+        gather_scales(0, 1, held([P, C], U8, "xsg0"))
+        gather_words(0, 1, "xg0")
+        gather_words(1, 2, "xg1")
+        gather_words(2, 4, "xg2")
+        gather_words(4, CHUNKS, "xg4")
 
-        turn(0, 0, 0, 2)
-        gather_scales(2, 3, keep.tile([P, C], U8, name="xsg2", tag="xg0", align_bytes=64))
-        turn(0, 1, 1, 3)
+        turn(0, 0, (0, 7), 2)
+        gather_scales(1, 3, keep.tile([P, 2 * C], U8, name="xsg12", tag="xg0", align_bytes=64))
+        turn(0, 1, (1,), 3)
         quantise_first_chunk(0)
         gather_scales(3, 4, in_h_buffer(0, [P, C], U8, "xsg3"))
         quantise_first_chunk(1)
-        turn(1, 0, 0, 2)
-        turn(1, 1, 1, 2)
+        turn(1, 0, (0,), 2)
+        turn(1, 1, (1,), 2)
         second_layer_chunk(0, [0], banks[4], nc.vector.tensor_copy)
         scatter(0, 0, 1)
         second_layer_one(0, 1, banks[5])
@@ -253,13 +258,13 @@ def tile_moe_adp_silu_kernel(
         quantise(1, 2)
         second_layer_one(0, 2, banks[1])
         scatter(2, 0, 2)
-        turn(2, 0, 5, 3)
-        turn(2, 1, 6, 3)
+        turn(2, 0, (5,), 3)
+        turn(2, 1, (6,), 3)
         quantise(2, 3)
-        turn(3, 0, 7, 2)
+        turn(3, 0, (7,), 2)
         second_layer_one(1, 0, banks[6])
         scatter(0, 2, 4)
-        turn(3, 1, 1, 2)
+        turn(3, 1, (1,), 2)
         quantise(3, 2)
         second_layer_one(1, 1, banks[1])
         scatter(1, 2, 4)

@@ -196,14 +196,17 @@ def tile_moe_adp_silu_kernel(
             nc.scalar.copy(base[nb, th][:], bank[:])
 
         def finish_on_tensor(nb, sum_banks, back_banks):
+            summed_halves = [banks[b][:].rearrange("p (j n) -> p j n", j=4) for b in sum_banks]
             for th in range(2):
-                summed = banks[sum_banks[th]][:].rearrange("p (j n) -> p j n", j=4)
+                for j in range(4):
+                    nc.tensor.matmul(summed_halves[th][:, j, :], base[nb, th][:, j * P : (j + 1) * P], ident[:],
+                                     start=j == 0, stop=False, is_transpose=True)
+            for th in range(2):
+                summed = summed_halves[th]
                 for j in range(4):
                     t0 = th * BANK + j * P
-                    nc.tensor.matmul(summed[:, j, :], base[nb, th][:, j * P : (j + 1) * P], ident[:],
-                                     start=True, stop=False, is_transpose=True)
                     nc.tensor.matmul(summed[:, j, :], win[nb][:, t0 : t0 + P], ident[:],
-                                     start=False, stop=True, is_transpose=True)
+                                     start=False, stop=j == 3, is_transpose=True)
                 flipped = ring.tile([P, 4, P], F32, tag="flipped", name="flipped")
                 nc.scalar.copy(flipped[:], summed)
                 back = banks[back_banks[th]][:].rearrange("p (j t) -> p j t", j=4)
@@ -289,6 +292,6 @@ def tile_moe_adp_silu_kernel(
         frozen_to_sbuf(2, 1, banks[4])
         base_tail = held([P, GPSIMD_COLS], F32, "base_tail")
         nc.scalar.copy(base_tail[:], banks[5][:, BANK - GPSIMD_COLS : BANK])
-        finish_on_tensor(1, (6, 3), (0, 7))
-        finish_on_tensor(2, (3, 0), (7, 6))
+        finish_on_tensor(1, (3, 0), (7, 6))
+        finish_on_tensor(2, (7, 6), (3, 0))
         finish_on_vector(3, (2, 5))

@@ -19,10 +19,8 @@ ALU = mybir.AluOpType
 
 P = 128
 BANK = 512
-ROW_BLOCKS = N // P
 CHUNKS = E * C // P
-QUARTER = T // 4
-GPSIMD_COLS = QUARTER
+GPSIMD_COLS = T // 4
 LIST_COLS = P // 16
 
 
@@ -35,8 +33,8 @@ def tile_moe_adp_silu_kernel(
         ring = ctx.enter_context(tc.tile_pool(name="ring", bufs=2))
         psum = ctx.enter_context(tc.psum_pool(name="psum", bufs=1))
 
-        def held(shape, dtype, name):
-            return keep.tile(shape, dtype, name=name, align_bytes=64)
+        def held(shape, dtype, name, tag=None):
+            return keep.tile(shape, dtype, name=name, tag=tag or name, align_bytes=64)
 
         offsets = keep.tile([P, E * C // 16], U16, name="offsets")
         nc.sync.dma_start(offsets[:], offs)
@@ -49,16 +47,20 @@ def tile_moe_adp_silu_kernel(
         nc.vector.memset(wbs[:].bitcast(I32), 0)
         nc.vector.memset(ws[:].bitcast(I32), 0)
 
-        def load_adapter_planes(plane, scales, quadrants, queue):
-            for q in quadrants:
-                queue.dma_start(
-                    plane[32 * q : 32 * q + 16, :].bitcast(I32), scales[:, 0, 4 * q : 4 * q + 4, :].bitcast(I32)
-                )
+        def load_adapter_plane(plane, scales, q, queue):
+            queue.dma_start(
+                plane[32 * q : 32 * q + 16, :].bitcast(I32), scales[:, 0, 4 * q : 4 * q + 4, :].bitcast(I32)
+            )
 
         def load_words(src, name):
             words = held([P, src.shape[1]], I32, name)
             nc.sync.dma_start(words[:], src.rearrange("p c d -> p (c d)").bitcast(I32))
             return words
+
+        def load_many(src, name):
+            words = held([P, src.shape[0], src.shape[2]], I32, name)
+            nc.sync.dma_start(words[:], src.rearrange("e p c d -> p e (c d)").bitcast(I32))
+            return [words[:, e, :] for e in range(src.shape[0])]
 
         for q in range(4):
             four_rows = x_scales[0][4 * q : 4 * q + 4, :].bitcast(I32)
@@ -66,21 +68,23 @@ def tile_moe_adp_silu_kernel(
                 xs[32 * q : 32 * q + 32, :].bitcast(I32),
                 four_rows.unsqueeze(0).broadcast_to([8, 4, T // 4]),
             )
-        load_adapter_planes(was, wa_scales, range(4), nc.scalar)
+        for q in range(4):
+            load_adapter_plane(was, wa_scales, q, nc.scalar)
         xw = load_words(x_words[0], "xw")
         wa0 = load_words(wa_words[0, 0], "wa0")
         wb0 = load_words(wb_words[0, 0], "wb0")
-        load_adapter_planes(wbs, wb_scales, range(4), nc.sync)
+        for q in range(4):
+            load_adapter_plane(wbs, wb_scales, q, nc.sync)
+        g0 = held([P, C], F32, "g0")
+        nc.sync.dma_start(g0[:], gate[:, 0:C])
         wa1 = load_words(wa_words[1, 0], "wa1")
-        g = held([P, E * C], F32, "g")
-        nc.sync.dma_start(g[:], gate)
-        wb1 = load_words(wb_words[1, 0], "wb1")
-        wa_rest = held([P, E - 2, H], I32, "wa_rest")
-        nc.sync.dma_start(wa_rest[:], wa_words[2:E, 0].rearrange("e p c d -> p e (c d)").bitcast(I32))
-        wb_rest = held([P, E - 2, N], I32, "wb_rest")
-        nc.sync.dma_start(wb_rest[:], wb_words[2:E, 0].rearrange("e p c d -> p e (c d)").bitcast(I32))
-        wa = [wa0[:], wa1[:]] + [wa_rest[:, e, :] for e in range(E - 2)]
-        wb = [wb0[:], wb1[:]] + [wb_rest[:, e, :] for e in range(E - 2)]
+        wa = [wa0[:], wa1[:]] + load_many(wa_words[2:E, 0], "wa_rest")
+        wb = [wb0[:]] + load_many(wb_words[1:E, 0], "wb_rest")
+        g1 = held([P, (E - 1) * C], F32, "g1")
+        nc.sync.dma_start(g1[:], gate[:, C : E * C])
+        gcol = held([P, CHUNKS - 2], F32, "gcol")
+        with nc.allow_non_contiguous_dma(reason="one gate value a slot, slots on the partitions"):
+            nc.sync.dma_start(gcol[:], gate[0:1, C : E * C].rearrange("o (c p) -> p (o c)", p=P))
         ww = held([P, 2 * N], U8, "ww")
         nc.sync.dma_start(ww[:].bitcast(I32), w_words[0].bitcast(I32))
         for r in range(4):
@@ -92,206 +96,198 @@ def tile_moe_adp_silu_kernel(
         def entries(c0, c1):
             return offsets[:, c0 * LIST_COLS : c1 * LIST_COLS]
 
-        def in_h_buffer(e, shape, dtype, name):
-            return keep.tile(shape, dtype, name=name, tag="hcol%d" % e, align_bytes=64)
+        def gate_rows(c0, c1):
+            return g0[:, c0 * P : c1 * P] if c1 <= 2 else g1[:, (c0 - 2) * P : (c1 - 2) * P]
 
         banks = [psum.tile([P, BANK], F32, name="bank%d" % b) for b in range(8)]
         xg, xsg, base = {}, {}, {}
         hq = [held([P, C], U32, "hq%d" % e) for e in range(E)]
         hs = [held([P, C], U8, "hs%d" % e) for e in range(E)]
-        win = [held([P, T if nb < 2 else 2 * T], F32, "win%d" % nb) for nb in range(ROW_BLOCKS)]
+        win = [held([P, T], F32, "win%d" % nb) for nb in range(4)]
+        y_front = held([P, 2, E * C], F32, "y_front")
+        y_back = held([P, 2, (E - 1) * C], F32, "y_back")
 
-        def gather_scales(e0, e1, tile):
+        def gather_scales(e0, e1, buffer):
+            tile = held([P, (e1 - e0) * C], U8, "xsg%d" % e0, buffer)
             nc.vector.tensor_copy(tile[:], xs[:].indirect(entries(2 * e0, 2 * e1)))
             for e in range(e0, e1):
                 xsg[e] = tile[:, (e - e0) * C : (e - e0 + 1) * C]
 
-        def gather_words(c0, c1, buffer):
-            tile = keep.tile([P, (c1 - c0) * P], U32, name="xg%d" % c0, tag=buffer, align_bytes=64)
+        def gather_words(c0, c1):
+            tile = held([P, (c1 - c0) * P], U32, "xg%d" % c0)
             nc.vector.tensor_copy(tile[:], xw[:].bitcast(U32).indirect(entries(c0, c1)))
             for c in range(c0, c1):
                 xg[c] = tile[:, (c - c0) * P : (c - c0 + 1) * P]
 
-        def turn_hidden_chunk(e, half, pre, turned):
-            hrow = ring.tile([P, H], BF16, tag="hrow", name="hrow", align_bytes=64)
+        hrow = {}
+
+        def first_layer(c, pre):
+            e, half = divmod(c, 2)
+            hrow[c] = held([P, H], BF16, "hrow%d" % c)
             width = H // len(pre)
-            for part, bank in enumerate(pre):
+            for part, b in enumerate(pre):
                 cols = slice(part * width, (part + 1) * width)
                 nc.tensor.matmul_mx(
-                    bank[:, 0:width], lhsT=xg[2 * e + half].bitcast(FP8X4),
-                    lhsT_scale=xsg[e][:, half * P : (half + 1) * P],
+                    banks[b][:, 0:width], lhsT=xg[c].bitcast(FP8X4), lhsT_scale=xsg[e][:, half * P : (half + 1) * P],
                     rhs=wa[e][:, cols].bitcast(FP8X4), rhs_scale=was[4 * e : P, cols], start=True, stop=True,
                 )
                 p0, p1 = cols.start // 4, cols.stop // 4
                 nc.scalar.activation(
-                    hrow[:].rearrange("s (u p b) -> s u p b", u=2, b=2)[:, :, p0:p1, :],
-                    bank[:, 0:width].rearrange("s (p u b) -> s u p b", u=2, b=2),
+                    hrow[c][:].rearrange("s (u p b) -> s u p b", u=2, b=2)[:, :, p0:p1, :],
+                    banks[b][:, 0:width].rearrange("s (p u b) -> s u p b", u=2, b=2),
                     ACT.Silu,
                 )
-            pairs = hrow[:].bitcast(F32)
+
+        def turn(c, b, off):
+            pairs = hrow[c][:].bitcast(F32)
             for u in range(2):
-                nc.tensor.transpose(turned[:, u, :], pairs[:, u * P : (u + 1) * P], ident[:])
-
-        def quantise_first_chunk(half):
-            cols = slice(half * P, (half + 1) * P)
-            turned = banks[2 + half][:, 0 : 2 * P].rearrange("p (u s) -> p u s", u=2)
-            hcol = held([P, 4 * P], BF16, "half1") if half else in_h_buffer(0, [P, 4 * P], BF16, "half0")
-            nc.scalar.copy(
-                hcol[:].bitcast(F32).rearrange("p (s u) -> p s u", u=2), turned.rearrange("p u s -> p s u")
-            )
-            nc.vector.quantize_mx(hq[0][:, cols].bitcast(FP8X4), hs[0][:, cols], hcol[:])
-
-        def turn(e, half, pre_banks, turn_bank):
-            off = half * 2 * P if e else 0
-            turned = banks[turn_bank][:, off : off + 2 * P].rearrange("p (u s) -> p u s", u=2)
-            turn_hidden_chunk(e, half, [banks[b] for b in pre_banks], turned)
-
-        def quantise(e, turn_bank):
-            hcol = held([P, 4 * C], BF16, "hcol%d_" % e)
-            nc.scalar.copy(
-                hcol[:].bitcast(F32).rearrange("p (c s u) -> p c s u", c=2, u=2),
-                banks[turn_bank][:].rearrange("p (c u s) -> p c s u", c=2, u=2),
-            )
-            nc.vector.quantize_mx(hq[e][:].bitcast(FP8X4), hs[e][:], hcol[:])
-
-        def second_layer(bank, pieces, dst):
-            for j, (e, nb) in enumerate(pieces):
-                cols = slice(nb * P, (nb + 1) * P)
-                nc.tensor.matmul_mx(
-                    bank[:, j * C : (j + 1) * C], lhsT=wb[e][:, cols].bitcast(FP8X4), lhsT_scale=wbs[4 * e : P, cols],
-                    rhs=hq[e][:].bitcast(FP8X4), rhs_scale=hs[e][:], start=True, stop=True,
+                nc.tensor.transpose(
+                    banks[b][:, off + u * P : off + (u + 1) * P], pairs[:, u * P : (u + 1) * P], ident[:]
                 )
-            nc.scalar.copy(dst, bank[:, 0 : len(pieces) * C].rearrange("p (j s) -> p j s", s=C))
 
-        def second_layer_chunk(half, blocks, bank, copy):
-            cols = slice(half * P, (half + 1) * P)
+        def quantise(c0, c1, b, buffer):
+            n = c1 - c0
+            e, half = divmod(c0, 2)
+            cols = slice(half * P, (half + n) * P)
+            hcol = held([P, 4 * n * P], BF16, "hcol%d" % c0, buffer)
+            nc.scalar.copy(
+                hcol[:].bitcast(F32).rearrange("p (c s u) -> p c s u", c=n, u=2),
+                banks[b][:, 0 : 2 * n * P].rearrange("p (c u s) -> p c s u", c=n, u=2),
+            )
+            nc.vector.quantize_mx(hq[e][:, cols].bitcast(FP8X4), hs[e][:, cols], hcol[:])
+
+        def second_layer(c0, c1, blocks, b, dst):
+            e, half = divmod(c0, 2)
+            width = (c1 - c0) * P
+            cols = slice(half * P, half * P + width)
             for j, nb in enumerate(blocks):
                 rows = slice(nb * P, (nb + 1) * P)
                 nc.tensor.matmul_mx(
-                    bank[:, j * P : (j + 1) * P], lhsT=wb[0][:, rows].bitcast(FP8X4), lhsT_scale=wbs[:, rows],
-                    rhs=hq[0][:, cols].bitcast(FP8X4), rhs_scale=hs[0][:, cols], start=True, stop=True,
+                    banks[b][:, j * width : (j + 1) * width], lhsT=wb[e][:, rows].bitcast(FP8X4),
+                    lhsT_scale=wbs[4 * e : P, rows], rhs=hq[e][:, cols].bitcast(FP8X4), rhs_scale=hs[e][:, cols],
+                    start=True, stop=True,
                 )
-            copy(
-                y[0][:, blocks[0] : blocks[-1] + 1, cols],
-                bank[:, 0 : len(blocks) * P].rearrange("p (j s) -> p j s", s=P),
-            )
+            nc.scalar.copy(dst, banks[b][:, 0 : len(blocks) * width].rearrange("p (j s) -> p j s", s=width))
 
-        def scatter(nb, c0, c1):
+        def scatter_gated(nb, c0, c1, src):
+            nc.vector.tensor_tensor(win[nb][:].indirect(entries(c0, c1)), src, gate_rows(c0, c1), ALU.mult)
+
+        def front(c0, c1, b):
             cols = slice(c0 * P, c1 * P)
-            nc.vector.tensor_tensor(
-                win[nb][:].indirect(entries(c0, c1)), y[nb // 2][:, nb % 2, cols], g[:, cols], ALU.mult
+            second_layer(c0, c1, [0, 1], b, y_front[:, :, cols])
+            for nb in range(2):
+                scatter_gated(nb, c0, c1, y_front[:, nb, cols])
+
+        def first_back(nb, b, buffer):
+            y_first = held([P, 1, C], F32, "y_first%d" % nb, buffer)
+            second_layer(0, 2, [nb], b, y_first[:])
+            scatter_gated(nb, 0, 2, y_first[:, 0, :])
+
+        def back(e, b_slots, b_rows):
+            gated = ring.tile([P, 2, 2 * P], F32, tag="gated", name="gated", align_bytes=64)
+            cols = slice(2 * P, 4 * P)
+            for half in range(2):
+                slots = slice(half * P, (half + 1) * P)
+                nc.tensor.matmul_mx(
+                    banks[b_slots][:, half * C : (half + 1) * C], lhsT=hq[e][:, slots].bitcast(FP8X4),
+                    lhsT_scale=hs[e][:, slots], rhs=wb[e][:, cols].bitcast(FP8X4), rhs_scale=wbs[4 * e : P, cols],
+                    start=True, stop=True,
+                )
+            for half in range(2):
+                c = 2 * e + half
+                nc.scalar.activation(
+                    gated[:, half, :], banks[b_slots][:, half * C : (half + 1) * C], ACT.Copy,
+                    scale=gcol[:, c - 2 : c - 1],
+                )
+            for half in range(2):
+                for j in range(2):
+                    col = j * C + half * P
+                    nc.tensor.transpose(banks[b_rows][:, col : col + P], gated[:, half, j * P : (j + 1) * P], ident[:])
+            nc.scalar.copy(
+                y_back[:, :, (e - 1) * C : e * C], banks[b_rows][:].rearrange("p (j s) -> p j s", s=C)
             )
 
-        def frozen(nb, th, bank):
+        def frozen(nb, th, b):
             cols = slice(th * BANK, (th + 1) * BANK)
             nc.tensor.matmul_mx(
-                bank[:], lhsT=ww[:, 2 * nb * P : 2 * (nb + 1) * P].bitcast(FP4X4),
+                banks[b][:], lhsT=ww[:, 2 * nb * P : 2 * (nb + 1) * P].bitcast(FP4X4),
                 lhsT_scale=ws[:, nb * P : (nb + 1) * P],
                 rhs=xw[:, cols].bitcast(FP8X4), rhs_scale=xs[:, cols], start=True, stop=True,
             )
 
-        def frozen_to_sbuf(nb, th, bank):
-            frozen(nb, th, bank)
-            base[nb, th] = keep.tile([P, BANK], F32, name="base%d_%d" % (nb, th), tag="base%d_%d" % (nb, th), align_bytes=64)
-            nc.scalar.copy(base[nb, th][:], bank[:])
+        def frozen_to_sbuf(nb, two_banks):
+            base[nb] = held([P, T], F32, "base%d" % nb)
+            for th, b in enumerate(two_banks):
+                frozen(nb, th, b)
+                nc.scalar.copy(base[nb][:, th * BANK : (th + 1) * BANK], banks[b][:])
 
-        def finish_on_tensor(nb, sum_banks, back_banks):
-            summed_halves = [banks[b][:].rearrange("p (j n) -> p j n", j=4) for b in sum_banks]
-            for th in range(2):
-                for j in range(4):
-                    nc.tensor.matmul(summed_halves[th][:, j, :], base[nb, th][:, j * P : (j + 1) * P], ident[:],
-                                     start=j == 0, stop=False, is_transpose=True)
-            for th in range(2):
-                summed = summed_halves[th]
-                for j in range(4):
-                    t0 = th * BANK + j * P
-                    nc.tensor.matmul(summed[:, j, :], win[nb][:, t0 : t0 + P], ident[:],
-                                     start=False, stop=j == 3, is_transpose=True)
-                flipped = ring.tile([P, 4, P], F32, tag="flipped", name="flipped")
-                nc.scalar.copy(flipped[:], summed)
-                back = banks[back_banks[th]][:].rearrange("p (j t) -> p j t", j=4)
-                for j in range(4):
-                    nc.tensor.transpose(back[:, j, :], flipped[:, j, :], ident[:])
-                res = held([P, BANK], F32, "res%d_%d" % (nb, th))
-                nc.scalar.copy(res[:], banks[back_banks[th]][:])
-                nc.scalar.dma_start(out[nb * P : (nb + 1) * P, th * BANK : (th + 1) * BANK], res[:])
+        def finish_on_gpsimd(nb, buffer):
+            res = held([P, T], F32, "res%d" % nb, buffer)
+            nc.gpsimd.tensor_tensor(res[:], base[nb][:], win[nb][:], ALU.add)
+            nc.sync.dma_start(out[nb * P : (nb + 1) * P, :], res[:])
 
-        def finish_on_vector(nb, base_banks):
-            res = keep.tile([P, T], F32, name="last", tag="base1_1", align_bytes=64)
+        def finish_last(nb, base_banks):
+            res = held([P, T], F32, "last")
             for col, end in ((0, P), (P, BANK), (BANK, T - GPSIMD_COLS)):
                 th, off = divmod(col, BANK)
                 cols = slice(col, end)
                 nc.vector.tensor_tensor(
                     res[:, cols], banks[base_banks[th]][:, off : off + end - col], win[nb][:, cols], ALU.add
                 )
-                nc.sync.dma_start(out[nb * P : (nb + 1) * P, cols], res[:, cols])
+                nc.scalar.dma_start(out[nb * P : (nb + 1) * P, cols], res[:, cols])
             cols = slice(T - GPSIMD_COLS, T)
             nc.gpsimd.tensor_tensor(res[:, cols], base_tail[:], win[nb][:, cols], ALU.add)
-            nc.sync.dma_start(out[nb * P : (nb + 1) * P, cols], res[:, cols])
+            nc.scalar.dma_start(out[nb * P : (nb + 1) * P, cols], res[:, cols])
 
-        y = [held([P, 2, E * C], F32, "y%d" % h) for h in range(2)]
+        gather_scales(0, 1, None)
+        gather_words(0, 1)
+        gather_words(1, 2)
+        gather_words(2, 4)
+        gather_words(4, CHUNKS)
 
-        def second_layer_one(e, nb, bank):
-            second_layer(bank, [(e, nb)], y[nb // 2][:, nb % 2 : nb % 2 + 1, e * C : (e + 1) * C])
-
-        def second_layer_pair(e, nb, bank):
-            dst = y[nb // 2][:, nb % 2, e * C : (e + 2) * C].rearrange("p (j s) -> p j s", s=C)
-            second_layer(bank, [(e, nb), (e + 1, nb)], dst)
-
-        gather_scales(0, 1, held([P, C], U8, "xsg0"))
-        gather_words(0, 1, "xg0")
-        gather_words(1, 2, "xg1")
-        gather_words(2, 4, "xg2")
-        gather_words(4, CHUNKS, "xg4")
-
-        turn(0, 0, (0, 7), 2)
-        gather_scales(1, 3, keep.tile([P, 2 * C], U8, name="xsg12", tag="xg0", align_bytes=64))
-        turn(0, 1, (1,), 3)
-        quantise_first_chunk(0)
-        gather_scales(3, 4, in_h_buffer(0, [P, C], U8, "xsg3"))
-        quantise_first_chunk(1)
-        turn(1, 0, (0,), 2)
-        turn(1, 1, (1,), 2)
-        second_layer_chunk(0, [0], banks[4], nc.vector.tensor_copy)
-        scatter(0, 0, 1)
-        second_layer_one(0, 1, banks[5])
-        scatter(1, 0, 2)
-        second_layer_chunk(1, [0], banks[6], nc.scalar.copy)
-        scatter(0, 1, 2)
-        quantise(1, 2)
-        second_layer_one(0, 2, banks[1])
-        scatter(2, 0, 2)
-        turn(2, 0, (5,), 3)
-        turn(2, 1, (6,), 3)
-        quantise(2, 3)
-        turn(3, 0, (7,), 2)
-        second_layer_one(1, 0, banks[6])
-        scatter(0, 2, 4)
-        turn(3, 1, (1,), 2)
-        quantise(3, 2)
-        second_layer_one(1, 1, banks[1])
-        scatter(1, 2, 4)
-        frozen_to_sbuf(0, 0, banks[5])
-        frozen_to_sbuf(0, 1, banks[3])
-        second_layer_pair(2, 0, banks[6])
-        scatter(0, 4, CHUNKS)
-        frozen_to_sbuf(1, 0, banks[7])
-        frozen_to_sbuf(1, 1, banks[0])
-        second_layer_pair(2, 1, banks[2])
-        scatter(1, 4, CHUNKS)
-        second_layer_pair(0, 3, banks[5])
-        second_layer_one(1, 2, banks[3])
-        second_layer_pair(2, 2, banks[6])
-        scatter(2, 2, CHUNKS)
-        second_layer_pair(2, 3, banks[7])
-        scatter(3, 0, CHUNKS)
-        frozen(3, 0, banks[2])
-        frozen(3, 1, banks[5])
-        finish_on_tensor(0, (7, 6), (3, 0))
-        frozen_to_sbuf(2, 0, banks[1])
-        frozen_to_sbuf(2, 1, banks[4])
+        first_layer(0, (0, 7))
+        gather_scales(1, 2, "xg0")
+        first_layer(1, (1,))
+        turn(0, 2, 0)
+        quantise(0, 1, 2, None)
+        gather_scales(2, 4, "hcol0")
+        turn(1, 3, 0)
+        quantise(1, 2, 3, None)
+        front(0, 1, 4)
+        front(1, 2, 5)
+        first_back(2, 6, None)
+        first_layer(2, (0,))
+        first_layer(3, (1,))
+        turn(2, 2, 0)
+        turn(3, 2, 2 * P)
+        first_layer(4, (0,))
+        quantise(2, 4, 2, None)
+        first_back(3, 7, "hrow3")
+        turn(4, 3, 0)
+        first_layer(5, (1,))
+        turn(5, 3, 2 * P)
+        first_layer(6, (0,))
+        quantise(4, 6, 3, None)
+        front(2, 4, 1)
+        turn(6, 2, 0)
+        first_layer(7, (7,))
+        turn(7, 2, 2 * P)
+        quantise(6, 8, 2, None)
+        front(4, 6, 7)
+        back(1, 6, 4)
+        back(2, 5, 3)
+        front(6, 8, 4)
+        back(3, 4, 2)
+        for nb in (2, 3):
+            nc.vector.tensor_copy(win[nb][:].indirect(entries(2, CHUNKS)), y_back[:, nb - 2, :])
+        frozen_to_sbuf(0, (6, 5))
+        frozen_to_sbuf(1, (3, 0))
+        frozen_to_sbuf(2, (4, 2))
+        frozen(3, 1, 4)
+        frozen(3, 0, 2)
         base_tail = held([P, GPSIMD_COLS], F32, "base_tail")
-        nc.scalar.copy(base_tail[:], banks[5][:, BANK - GPSIMD_COLS : BANK])
-        finish_on_tensor(1, (3, 0), (7, 6))
-        finish_on_tensor(2, (7, 6), (3, 0))
-        finish_on_vector(3, (2, 5))
+        nc.scalar.copy(base_tail[:], banks[4][:, BANK - GPSIMD_COLS : BANK])
+        finish_on_gpsimd(0, "y_front")
+        finish_on_gpsimd(1, None)
+        finish_on_gpsimd(2, None)
+        finish_last(3, (2, 4))

@@ -20,7 +20,7 @@ ALU = mybir.AluOpType
 P = 128
 BANK = 512
 CHUNKS = E * C // P
-GPSIMD_COLS = T // 4
+GPSIMD_COLS = 320
 LIST_COLS = P // 16
 
 
@@ -30,7 +30,6 @@ def tile_moe_adp_silu_kernel(
     nc = tc.nc
     with ExitStack() as ctx:
         keep = ctx.enter_context(tc.tile_pool(name="keep", bufs=1))
-        ring = ctx.enter_context(tc.tile_pool(name="ring", bufs=2))
         psum = ctx.enter_context(tc.psum_pool(name="psum", bufs=1))
 
         def held(shape, dtype, name, tag=None):
@@ -68,20 +67,22 @@ def tile_moe_adp_silu_kernel(
                 xs[32 * q : 32 * q + 32, :].bitcast(I32),
                 four_rows.unsqueeze(0).broadcast_to([8, 4, T // 4]),
             )
-        for q in range(4):
-            load_adapter_plane(was, wa_scales, q, nc.scalar)
-        xw = load_words(x_words[0], "xw")
+        load_adapter_plane(was, wa_scales, 0, nc.scalar)
         wa0 = load_words(wa_words[0, 0], "wa0")
+        xw = load_words(x_words[0], "xw")
+        for q in range(1, 4):
+            load_adapter_plane(was, wa_scales, q, nc.sync)
         wb0 = load_words(wb_words[0, 0], "wb0")
         for q in range(4):
             load_adapter_plane(wbs, wb_scales, q, nc.sync)
         g0 = held([P, C], F32, "g0")
         nc.sync.dma_start(g0[:], gate[:, 0:C])
         wa1 = load_words(wa_words[1, 0], "wa1")
+        wb1 = load_words(wb_words[1, 0], "wb1")
         wa = [wa0[:], wa1[:]] + load_many(wa_words[2:E, 0], "wa_rest")
-        wb = [wb0[:]] + load_many(wb_words[1:E, 0], "wb_rest")
         g1 = held([P, (E - 1) * C], F32, "g1")
         nc.sync.dma_start(g1[:], gate[:, C : E * C])
+        wb = [wb0[:], wb1[:]] + load_many(wb_words[2:E, 0], "wb_rest")
         gcol = held([P, CHUNKS - 2], F32, "gcol")
         with nc.allow_non_contiguous_dma(reason="one gate value a slot, slots on the partitions"):
             nc.sync.dma_start(gcol[:], gate[0:1, C : E * C].rearrange("o (c p) -> p (o c)", p=P))
@@ -92,6 +93,15 @@ def tile_moe_adp_silu_kernel(
 
         ident = held([P, P], F32, "ident")
         make_identity(nc, ident[:])
+
+        wa0_dealt = held([P, H], I32, "wa0_dealt")
+        nc.gpsimd.tensor_copy(
+            wa0_dealt[:].rearrange("p (d m) -> p d m", d=4), wa0[:].rearrange("p (m d) -> p d m", d=4)
+        )
+        was_dealt = held([P, H], U8, "was_dealt")
+        nc.gpsimd.tensor_copy(
+            was_dealt[:].rearrange("p (d m) -> p d m", d=4), was[:].rearrange("p (m d) -> p d m", d=4)
+        )
 
         def entries(c0, c1):
             return offsets[:, c0 * LIST_COLS : c1 * LIST_COLS]
@@ -138,6 +148,20 @@ def tile_moe_adp_silu_kernel(
                     ACT.Silu,
                 )
 
+        def first_layer_direct(c, b):
+            cols = slice(c * P, (c + 1) * P)
+            for d in range(4):
+                part = slice(d * P, (d + 1) * P)
+                nc.tensor.matmul_mx(
+                    banks[b][:, part], lhsT=wa0_dealt[:, part].bitcast(FP8X4), lhsT_scale=was_dealt[:, part],
+                    rhs=xg[c].bitcast(FP8X4), rhs_scale=xsg[0][:, cols], start=True, stop=True,
+                )
+            hcol = held([P, 4 * P], BF16, "hcol%d" % c)
+            nc.scalar.activation(
+                hcol[:].rearrange("p (s d) -> p s d", d=4), banks[b][:].rearrange("p (d s) -> p s d", d=4), ACT.Silu
+            )
+            nc.vector.quantize_mx(hq[0][:, cols].bitcast(FP8X4), hs[0][:, cols], hcol[:])
+
         def turn(c, b, off):
             pairs = hrow[c][:].bitcast(F32)
             for u in range(2):
@@ -172,40 +196,41 @@ def tile_moe_adp_silu_kernel(
         def scatter_gated(nb, c0, c1, src):
             nc.vector.tensor_tensor(win[nb][:].indirect(entries(c0, c1)), src, gate_rows(c0, c1), ALU.mult)
 
-        def front(c0, c1, b):
+        def front_one(nb, c0, c1, b):
             cols = slice(c0 * P, c1 * P)
-            second_layer(c0, c1, [0, 1], b, y_front[:, :, cols])
-            for nb in range(2):
-                scatter_gated(nb, c0, c1, y_front[:, nb, cols])
+            second_layer(c0, c1, [nb], b, y_front[:, nb : nb + 1, cols])
+            scatter_gated(nb, c0, c1, y_front[:, nb, cols])
 
         def first_back(nb, b, buffer):
             y_first = held([P, 1, C], F32, "y_first%d" % nb, buffer)
             second_layer(0, 2, [nb], b, y_first[:])
             scatter_gated(nb, 0, 2, y_first[:, 0, :])
 
-        def back(e, b_slots, b_rows):
-            gated = ring.tile([P, 2, 2 * P], F32, tag="gated", name="gated", align_bytes=64)
+        gated = {}
+
+        def back_by_slots(e, b, buffer):
+            gated[e] = held([P, 2, 2 * P], F32, "gated%d" % e, buffer)
             cols = slice(2 * P, 4 * P)
             for half in range(2):
                 slots = slice(half * P, (half + 1) * P)
                 nc.tensor.matmul_mx(
-                    banks[b_slots][:, half * C : (half + 1) * C], lhsT=hq[e][:, slots].bitcast(FP8X4),
+                    banks[b][:, half * C : (half + 1) * C], lhsT=hq[e][:, slots].bitcast(FP8X4),
                     lhsT_scale=hs[e][:, slots], rhs=wb[e][:, cols].bitcast(FP8X4), rhs_scale=wbs[4 * e : P, cols],
                     start=True, stop=True,
                 )
             for half in range(2):
                 c = 2 * e + half
                 nc.scalar.activation(
-                    gated[:, half, :], banks[b_slots][:, half * C : (half + 1) * C], ACT.Copy,
+                    gated[e][:, half, :], banks[b][:, half * C : (half + 1) * C], ACT.Copy,
                     scale=gcol[:, c - 2 : c - 1],
                 )
+
+        def back_by_rows(e, b):
             for half in range(2):
                 for j in range(2):
                     col = j * C + half * P
-                    nc.tensor.transpose(banks[b_rows][:, col : col + P], gated[:, half, j * P : (j + 1) * P], ident[:])
-            nc.scalar.copy(
-                y_back[:, :, (e - 1) * C : e * C], banks[b_rows][:].rearrange("p (j s) -> p j s", s=C)
-            )
+                    nc.tensor.transpose(banks[b][:, col : col + P], gated[e][:, half, j * P : (j + 1) * P], ident[:])
+            nc.scalar.copy(y_back[:, :, (e - 1) * C : e * C], banks[b][:].rearrange("p (j s) -> p j s", s=C))
 
         def frozen(nb, th, b):
             cols = slice(th * BANK, (th + 1) * BANK)
@@ -239,22 +264,18 @@ def tile_moe_adp_silu_kernel(
             nc.gpsimd.tensor_tensor(res[:, cols], base_tail[:], win[nb][:, cols], ALU.add)
             nc.scalar.dma_start(out[nb * P : (nb + 1) * P, cols], res[:, cols])
 
-        gather_scales(0, 1, None)
+        gather_scales(0, 3, None)
         gather_words(0, 1)
         gather_words(1, 2)
         gather_words(2, 4)
         gather_words(4, CHUNKS)
 
-        first_layer(0, (0, 7))
-        gather_scales(1, 2, "xg0")
-        first_layer(1, (1,))
-        turn(0, 2, 0)
-        quantise(0, 1, 2, None)
-        gather_scales(2, 4, "hcol0")
-        turn(1, 3, 0)
-        quantise(1, 2, 3, None)
-        front(0, 1, 4)
-        front(1, 2, 5)
+        first_layer_direct(0, 0)
+        gather_scales(3, 4, "xg0")
+        first_layer_direct(1, 1)
+        front_one(0, 0, 1, 4)
+        front_one(1, 0, 2, 5)
+        front_one(0, 1, 2, 4)
         first_back(2, 6, None)
         first_layer(2, (0,))
         first_layer(3, (1,))
@@ -263,31 +284,38 @@ def tile_moe_adp_silu_kernel(
         first_layer(4, (0,))
         quantise(2, 4, 2, None)
         first_back(3, 7, "hrow3")
+        front_one(0, 2, 4, 5)
         turn(4, 3, 0)
         first_layer(5, (1,))
         turn(5, 3, 2 * P)
         first_layer(6, (0,))
         quantise(4, 6, 3, None)
-        front(2, 4, 1)
+        front_one(1, 2, 4, 1)
         turn(6, 2, 0)
         first_layer(7, (7,))
         turn(7, 2, 2 * P)
         quantise(6, 8, 2, None)
-        front(4, 6, 7)
-        back(1, 6, 4)
-        back(2, 5, 3)
-        front(6, 8, 4)
-        back(3, 4, 2)
+        second_layer(4, 6, [0, 1], 7, y_front[:, :, 2 * C : 3 * C])
+        scatter_gated(0, 4, 6, y_front[:, 0, 2 * C : 3 * C])
+        back_by_slots(1, 3, "hrow7")
+        back_by_slots(2, 2, None)
+        second_layer(6, 8, [0, 1], 1, y_front[:, :, 3 * C : 4 * C])
+        scatter_gated(1, 4, 8, y_front[:, 1, 2 * C : 4 * C])
+        scatter_gated(0, 6, 8, y_front[:, 0, 3 * C : 4 * C])
+        back_by_rows(1, 4)
+        back_by_rows(2, 5)
+        back_by_slots(3, 1, None)
+        back_by_rows(3, 6)
         for nb in (2, 3):
             nc.vector.tensor_copy(win[nb][:].indirect(entries(2, CHUNKS)), y_back[:, nb - 2, :])
-        frozen_to_sbuf(0, (6, 5))
-        frozen_to_sbuf(1, (3, 0))
-        frozen_to_sbuf(2, (4, 2))
+        frozen_to_sbuf(0, (4, 5))
+        frozen_to_sbuf(1, (1, 6))
+        frozen_to_sbuf(2, (4, 5))
         frozen(3, 1, 4)
-        frozen(3, 0, 2)
+        frozen(3, 0, 5)
         base_tail = held([P, GPSIMD_COLS], F32, "base_tail")
         nc.scalar.copy(base_tail[:], banks[4][:, BANK - GPSIMD_COLS : BANK])
         finish_on_gpsimd(0, "y_front")
         finish_on_gpsimd(1, None)
         finish_on_gpsimd(2, None)
-        finish_last(3, (2, 4))
+        finish_last(3, (5, 4))

@@ -73,11 +73,12 @@ def tile_moe_adp_silu_kernel(
         for q in range(1, 4):
             load_adapter_plane(was, wa_scales, q, nc.sync)
         wb0 = load_words(wb_words[0, 0], "wb0")
-        for q in range(4):
+        for q in range(3):
             load_adapter_plane(wbs, wb_scales, q, nc.sync)
+        wa1 = load_words(wa_words[1, 0], "wa1")
+        load_adapter_plane(wbs, wb_scales, 3, nc.sync)
         g0 = held([P, C], F32, "g0")
         nc.sync.dma_start(g0[:], gate[:, 0:C])
-        wa1 = load_words(wa_words[1, 0], "wa1")
         wb1 = load_words(wb_words[1, 0], "wb1")
         wa = [wa0[:], wa1[:]] + load_many(wa_words[2:E, 0], "wa_rest")
         g1 = held([P, (E - 1) * C], F32, "g1")
@@ -99,9 +100,11 @@ def tile_moe_adp_silu_kernel(
             wa0_dealt[:].rearrange("p (d m) -> p d m", d=4), wa0[:].rearrange("p (m d) -> p d m", d=4)
         )
         was_dealt = held([P, H], U8, "was_dealt")
-        nc.gpsimd.tensor_copy(
-            was_dealt[:].rearrange("p (d m) -> p d m", d=4), was[:].rearrange("p (m d) -> p d m", d=4)
-        )
+        for d0 in (0, 2):
+            nc.gpsimd.tensor_copy(
+                was_dealt[:].rearrange("p (d m) -> p d m", d=4)[:, d0 : d0 + 2, :],
+                was[:].rearrange("p (m d) -> p d m", d=4)[:, d0 : d0 + 2, :],
+            )
 
         def entries(c0, c1):
             return offsets[:, c0 * LIST_COLS : c1 * LIST_COLS]
@@ -273,49 +276,49 @@ def tile_moe_adp_silu_kernel(
         first_layer_direct(0, 0)
         gather_scales(3, 4, "xg0")
         first_layer_direct(1, 1)
+        first_layer(2, (2,))
         front_one(0, 0, 1, 4)
         front_one(1, 0, 2, 5)
-        front_one(0, 1, 2, 4)
+        front_one(0, 1, 2, 3)
+        first_layer(3, (4,))
         first_back(2, 6, None)
-        first_layer(2, (0,))
-        first_layer(3, (1,))
-        turn(2, 2, 0)
-        turn(3, 2, 2 * P)
-        first_layer(4, (0,))
-        quantise(2, 4, 2, None)
+        turn(2, 5, 0)
+        turn(3, 5, 2 * P)
+        first_layer(4, (2,))
+        quantise(2, 4, 5, None)
         first_back(3, 7, "hrow3")
-        front_one(0, 2, 4, 5)
+        front_one(0, 2, 4, 0)
         turn(4, 3, 0)
-        first_layer(5, (1,))
+        first_layer(5, (4,))
         turn(5, 3, 2 * P)
-        first_layer(6, (0,))
+        first_layer(6, (2,))
         quantise(4, 6, 3, None)
-        front_one(1, 2, 4, 1)
-        turn(6, 2, 0)
+        front_one(1, 2, 4, 4)
+        turn(6, 5, 0)
         first_layer(7, (7,))
-        turn(7, 2, 2 * P)
-        quantise(6, 8, 2, None)
+        turn(7, 5, 2 * P)
+        quantise(6, 8, 5, None)
         second_layer(4, 6, [0, 1], 7, y_front[:, :, 2 * C : 3 * C])
         scatter_gated(0, 4, 6, y_front[:, 0, 2 * C : 3 * C])
         back_by_slots(1, 3, "hrow7")
-        back_by_slots(2, 2, None)
+        back_by_slots(2, 5, None)
         second_layer(6, 8, [0, 1], 1, y_front[:, :, 3 * C : 4 * C])
         scatter_gated(1, 4, 8, y_front[:, 1, 2 * C : 4 * C])
         scatter_gated(0, 6, 8, y_front[:, 0, 3 * C : 4 * C])
-        back_by_rows(1, 4)
-        back_by_rows(2, 5)
+        back_by_rows(1, 0)
+        back_by_rows(2, 2)
         back_by_slots(3, 1, None)
         back_by_rows(3, 6)
         for nb in (2, 3):
             nc.vector.tensor_copy(win[nb][:].indirect(entries(2, CHUNKS)), y_back[:, nb - 2, :])
-        frozen_to_sbuf(0, (4, 5))
+        frozen_to_sbuf(0, (0, 2))
         frozen_to_sbuf(1, (1, 6))
-        frozen_to_sbuf(2, (4, 5))
-        frozen(3, 1, 4)
-        frozen(3, 0, 5)
+        frozen_to_sbuf(2, (0, 2))
+        frozen(3, 1, 0)
+        frozen(3, 0, 2)
         base_tail = held([P, GPSIMD_COLS], F32, "base_tail")
-        nc.scalar.copy(base_tail[:], banks[4][:, BANK - GPSIMD_COLS : BANK])
+        nc.scalar.copy(base_tail[:], banks[0][:, BANK - GPSIMD_COLS : BANK])
         finish_on_gpsimd(0, "y_front")
         finish_on_gpsimd(1, None)
         finish_on_gpsimd(2, None)
-        finish_last(3, (5, 4))
+        finish_last(3, (2, 0))

@@ -254,8 +254,29 @@ def tile_moe_adp_silu_kernel(
             nc.gpsimd.tensor_tensor(res[:], base[nb][:], win[nb][:], ALU.add)
             nc.sync.dma_start(out[nb * P : (nb + 1) * P, :], res[:])
 
+        def finish_on_tensor(nb, sum_banks, back_banks):
+            summed = [banks[b][:].rearrange("p (j n) -> p j n", j=4) for b in sum_banks]
+            for th in range(2):
+                for j in range(4):
+                    t0 = th * BANK + j * P
+                    nc.tensor.matmul(summed[th][:, j, :], base[nb][:, t0 : t0 + P], ident[:],
+                                     start=j == 0, stop=False, is_transpose=True)
+            for th in range(2):
+                for j in range(4):
+                    t0 = th * BANK + j * P
+                    nc.tensor.matmul(summed[th][:, j, :], win[nb][:, t0 : t0 + P], ident[:],
+                                     start=False, stop=j == 3, is_transpose=True)
+                flipped = held([P, 4, P], F32, "flipped%d" % th)
+                nc.scalar.copy(flipped[:], summed[th])
+                back = banks[back_banks[th]][:].rearrange("p (j t) -> p j t", j=4)
+                for j in range(4):
+                    nc.tensor.transpose(back[:, j, :], flipped[:, j, :], ident[:])
+                res = held([P, BANK], F32, "res%d_%d" % (nb, th))
+                nc.scalar.copy(res[:], banks[back_banks[th]][:])
+                nc.scalar.dma_start(out[nb * P : (nb + 1) * P, th * BANK : (th + 1) * BANK], res[:])
+
         def finish_last(nb, base_banks):
-            res = held([P, T], F32, "last")
+            res = held([P, T - GPSIMD_COLS], F32, "last", "res0_0")
             for col, end in ((0, P), (P, BANK), (BANK, T - GPSIMD_COLS)):
                 th, off = divmod(col, BANK)
                 cols = slice(col, end)
@@ -264,8 +285,9 @@ def tile_moe_adp_silu_kernel(
                 )
                 nc.scalar.dma_start(out[nb * P : (nb + 1) * P, cols], res[:, cols])
             cols = slice(T - GPSIMD_COLS, T)
-            nc.gpsimd.tensor_tensor(res[:, cols], base_tail[:], win[nb][:, cols], ALU.add)
-            nc.scalar.dma_start(out[nb * P : (nb + 1) * P, cols], res[:, cols])
+            tail = held([P, GPSIMD_COLS], F32, "tail", "res0_1")
+            nc.gpsimd.tensor_tensor(tail[:], base_tail[:], win[nb][:, cols], ALU.add)
+            nc.scalar.dma_start(out[nb * P : (nb + 1) * P, cols], tail[:])
 
         gather_scales(0, 3, None)
         gather_words(0, 1)
@@ -314,11 +336,11 @@ def tile_moe_adp_silu_kernel(
         frozen_to_sbuf(0, (0, 2))
         frozen_to_sbuf(1, (1, 6))
         frozen_to_sbuf(2, (0, 2))
-        frozen(3, 1, 0)
-        frozen(3, 0, 2)
-        base_tail = held([P, GPSIMD_COLS], F32, "base_tail")
-        nc.scalar.copy(base_tail[:], banks[0][:, BANK - GPSIMD_COLS : BANK])
-        finish_on_gpsimd(0, "y_front")
-        finish_on_gpsimd(1, None)
+        frozen(3, 1, 1)
+        finish_on_tensor(0, (0, 2), (3, 4))
+        frozen(3, 0, 3)
+        base_tail = held([P, GPSIMD_COLS], F32, "base_tail", "flipped0")
+        nc.scalar.copy(base_tail[:], banks[1][:, BANK - GPSIMD_COLS : BANK])
+        finish_on_gpsimd(1, "y_front")
         finish_on_gpsimd(2, None)
-        finish_last(3, (2, 0))
+        finish_last(3, (3, 1))

@@ -266,7 +266,7 @@ def tile_moe_adp_silu_kernel(
                     t0 = th * BANK + j * P
                     nc.tensor.matmul(summed[th][:, j, :], win[nb][:, t0 : t0 + P], ident[:],
                                      start=False, stop=j == 3, is_transpose=True)
-                flipped = held([P, 4, P], F32, "flipped%d" % th)
+                flipped = held([P, 4, P], F32, "flipped%d_%d" % (nb, th))
                 nc.scalar.copy(flipped[:], summed[th])
                 back = banks[back_banks[th]][:].rearrange("p (j t) -> p j t", j=4)
                 for j in range(4):
@@ -333,14 +333,14 @@ def tile_moe_adp_silu_kernel(
         back_by_rows(3, 6)
         for nb in (2, 3):
             nc.vector.tensor_copy(win[nb][:].indirect(entries(2, CHUNKS)), y_back[:, nb - 2, :])
-        frozen_to_sbuf(0, (0, 2))
-        frozen_to_sbuf(1, (1, 6))
+        frozen_to_sbuf(1, (0, 2))
+        frozen_to_sbuf(0, (1, 6))
         frozen_to_sbuf(2, (0, 2))
         frozen(3, 1, 1)
-        finish_on_tensor(0, (0, 2), (3, 4))
-        frozen(3, 0, 3)
-        base_tail = held([P, GPSIMD_COLS], F32, "base_tail", "flipped0")
+        frozen(3, 0, 6)
+        base_tail = held([P, GPSIMD_COLS], F32, "base_tail")
         nc.scalar.copy(base_tail[:], banks[1][:, BANK - GPSIMD_COLS : BANK])
-        finish_on_gpsimd(1, "y_front")
+        finish_on_tensor(1, (3, 5), (0, 2))
+        finish_on_tensor(0, (4, 7), (3, 5))
         finish_on_gpsimd(2, None)
-        finish_last(3, (3, 1))
+        finish_last(3, (6, 1))

@@ -276,7 +276,7 @@ def tile_moe_adp_silu_kernel(
                 nc.scalar.dma_start(out[nb * P : (nb + 1) * P, th * BANK : (th + 1) * BANK], res[:])
 
         def finish_last(nb, base_banks):
-            res = held([P, T - GPSIMD_COLS], F32, "last", "res0_0")
+            res = held([P, T - GPSIMD_COLS], F32, "last")
             for col, end in ((0, P), (P, BANK), (BANK, T - GPSIMD_COLS)):
                 th, off = divmod(col, BANK)
                 cols = slice(col, end)
@@ -285,7 +285,7 @@ def tile_moe_adp_silu_kernel(
                 )
                 nc.scalar.dma_start(out[nb * P : (nb + 1) * P, cols], res[:, cols])
             cols = slice(T - GPSIMD_COLS, T)
-            tail = held([P, GPSIMD_COLS], F32, "tail", "res0_1")
+            tail = held([P, GPSIMD_COLS], F32, "tail")
             nc.gpsimd.tensor_tensor(tail[:], base_tail[:], win[nb][:, cols], ALU.add)
             nc.scalar.dma_start(out[nb * P : (nb + 1) * P, cols], tail[:])
 
@@ -335,12 +335,12 @@ def tile_moe_adp_silu_kernel(
             nc.vector.tensor_copy(win[nb][:].indirect(entries(2, CHUNKS)), y_back[:, nb - 2, :])
         frozen_to_sbuf(1, (0, 2))
         frozen_to_sbuf(0, (1, 6))
+        finish_on_tensor(1, (3, 5), (1, 6))
         frozen_to_sbuf(2, (0, 2))
-        frozen(3, 1, 1)
-        frozen(3, 0, 6)
-        base_tail = held([P, GPSIMD_COLS], F32, "base_tail")
-        nc.scalar.copy(base_tail[:], banks[1][:, BANK - GPSIMD_COLS : BANK])
-        finish_on_tensor(1, (3, 5), (0, 2))
         finish_on_tensor(0, (4, 7), (3, 5))
+        frozen(3, 1, 3)
+        frozen(3, 0, 5)
+        base_tail = held([P, GPSIMD_COLS], F32, "base_tail")
+        nc.scalar.copy(base_tail[:], banks[3][:, BANK - GPSIMD_COLS : BANK])
         finish_on_gpsimd(2, None)
-        finish_last(3, (6, 1))
+        finish_last(3, (5, 3))

@@ -20,7 +20,7 @@ ALU = mybir.AluOpType
 P = 128
 BANK = 512
 CHUNKS = E * C // P
-GPSIMD_COLS = 320
+GPSIMD_COLS = 384
 LIST_COLS = P // 16
 
 
@@ -116,9 +116,10 @@ def tile_moe_adp_silu_kernel(
         xg, xsg, base = {}, {}, {}
         hq = [held([P, C], U32, "hq%d" % e) for e in range(E)]
         hs = [held([P, C], U8, "hs%d" % e) for e in range(E)]
-        win = [held([P, T], F32, "win%d" % nb) for nb in range(4)]
+        win = [held([P, 2 * T if nb == 2 else T], F32, "win%d" % nb) for nb in range(4)]
         y_front = held([P, 2, E * C], F32, "y_front")
-        y_back = held([P, 2, (E - 1) * C], F32, "y_back")
+        y_third = held([P, (E - 1) * C], F32, "y_third")
+        y_last = held([P, (E - 1) * C], F32, "y_last")
 
         def gather_scales(e0, e1, buffer):
             tile = held([P, (e1 - e0) * C], U8, "xsg%d" % e0, buffer)
@@ -209,31 +210,39 @@ def tile_moe_adp_silu_kernel(
             second_layer(0, 2, [nb], b, y_first[:])
             scatter_gated(nb, 0, 2, y_first[:, 0, :])
 
+        def third(e0, e1, b):
+            rows = slice(2 * P, 3 * P)
+            for e in range(e0, e1):
+                nc.tensor.matmul_mx(
+                    banks[b][:, (e - e0) * C : (e - e0 + 1) * C], lhsT=wb[e][:, rows].bitcast(FP8X4),
+                    lhsT_scale=wbs[4 * e : P, rows], rhs=hq[e][:].bitcast(FP8X4), rhs_scale=hs[e][:],
+                    start=True, stop=True,
+                )
+            nc.scalar.copy(y_third[:, (e0 - 1) * C : (e1 - 1) * C], banks[b][:, 0 : (e1 - e0) * C])
+
         gated = {}
 
-        def back_by_slots(e, b, buffer):
-            gated[e] = held([P, 2, 2 * P], F32, "gated%d" % e, buffer)
-            cols = slice(2 * P, 4 * P)
-            for half in range(2):
+        def last_by_slots(c0, c1, b, buffer):
+            gated[c0] = held([P, c1 - c0, P], F32, "gated%d" % c0, buffer)
+            cols = slice(3 * P, 4 * P)
+            for c in range(c0, c1):
+                e, half = divmod(c, 2)
                 slots = slice(half * P, (half + 1) * P)
                 nc.tensor.matmul_mx(
-                    banks[b][:, half * C : (half + 1) * C], lhsT=hq[e][:, slots].bitcast(FP8X4),
+                    banks[b][:, (c - c0) * P : (c - c0 + 1) * P], lhsT=hq[e][:, slots].bitcast(FP8X4),
                     lhsT_scale=hs[e][:, slots], rhs=wb[e][:, cols].bitcast(FP8X4), rhs_scale=wbs[4 * e : P, cols],
                     start=True, stop=True,
                 )
-            for half in range(2):
-                c = 2 * e + half
+            for c in range(c0, c1):
                 nc.scalar.activation(
-                    gated[e][:, half, :], banks[b][:, half * C : (half + 1) * C], ACT.Copy,
+                    gated[c0][:, c - c0, :], banks[b][:, (c - c0) * P : (c - c0 + 1) * P], ACT.Copy,
                     scale=gcol[:, c - 2 : c - 1],
                 )
 
-        def back_by_rows(e, b):
-            for half in range(2):
-                for j in range(2):
-                    col = j * C + half * P
-                    nc.tensor.transpose(banks[b][:, col : col + P], gated[e][:, half, j * P : (j + 1) * P], ident[:])
-            nc.scalar.copy(y_back[:, :, (e - 1) * C : e * C], banks[b][:].rearrange("p (j s) -> p j s", s=C))
+        def last_by_rows(c0, c1, b):
+            for j in range(c1 - c0):
+                nc.tensor.transpose(banks[b][:, j * P : (j + 1) * P], gated[c0][:, j, :], ident[:])
+            nc.scalar.copy(y_last[:, (c0 - 2) * P : (c1 - 2) * P], banks[b][:, 0 : (c1 - c0) * P])
 
         def frozen(nb, th, b):
             cols = slice(th * BANK, (th + 1) * BANK)
@@ -251,7 +260,7 @@ def tile_moe_adp_silu_kernel(
 
         def finish_on_gpsimd(nb, buffer):
             res = held([P, T], F32, "res%d" % nb, buffer)
-            nc.gpsimd.tensor_tensor(res[:], base[nb][:], win[nb][:], ALU.add)
+            nc.gpsimd.tensor_tensor(res[:], base[nb][:], win[nb][:, 0:T], ALU.add)
             nc.sync.dma_start(out[nb * P : (nb + 1) * P, :], res[:])
 
         def finish_on_tensor(nb, sum_banks, back_banks):
@@ -277,7 +286,7 @@ def tile_moe_adp_silu_kernel(
 
         def finish_last(nb, base_banks):
             res = held([P, T - GPSIMD_COLS], F32, "last")
-            for col, end in ((0, P), (P, BANK), (BANK, T - GPSIMD_COLS)):
+            for col, end in ((0, 192), (192, BANK), (BANK, T - GPSIMD_COLS)):
                 th, off = divmod(col, BANK)
                 cols = slice(col, end)
                 nc.vector.tensor_tensor(
@@ -322,25 +331,25 @@ def tile_moe_adp_silu_kernel(
         quantise(6, 8, 5, None)
         second_layer(4, 6, [0, 1], 7, y_front[:, :, 2 * C : 3 * C])
         scatter_gated(0, 4, 6, y_front[:, 0, 2 * C : 3 * C])
-        back_by_slots(1, 3, "hrow7")
-        back_by_slots(2, 5, None)
+        third(1, 3, 5)
         second_layer(6, 8, [0, 1], 1, y_front[:, :, 3 * C : 4 * C])
         scatter_gated(1, 4, 8, y_front[:, 1, 2 * C : 4 * C])
         scatter_gated(0, 6, 8, y_front[:, 0, 3 * C : 4 * C])
-        back_by_rows(1, 0)
-        back_by_rows(2, 2)
-        back_by_slots(3, 1, None)
-        back_by_rows(3, 6)
-        for nb in (2, 3):
-            nc.vector.tensor_copy(win[nb][:].indirect(entries(2, CHUNKS)), y_back[:, nb - 2, :])
-        frozen_to_sbuf(1, (0, 2))
-        frozen_to_sbuf(0, (1, 6))
-        finish_on_tensor(1, (3, 5), (1, 6))
-        frozen_to_sbuf(2, (0, 2))
-        finish_on_tensor(0, (4, 7), (3, 5))
-        frozen(3, 1, 3)
-        frozen(3, 0, 5)
+        third(3, 4, 7)
+        scatter_gated(2, 2, CHUNKS, y_third[:])
+        frozen_to_sbuf(1, (5, 7))
+        last_by_slots(2, 6, 1, None)
+        last_by_slots(6, 8, 6, None)
+        frozen_to_sbuf(0, (5, 7))
+        last_by_rows(2, 6, 1)
+        last_by_rows(6, 8, 6)
+        nc.vector.tensor_copy(win[3][:].indirect(entries(2, CHUNKS)), y_last[:])
+        finish_on_tensor(1, (0, 2), (5, 7))
+        frozen_to_sbuf(2, (1, 6))
+        finish_on_tensor(0, (3, 4), (0, 2))
+        frozen(3, 1, 0)
+        frozen(3, 0, 2)
         base_tail = held([P, GPSIMD_COLS], F32, "base_tail")
-        nc.scalar.copy(base_tail[:], banks[3][:, BANK - GPSIMD_COLS : BANK])
+        nc.scalar.copy(base_tail[:], banks[0][:, BANK - GPSIMD_COLS : BANK])
         finish_on_gpsimd(2, None)
-        finish_last(3, (5, 3))
+        finish_last(3, (2, 0))

@@ -309,8 +309,10 @@ def tile_moe_adp_silu_kernel(
         first_layer_direct(1, 1)
         first_layer(2, (2,))
         front_one(0, 0, 1, 4)
-        front_one(1, 0, 2, 5)
-        front_one(0, 1, 2, 3)
+        front_one(1, 0, 1, 5)
+        second_layer(1, 2, [0, 1], 3, y_front[:, :, P : 2 * P])
+        for nb in range(2):
+            scatter_gated(nb, 1, 2, y_front[:, nb, P : 2 * P])
         first_layer(3, (4,))
         first_back(2, 6, None)
         turn(2, 5, 0)
@@ -329,13 +331,13 @@ def tile_moe_adp_silu_kernel(
         first_layer(7, (7,))
         turn(7, 5, 2 * P)
         quantise(6, 8, 5, None)
-        second_layer(4, 6, [0, 1], 7, y_front[:, :, 2 * C : 3 * C])
-        scatter_gated(0, 4, 6, y_front[:, 0, 2 * C : 3 * C])
-        third(1, 3, 5)
-        second_layer(6, 8, [0, 1], 1, y_front[:, :, 3 * C : 4 * C])
+        front_one(0, 4, 6, 7)
+        second_layer(4, 6, [1], 5, y_front[:, 1:2, 2 * C : 3 * C])
+        third(1, 3, 7)
+        second_layer(6, 8, [1], 3, y_front[:, 1:2, 3 * C : 4 * C])
         scatter_gated(1, 4, 8, y_front[:, 1, 2 * C : 4 * C])
-        scatter_gated(0, 6, 8, y_front[:, 0, 3 * C : 4 * C])
-        third(3, 4, 7)
+        front_one(0, 6, 8, 1)
+        third(3, 4, 5)
         scatter_gated(2, 2, CHUNKS, y_third[:])
         frozen_to_sbuf(1, (5, 7))
         last_by_slots(2, 6, 1, None)

@@ -305,14 +305,13 @@ def tile_moe_adp_silu_kernel(
         gather_words(4, CHUNKS)
 
         first_layer_direct(0, 0)
-        gather_scales(3, 4, "xg0")
+        gather_scales(3, 4, "hcol0")
         first_layer_direct(1, 1)
         first_layer(2, (2,))
         front_one(0, 0, 1, 4)
         front_one(1, 0, 1, 5)
-        second_layer(1, 2, [0, 1], 3, y_front[:, :, P : 2 * P])
-        for nb in range(2):
-            scatter_gated(nb, 1, 2, y_front[:, nb, P : 2 * P])
+        front_one(0, 1, 2, 3)
+        front_one(1, 1, 2, 1)
         first_layer(3, (4,))
         first_back(2, 6, None)
         turn(2, 5, 0)
@@ -332,23 +331,22 @@ def tile_moe_adp_silu_kernel(
         turn(7, 5, 2 * P)
         quantise(6, 8, 5, None)
         front_one(0, 4, 6, 7)
-        second_layer(4, 6, [1], 5, y_front[:, 1:2, 2 * C : 3 * C])
+        front_one(1, 4, 6, 5)
         third(1, 3, 7)
-        second_layer(6, 8, [1], 3, y_front[:, 1:2, 3 * C : 4 * C])
-        scatter_gated(1, 4, 8, y_front[:, 1, 2 * C : 4 * C])
-        front_one(0, 6, 8, 1)
+        front_one(0, 6, 8, 3)
+        front_one(1, 6, 8, 1)
         third(3, 4, 5)
         scatter_gated(2, 2, CHUNKS, y_third[:])
-        frozen_to_sbuf(1, (5, 7))
+        frozen_to_sbuf(0, (5, 7))
         last_by_slots(2, 6, 1, None)
         last_by_slots(6, 8, 6, None)
-        frozen_to_sbuf(0, (5, 7))
+        frozen_to_sbuf(1, (5, 7))
         last_by_rows(2, 6, 1)
         last_by_rows(6, 8, 6)
         nc.vector.tensor_copy(win[3][:].indirect(entries(2, CHUNKS)), y_last[:])
-        finish_on_tensor(1, (0, 2), (5, 7))
+        finish_on_tensor(0, (0, 2), (5, 7))
         frozen_to_sbuf(2, (1, 6))
-        finish_on_tensor(0, (3, 4), (0, 2))
+        finish_on_tensor(1, (3, 4), (0, 2))
         frozen(3, 1, 0)
         frozen(3, 0, 2)
         base_tail = held([P, GPSIMD_COLS], F32, "base_tail")

@@ -1,7 +1,6 @@
 from contextlib import ExitStack
 
 import concourse.mybir as mybir
-from concourse.masks import make_identity
 
 K, T, E, C, H, N = 512, 1024, 4, 256, 512, 512
 FLOPS = 2 * K * N * T + 2 * K * H * E * C + 2 * H * N * E * C
@@ -20,7 +19,6 @@ ALU = mybir.AluOpType
 P = 128
 BANK = 512
 CHUNKS = E * C // P
-GPSIMD_COLS = 384
 LIST_COLS = P // 16
 
 
@@ -72,231 +70,133 @@ def tile_moe_adp_silu_kernel(
         xw = load_words(x_words[0], "xw")
         for q in range(1, 4):
             load_adapter_plane(was, wa_scales, q, nc.sync)
-        wb0 = load_words(wb_words[0, 0], "wb0")
-        for q in range(3):
-            load_adapter_plane(wbs, wb_scales, q, nc.sync)
         wa1 = load_words(wa_words[1, 0], "wa1")
-        load_adapter_plane(wbs, wb_scales, 3, nc.sync)
+        for q in range(4):
+            load_adapter_plane(wbs, wb_scales, q, nc.sync)
+        wb0 = load_words(wb_words[0, 0], "wb0")
         g0 = held([P, C], F32, "g0")
         nc.sync.dma_start(g0[:], gate[:, 0:C])
-        wb1 = load_words(wb_words[1, 0], "wb1")
         wa = [wa0[:], wa1[:]] + load_many(wa_words[2:E, 0], "wa_rest")
         g1 = held([P, (E - 1) * C], F32, "g1")
         nc.sync.dma_start(g1[:], gate[:, C : E * C])
-        wb = [wb0[:], wb1[:]] + load_many(wb_words[2:E, 0], "wb_rest")
-        gcol = held([P, CHUNKS - 2], F32, "gcol")
-        with nc.allow_non_contiguous_dma(reason="one gate value a slot, slots on the partitions"):
-            nc.sync.dma_start(gcol[:], gate[0:1, C : E * C].rearrange("o (c p) -> p (o c)", p=P))
+        wb1 = load_words(wb_words[1, 0], "wb1")
         ww = held([P, 2 * N], U8, "ww")
         nc.sync.dma_start(ww[:].bitcast(I32), w_words[0].bitcast(I32))
         for r in range(4):
             nc.sync.dma_start(ws[r:P:32, :].bitcast(I32), w_scales[0, r:16:4, :].bitcast(I32))
+        wb = [wb0[:], wb1[:]] + load_many(wb_words[2:E, 0], "wb_rest")
 
-        ident = held([P, P], F32, "ident")
-        make_identity(nc, ident[:])
-
-        wa0_dealt = held([P, H], I32, "wa0_dealt")
-        nc.gpsimd.tensor_copy(
-            wa0_dealt[:].rearrange("p (d m) -> p d m", d=4), wa0[:].rearrange("p (m d) -> p d m", d=4)
-        )
+        wa_dealt = [held([P, H], I32, "wa_dealt%d" % e) for e in range(E)]
         was_dealt = held([P, H], U8, "was_dealt")
+
+        def deal_words(e):
+            nc.gpsimd.tensor_copy(
+                wa_dealt[e][:].rearrange("p (d m) -> p d m", d=4), wa[e].rearrange("p (m d) -> p d m", d=4)
+            )
+
+        deal_words(0)
         for d0 in (0, 2):
             nc.gpsimd.tensor_copy(
                 was_dealt[:].rearrange("p (d m) -> p d m", d=4)[:, d0 : d0 + 2, :],
                 was[:].rearrange("p (m d) -> p d m", d=4)[:, d0 : d0 + 2, :],
             )
+        for e in range(1, E):
+            deal_words(e)
 
-        def entries(c0, c1):
-            return offsets[:, c0 * LIST_COLS : c1 * LIST_COLS]
-
-        def gate_rows(c0, c1):
-            return g0[:, c0 * P : c1 * P] if c1 <= 2 else g1[:, (c0 - 2) * P : (c1 - 2) * P]
+        def entries(e0, e1):
+            return offsets[:, e0 * C // 16 : e1 * C // 16]
 
         banks = [psum.tile([P, BANK], F32, name="bank%d" % b) for b in range(8)]
-        xg, xsg, base = {}, {}, {}
-        hq = [held([P, C], U32, "hq%d" % e) for e in range(E)]
+        xg, xsg = {}, {}
+        hq = {}
         hs = [held([P, C], U8, "hs%d" % e) for e in range(E)]
-        win = [held([P, 2 * T if nb == 2 else T], F32, "win%d" % nb) for nb in range(4)]
-        y_front = held([P, 2, E * C], F32, "y_front")
-        y_third = held([P, (E - 1) * C], F32, "y_third")
-        y_last = held([P, (E - 1) * C], F32, "y_last")
+        win = [held([P, T], F32, "win%d" % nb) for nb in range(4)]
+        gated = held([P, 4, E * C], F32, "gated")
+        hcol = {}
 
         def gather_scales(e0, e1, buffer):
             tile = held([P, (e1 - e0) * C], U8, "xsg%d" % e0, buffer)
-            nc.vector.tensor_copy(tile[:], xs[:].indirect(entries(2 * e0, 2 * e1)))
+            nc.vector.tensor_copy(tile[:], xs[:].indirect(entries(e0, e1)))
             for e in range(e0, e1):
                 xsg[e] = tile[:, (e - e0) * C : (e - e0 + 1) * C]
 
         def gather_words(c0, c1):
             tile = held([P, (c1 - c0) * P], U32, "xg%d" % c0)
-            nc.vector.tensor_copy(tile[:], xw[:].bitcast(U32).indirect(entries(c0, c1)))
+            nc.vector.tensor_copy(
+                tile[:], xw[:].bitcast(U32).indirect(offsets[:, c0 * LIST_COLS : c1 * LIST_COLS])
+            )
             for c in range(c0, c1):
                 xg[c] = tile[:, (c - c0) * P : (c - c0 + 1) * P]
 
-        hrow = {}
-
-        def first_layer(c, pre):
+        def first_layer(c, b):
             e, half = divmod(c, 2)
-            hrow[c] = held([P, H], BF16, "hrow%d" % c)
-            width = H // len(pre)
-            for part, b in enumerate(pre):
-                cols = slice(part * width, (part + 1) * width)
-                nc.tensor.matmul_mx(
-                    banks[b][:, 0:width], lhsT=xg[c].bitcast(FP8X4), lhsT_scale=xsg[e][:, half * P : (half + 1) * P],
-                    rhs=wa[e][:, cols].bitcast(FP8X4), rhs_scale=was[4 * e : P, cols], start=True, stop=True,
-                )
-                p0, p1 = cols.start // 4, cols.stop // 4
-                nc.scalar.activation(
-                    hrow[c][:].rearrange("s (u p b) -> s u p b", u=2, b=2)[:, :, p0:p1, :],
-                    banks[b][:, 0:width].rearrange("s (p u b) -> s u p b", u=2, b=2),
-                    ACT.Silu,
-                )
-
-        def first_layer_direct(c, b):
-            cols = slice(c * P, (c + 1) * P)
+            if half == 0:
+                hcol[e] = held([P, 4 * C], BF16, "hcol%d" % e)
             for d in range(4):
                 part = slice(d * P, (d + 1) * P)
                 nc.tensor.matmul_mx(
-                    banks[b][:, part], lhsT=wa0_dealt[:, part].bitcast(FP8X4), lhsT_scale=was_dealt[:, part],
-                    rhs=xg[c].bitcast(FP8X4), rhs_scale=xsg[0][:, cols], start=True, stop=True,
+                    banks[b][:, part], lhsT=wa_dealt[e][:, part].bitcast(FP8X4), lhsT_scale=was_dealt[4 * e : P, part],
+                    rhs=xg[c].bitcast(FP8X4), rhs_scale=xsg[e][:, half * P : (half + 1) * P], start=True, stop=True,
                 )
-            hcol = held([P, 4 * P], BF16, "hcol%d" % c)
             nc.scalar.activation(
-                hcol[:].rearrange("p (s d) -> p s d", d=4), banks[b][:].rearrange("p (d s) -> p s d", d=4), ACT.Silu
+                hcol[e][:, half * BANK : (half + 1) * BANK].rearrange("p (s d) -> p s d", d=4),
+                banks[b][:].rearrange("p (d s) -> p s d", d=4),
+                ACT.Silu,
             )
-            nc.vector.quantize_mx(hq[0][:, cols].bitcast(FP8X4), hs[0][:, cols], hcol[:])
 
-        def turn(c, b, off):
-            pairs = hrow[c][:].bitcast(F32)
-            for u in range(2):
-                nc.tensor.transpose(
-                    banks[b][:, off + u * P : off + (u + 1) * P], pairs[:, u * P : (u + 1) * P], ident[:]
-                )
+        def quantise(e, buffer):
+            hq[e] = held([P, C], U32, "hq%d" % e, buffer)
+            nc.vector.quantize_mx(hq[e][:].bitcast(FP8X4), hs[e][:], hcol[e][:])
 
-        def quantise(c0, c1, b, buffer):
-            n = c1 - c0
-            e, half = divmod(c0, 2)
-            cols = slice(half * P, (half + n) * P)
-            hcol = held([P, 4 * n * P], BF16, "hcol%d" % c0, buffer)
-            nc.scalar.copy(
-                hcol[:].bitcast(F32).rearrange("p (c s u) -> p c s u", c=n, u=2),
-                banks[b][:, 0 : 2 * n * P].rearrange("p (c u s) -> p c s u", c=n, u=2),
-            )
-            nc.vector.quantize_mx(hq[e][:, cols].bitcast(FP8X4), hs[e][:, cols], hcol[:])
+        def quantise_chunk(c):
+            cols = slice(c * P, (c + 1) * P)
+            nc.vector.quantize_mx(hq[0][:, cols].bitcast(FP8X4), hs[0][:, cols], hcol[0][:, c * BANK : (c + 1) * BANK])
 
-        def second_layer(c0, c1, blocks, b, dst):
-            e, half = divmod(c0, 2)
-            width = (c1 - c0) * P
-            cols = slice(half * P, half * P + width)
-            for j, nb in enumerate(blocks):
+        def second_layer(e, s0, s1, nb0, nb1, b, g):
+            width = s1 - s0
+            for nb in range(nb0, nb1):
                 rows = slice(nb * P, (nb + 1) * P)
                 nc.tensor.matmul_mx(
-                    banks[b][:, j * width : (j + 1) * width], lhsT=wb[e][:, rows].bitcast(FP8X4),
-                    lhsT_scale=wbs[4 * e : P, rows], rhs=hq[e][:, cols].bitcast(FP8X4), rhs_scale=hs[e][:, cols],
+                    banks[b][:, (nb - nb0) * width : (nb - nb0 + 1) * width], lhsT=wb[e][:, rows].bitcast(FP8X4),
+                    lhsT_scale=wbs[4 * e : P, rows], rhs=hq[e][:, s0:s1].bitcast(FP8X4), rhs_scale=hs[e][:, s0:s1],
                     start=True, stop=True,
                 )
-            nc.scalar.copy(dst, banks[b][:, 0 : len(blocks) * width].rearrange("p (j s) -> p j s", s=width))
-
-        def scatter_gated(nb, c0, c1, src):
-            nc.vector.tensor_tensor(win[nb][:].indirect(entries(c0, c1)), src, gate_rows(c0, c1), ALU.mult)
-
-        def front_one(nb, c0, c1, b):
-            cols = slice(c0 * P, c1 * P)
-            second_layer(c0, c1, [nb], b, y_front[:, nb : nb + 1, cols])
-            scatter_gated(nb, c0, c1, y_front[:, nb, cols])
-
-        def first_back(nb, b, buffer):
-            y_first = held([P, 1, C], F32, "y_first%d" % nb, buffer)
-            second_layer(0, 2, [nb], b, y_first[:])
-            scatter_gated(nb, 0, 2, y_first[:, 0, :])
-
-        def third(e0, e1, b):
-            rows = slice(2 * P, 3 * P)
-            for e in range(e0, e1):
-                nc.tensor.matmul_mx(
-                    banks[b][:, (e - e0) * C : (e - e0 + 1) * C], lhsT=wb[e][:, rows].bitcast(FP8X4),
-                    lhsT_scale=wbs[4 * e : P, rows], rhs=hq[e][:].bitcast(FP8X4), rhs_scale=hs[e][:],
-                    start=True, stop=True,
-                )
-            nc.scalar.copy(y_third[:, (e0 - 1) * C : (e1 - 1) * C], banks[b][:, 0 : (e1 - e0) * C])
-
-        gated = {}
-
-        def last_by_slots(c0, c1, b, buffer):
-            gated[c0] = held([P, c1 - c0, P], F32, "gated%d" % c0, buffer)
-            cols = slice(3 * P, 4 * P)
-            for c in range(c0, c1):
-                e, half = divmod(c, 2)
-                slots = slice(half * P, (half + 1) * P)
-                nc.tensor.matmul_mx(
-                    banks[b][:, (c - c0) * P : (c - c0 + 1) * P], lhsT=hq[e][:, slots].bitcast(FP8X4),
-                    lhsT_scale=hs[e][:, slots], rhs=wb[e][:, cols].bitcast(FP8X4), rhs_scale=wbs[4 * e : P, cols],
-                    start=True, stop=True,
-                )
-            for c in range(c0, c1):
-                nc.scalar.activation(
-                    gated[c0][:, c - c0, :], banks[b][:, (c - c0) * P : (c - c0 + 1) * P], ACT.Copy,
-                    scale=gcol[:, c - 2 : c - 1],
-                )
-
-        def last_by_rows(c0, c1, b):
-            for j in range(c1 - c0):
-                nc.tensor.transpose(banks[b][:, j * P : (j + 1) * P], gated[c0][:, j, :], ident[:])
-            nc.scalar.copy(y_last[:, (c0 - 2) * P : (c1 - 2) * P], banks[b][:, 0 : (c1 - c0) * P])
-
-        def frozen(nb, th, b):
-            cols = slice(th * BANK, (th + 1) * BANK)
-            nc.tensor.matmul_mx(
-                banks[b][:], lhsT=ww[:, 2 * nb * P : 2 * (nb + 1) * P].bitcast(FP4X4),
-                lhsT_scale=ws[:, nb * P : (nb + 1) * P],
-                rhs=xw[:, cols].bitcast(FP8X4), rhs_scale=xs[:, cols], start=True, stop=True,
+            nc.vector.tensor_tensor(
+                gated[:, nb0:nb1, e * C + s0 : e * C + s1], banks[b][:].rearrange("p (j s) -> p j s", s=width),
+                g.unsqueeze(1).broadcast_to([P, nb1 - nb0, width]), ALU.mult,
             )
 
-        def frozen_to_sbuf(nb, two_banks):
-            base[nb] = held([P, T], F32, "base%d" % nb)
+        def two_blocks(e, nb0, b):
+            second_layer(e, 0, C, nb0, nb0 + 2, b, g1[:, (e - 1) * C : e * C])
+
+        def scatter_scalar(nb, j0, j1):
+            nc.scalar.activation(win[nb][:].indirect(offsets[:, j0 // 16 : j1 // 16]), gated[:, nb, j0:j1], ACT.Copy)
+
+        def scatter_vector(nb, j0, j1):
+            nc.vector.tensor_copy(win[nb][:].indirect(offsets[:, j0 // 16 : j1 // 16]), gated[:, nb, j0:j1])
+
+        def finish(nb, two_banks, cuts):
             for th, b in enumerate(two_banks):
-                frozen(nb, th, b)
-                nc.scalar.copy(base[nb][:, th * BANK : (th + 1) * BANK], banks[b][:])
-
-        def finish_on_gpsimd(nb, buffer):
-            res = held([P, T], F32, "res%d" % nb, buffer)
-            nc.gpsimd.tensor_tensor(res[:], base[nb][:], win[nb][:, 0:T], ALU.add)
-            nc.sync.dma_start(out[nb * P : (nb + 1) * P, :], res[:])
-
-        def finish_on_tensor(nb, sum_banks, back_banks):
-            summed = [banks[b][:].rearrange("p (j n) -> p j n", j=4) for b in sum_banks]
-            for th in range(2):
-                for j in range(4):
-                    t0 = th * BANK + j * P
-                    nc.tensor.matmul(summed[th][:, j, :], base[nb][:, t0 : t0 + P], ident[:],
-                                     start=j == 0, stop=False, is_transpose=True)
-            for th in range(2):
-                for j in range(4):
-                    t0 = th * BANK + j * P
-                    nc.tensor.matmul(summed[th][:, j, :], win[nb][:, t0 : t0 + P], ident[:],
-                                     start=False, stop=j == 3, is_transpose=True)
-                flipped = held([P, 4, P], F32, "flipped%d_%d" % (nb, th))
-                nc.scalar.copy(flipped[:], summed[th])
-                back = banks[back_banks[th]][:].rearrange("p (j t) -> p j t", j=4)
-                for j in range(4):
-                    nc.tensor.transpose(back[:, j, :], flipped[:, j, :], ident[:])
-                res = held([P, BANK], F32, "res%d_%d" % (nb, th))
-                nc.scalar.copy(res[:], banks[back_banks[th]][:])
-                nc.scalar.dma_start(out[nb * P : (nb + 1) * P, th * BANK : (th + 1) * BANK], res[:])
-
-        def finish_last(nb, base_banks):
-            res = held([P, T - GPSIMD_COLS], F32, "last")
-            for col, end in ((0, 192), (192, BANK), (BANK, T - GPSIMD_COLS)):
-                th, off = divmod(col, BANK)
-                cols = slice(col, end)
-                nc.vector.tensor_tensor(
-                    res[:, cols], banks[base_banks[th]][:, off : off + end - col], win[nb][:, cols], ALU.add
+                cols = slice(th * BANK, (th + 1) * BANK)
+                nc.tensor.matmul_mx(
+                    banks[b][:], lhsT=ww[:, 2 * nb * P : 2 * (nb + 1) * P].bitcast(FP4X4),
+                    lhsT_scale=ws[:, nb * P : (nb + 1) * P],
+                    rhs=xw[:, cols].bitcast(FP8X4), rhs_scale=xs[:, cols], start=True, stop=True,
                 )
-                nc.scalar.dma_start(out[nb * P : (nb + 1) * P, cols], res[:, cols])
-            cols = slice(T - GPSIMD_COLS, T)
-            tail = held([P, GPSIMD_COLS], F32, "tail")
-            nc.gpsimd.tensor_tensor(tail[:], base_tail[:], win[nb][:, cols], ALU.add)
-            nc.scalar.dma_start(out[nb * P : (nb + 1) * P, cols], tail[:])
+            res = held([P, T], F32, "res%d" % nb)
+            done = 0
+            for col, end, store in cuts:
+                th, off = divmod(col, BANK)
+                nc.vector.tensor_tensor(
+                    res[:, col:end], banks[two_banks[th]][:, off : off + end - col], win[nb][:, col:end], ALU.add
+                )
+                if store:
+                    nc.sync.dma_start(out[nb * P : (nb + 1) * P, done:end], res[:, done:end])
+                    done = end
+
+        whole = ((0, BANK, False), (BANK, T, True))
+        halves = ((0, BANK, True), (BANK, T, True))
+        last = ((0, 256, True), (256, BANK, True), (BANK, 832, True), (832, T, True))
 
         gather_scales(0, 3, None)
         gather_words(0, 1)
@@ -304,52 +204,43 @@ def tile_moe_adp_silu_kernel(
         gather_words(2, 4)
         gather_words(4, CHUNKS)
 
-        first_layer_direct(0, 0)
-        gather_scales(3, 4, "hcol0")
-        first_layer_direct(1, 1)
-        first_layer(2, (2,))
-        front_one(0, 0, 1, 4)
-        front_one(1, 0, 1, 5)
-        front_one(0, 1, 2, 3)
-        front_one(1, 1, 2, 1)
-        first_layer(3, (4,))
-        first_back(2, 6, None)
-        turn(2, 5, 0)
-        turn(3, 5, 2 * P)
-        first_layer(4, (2,))
-        quantise(2, 4, 5, None)
-        first_back(3, 7, "hrow3")
-        front_one(0, 2, 4, 0)
-        turn(4, 3, 0)
-        first_layer(5, (4,))
-        turn(5, 3, 2 * P)
-        first_layer(6, (2,))
-        quantise(4, 6, 3, None)
-        front_one(1, 2, 4, 4)
-        turn(6, 5, 0)
-        first_layer(7, (7,))
-        turn(7, 5, 2 * P)
-        quantise(6, 8, 5, None)
-        front_one(0, 4, 6, 7)
-        front_one(1, 4, 6, 5)
-        third(1, 3, 7)
-        front_one(0, 6, 8, 3)
-        front_one(1, 6, 8, 1)
-        third(3, 4, 5)
-        scatter_gated(2, 2, CHUNKS, y_third[:])
-        frozen_to_sbuf(0, (5, 7))
-        last_by_slots(2, 6, 1, None)
-        last_by_slots(6, 8, 6, None)
-        frozen_to_sbuf(1, (5, 7))
-        last_by_rows(2, 6, 1)
-        last_by_rows(6, 8, 6)
-        nc.vector.tensor_copy(win[3][:].indirect(entries(2, CHUNKS)), y_last[:])
-        finish_on_tensor(0, (0, 2), (5, 7))
-        frozen_to_sbuf(2, (1, 6))
-        finish_on_tensor(1, (3, 4), (0, 2))
-        frozen(3, 1, 0)
-        frozen(3, 0, 2)
-        base_tail = held([P, GPSIMD_COLS], F32, "base_tail")
-        nc.scalar.copy(base_tail[:], banks[0][:, BANK - GPSIMD_COLS : BANK])
-        finish_on_gpsimd(2, None)
-        finish_last(3, (2, 0))
+        hq[0] = held([P, C], U32, "hq0")
+        first_layer(0, 0)
+        quantise_chunk(0)
+        first_layer(1, 1)
+        gather_scales(3, 4, None)
+        quantise_chunk(1)
+        first_layer(2, 2)
+        first_layer(3, 0)
+        second_layer(0, 0, P, 0, 4, 3, g0[:, 0:P])
+        second_layer(0, P, C, 0, 4, 4, g0[:, P:C])
+        scatter_scalar(1, 0, 128)
+        scatter_vector(0, 0, 128)
+        quantise(1, "g0")
+        scatter_vector(0, 128, 256)
+        first_layer(4, 1)
+        first_layer(5, 2)
+        first_layer(6, 0)
+        first_layer(7, 7)
+        two_blocks(1, 0, 1)
+        quantise(2, None)
+        two_blocks(1, 2, 0)
+        quantise(3, None)
+        scatter_scalar(1, 128, 512)
+        scatter_vector(0, 256, 512)
+        scatter_scalar(2, 0, 384)
+        scatter_scalar(3, 0, 384)
+        two_blocks(2, 0, 2)
+        two_blocks(3, 0, 7)
+        two_blocks(2, 2, 1)
+        scatter_vector(0, 512, 1024)
+        two_blocks(3, 2, 0)
+        scatter_scalar(2, 384, 768)
+        scatter_scalar(3, 384, 768)
+        scatter_scalar(2, 768, 1024)
+        scatter_scalar(3, 768, 1024)
+        finish(0, (5, 6), whole)
+        scatter_vector(1, 512, 1024)
+        finish(1, (3, 4), halves)
+        finish(2, (3, 4), halves)
+        finish(3, (3, 4), last)

@@ -71,12 +71,12 @@ def tile_moe_adp_silu_kernel(
         for q in range(1, 4):
             load_adapter_plane(was, wa_scales, q, nc.sync)
         wa1 = load_words(wa_words[1, 0], "wa1")
+        wb0 = load_words(wb_words[0, 0], "wb0")
         for q in range(4):
             load_adapter_plane(wbs, wb_scales, q, nc.sync)
-        wb0 = load_words(wb_words[0, 0], "wb0")
+        wa = [wa0[:], wa1[:]] + [load_words(wa_words[e, 0], "wa%d" % e)[:] for e in range(2, E)]
         g0 = held([P, C], F32, "g0")
         nc.sync.dma_start(g0[:], gate[:, 0:C])
-        wa = [wa0[:], wa1[:]] + load_many(wa_words[2:E, 0], "wa_rest")
         g1 = held([P, (E - 1) * C], F32, "g1")
         nc.sync.dma_start(g1[:], gate[:, C : E * C])
         wb1 = load_words(wb_words[1, 0], "wb1")
@@ -130,8 +130,13 @@ def tile_moe_adp_silu_kernel(
 
         def first_layer(c, b):
             e, half = divmod(c, 2)
-            if half == 0:
-                hcol[e] = held([P, 4 * C], BF16, "hcol%d" % e)
+            if e == 0:
+                hcol[0, half] = held([P, BANK], BF16, "hchunk%d" % half)
+                h = hcol[0, half][:]
+            else:
+                if half == 0:
+                    hcol[e] = held([P, 4 * C], BF16, "hcol%d" % e)
+                h = hcol[e][:, half * BANK : (half + 1) * BANK]
             for d in range(4):
                 part = slice(d * P, (d + 1) * P)
                 nc.tensor.matmul_mx(
@@ -139,7 +144,7 @@ def tile_moe_adp_silu_kernel(
                     rhs=xg[c].bitcast(FP8X4), rhs_scale=xsg[e][:, half * P : (half + 1) * P], start=True, stop=True,
                 )
             nc.scalar.activation(
-                hcol[e][:, half * BANK : (half + 1) * BANK].rearrange("p (s d) -> p s d", d=4),
+                h.rearrange("p (s d) -> p s d", d=4),
                 banks[b][:].rearrange("p (d s) -> p s d", d=4),
                 ACT.Silu,
             )
@@ -150,10 +155,12 @@ def tile_moe_adp_silu_kernel(
 
         def quantise_chunk(c):
             cols = slice(c * P, (c + 1) * P)
-            nc.vector.quantize_mx(hq[0][:, cols].bitcast(FP8X4), hs[0][:, cols], hcol[0][:, c * BANK : (c + 1) * BANK])
+            nc.vector.quantize_mx(hq[0][:, cols].bitcast(FP8X4), hs[0][:, cols], hcol[0, c][:])
 
-        def second_layer(e, s0, s1, nb0, nb1, b, g):
+        def second_layer(e, s0, s1, nb0, nb1, b, g, dst=None):
             width = s1 - s0
+            if dst is None:
+                dst = gated[:, nb0:nb1, e * C + s0 : e * C + s1]
             for nb in range(nb0, nb1):
                 rows = slice(nb * P, (nb + 1) * P)
                 nc.tensor.matmul_mx(
@@ -162,7 +169,7 @@ def tile_moe_adp_silu_kernel(
                     start=True, stop=True,
                 )
             nc.vector.tensor_tensor(
-                gated[:, nb0:nb1, e * C + s0 : e * C + s1], banks[b][:].rearrange("p (j s) -> p j s", s=width),
+                dst, banks[b][:, 0 : (nb1 - nb0) * width].rearrange("p (j s) -> p j s", s=width),
                 g.unsqueeze(1).broadcast_to([P, nb1 - nb0, width]), ALU.mult,
             )
 
@@ -208,39 +215,40 @@ def tile_moe_adp_silu_kernel(
         first_layer(0, 0)
         quantise_chunk(0)
         first_layer(1, 1)
-        gather_scales(3, 4, None)
+        gather_scales(3, 4, "hchunk0")
         quantise_chunk(1)
         first_layer(2, 2)
-        first_layer(3, 0)
-        second_layer(0, 0, P, 0, 4, 3, g0[:, 0:P])
-        second_layer(0, P, C, 0, 4, 4, g0[:, P:C])
-        scatter_scalar(1, 0, 128)
-        scatter_vector(0, 0, 128)
-        quantise(1, "g0")
-        scatter_vector(0, 128, 256)
-        first_layer(4, 1)
-        first_layer(5, 2)
+        first_layer(3, 3)
+        first = held([P, 1, P], F32, "first")
+        second_layer(0, 0, P, 0, 1, 6, g0[:, 0:P], first[:])
+        second_layer(0, 0, P, 1, 4, 7, g0[:, 0:P])
+        nc.vector.tensor_copy(win[0][:].indirect(offsets[:, 0:LIST_COLS]), first[:, 0, :])
+        first_layer(4, 4)
+        first_layer(5, 5)
         first_layer(6, 0)
+        second_layer(0, P, C, 0, 4, 6, g0[:, P:C])
         first_layer(7, 7)
+        quantise(1, "first")
+        scatter_vector(0, 128, 256)
+        for nb in range(1, 4):
+            scatter_scalar(nb, 0, 256)
         two_blocks(1, 0, 1)
-        quantise(2, None)
+        quantise(2, "hcol1")
         two_blocks(1, 2, 0)
-        quantise(3, None)
-        scatter_scalar(1, 128, 512)
+        quantise(3, "hcol2")
+        scatter_scalar(1, 256, 512)
         scatter_vector(0, 256, 512)
-        scatter_scalar(2, 0, 384)
-        scatter_scalar(3, 0, 384)
         two_blocks(2, 0, 2)
-        two_blocks(3, 0, 7)
-        two_blocks(2, 2, 1)
+        two_blocks(3, 0, 3)
+        two_blocks(2, 2, 4)
         scatter_vector(0, 512, 1024)
-        two_blocks(3, 2, 0)
-        scatter_scalar(2, 384, 768)
-        scatter_scalar(3, 384, 768)
-        scatter_scalar(2, 768, 1024)
-        scatter_scalar(3, 768, 1024)
-        finish(0, (5, 6), whole)
+        two_blocks(3, 2, 5)
+        scatter_scalar(2, 256, 640)
+        scatter_scalar(3, 256, 640)
+        scatter_scalar(2, 640, 1024)
+        scatter_scalar(3, 640, 1024)
+        finish(0, (6, 7), whole)
         scatter_vector(1, 512, 1024)
-        finish(1, (3, 4), halves)
-        finish(2, (3, 4), halves)
-        finish(3, (3, 4), last)
+        finish(2, (6, 7), halves)
+        finish(1, (0, 1), halves)
+        finish(3, (6, 7), last)

@@ -71,10 +71,11 @@ def tile_moe_adp_silu_kernel(
         for q in range(1, 4):
             load_adapter_plane(was, wa_scales, q, nc.sync)
         wa1 = load_words(wa_words[1, 0], "wa1")
+        wa2 = load_words(wa_words[2, 0], "wa2")
         wb0 = load_words(wb_words[0, 0], "wb0")
         for q in range(4):
             load_adapter_plane(wbs, wb_scales, q, nc.sync)
-        wa = [wa0[:], wa1[:]] + [load_words(wa_words[e, 0], "wa%d" % e)[:] for e in range(2, E)]
+        wa = [wa0[:], wa1[:], wa2[:], load_words(wa_words[3, 0], "wa3")[:]]
         g0 = held([P, C], F32, "g0")
         nc.sync.dma_start(g0[:], gate[:, 0:C])
         g1 = held([P, (E - 1) * C], F32, "g1")
@@ -90,18 +91,15 @@ def tile_moe_adp_silu_kernel(
         was_dealt = held([P, H], U8, "was_dealt")
 
         def deal_words(e):
-            nc.gpsimd.tensor_copy(
-                wa_dealt[e][:].rearrange("p (d m) -> p d m", d=4), wa[e].rearrange("p (m d) -> p d m", d=4)
+            nc.vector.tensor_copy(
+                wa_dealt[e][:].rearrange("p (d g m) -> p g d m", d=4, m=4),
+                wa[e].rearrange("p (g m d) -> p g d m", d=4, m=4),
             )
 
-        deal_words(0)
-        for d0 in (0, 2):
-            nc.gpsimd.tensor_copy(
-                was_dealt[:].rearrange("p (d m) -> p d m", d=4)[:, d0 : d0 + 2, :],
-                was[:].rearrange("p (m d) -> p d m", d=4)[:, d0 : d0 + 2, :],
+        def deal_scales():
+            nc.vector.tensor_copy(
+                was_dealt[:].rearrange("p (d m) -> p d m", d=4), was[:].rearrange("p (m d) -> p d m", d=4)
             )
-        for e in range(1, E):
-            deal_words(e)
 
         def entries(e0, e1):
             return offsets[:, e0 * C // 16 : e1 * C // 16]
@@ -120,8 +118,8 @@ def tile_moe_adp_silu_kernel(
             for e in range(e0, e1):
                 xsg[e] = tile[:, (e - e0) * C : (e - e0 + 1) * C]
 
-        def gather_words(c0, c1):
-            tile = held([P, (c1 - c0) * P], U32, "xg%d" % c0)
+        def gather_words(c0, c1, buffer):
+            tile = held([P, (c1 - c0) * P], U32, "xg%d" % c0, buffer)
             nc.vector.tensor_copy(
                 tile[:], xw[:].bitcast(U32).indirect(offsets[:, c0 * LIST_COLS : c1 * LIST_COLS])
             )
@@ -130,13 +128,9 @@ def tile_moe_adp_silu_kernel(
 
         def first_layer(c, b):
             e, half = divmod(c, 2)
-            if e == 0:
-                hcol[0, half] = held([P, BANK], BF16, "hchunk%d" % half)
-                h = hcol[0, half][:]
-            else:
-                if half == 0:
-                    hcol[e] = held([P, 4 * C], BF16, "hcol%d" % e)
-                h = hcol[e][:, half * BANK : (half + 1) * BANK]
+            if half == 0:
+                hcol[e] = held([P, 4 * C], BF16, "hcol%d" % e)
+            h = hcol[e][:, half * BANK : (half + 1) * BANK]
             for d in range(4):
                 part = slice(d * P, (d + 1) * P)
                 nc.tensor.matmul_mx(
@@ -152,10 +146,6 @@ def tile_moe_adp_silu_kernel(
         def quantise(e, buffer):
             hq[e] = held([P, C], U32, "hq%d" % e, buffer)
             nc.vector.quantize_mx(hq[e][:].bitcast(FP8X4), hs[e][:], hcol[e][:])
-
-        def quantise_chunk(c):
-            cols = slice(c * P, (c + 1) * P)
-            nc.vector.quantize_mx(hq[0][:, cols].bitcast(FP8X4), hs[0][:, cols], hcol[0, c][:])
 
         def second_layer(e, s0, s1, nb0, nb1, b, g, dst=None):
             width = s1 - s0
@@ -174,7 +164,7 @@ def tile_moe_adp_silu_kernel(
             )
 
         def two_blocks(e, nb0, b):
-            second_layer(e, 0, C, nb0, nb0 + 2, b, g1[:, (e - 1) * C : e * C])
+            second_layer(e, 0, C, nb0, nb0 + 2, b, g1[:, (e - 1) * C : e * C] if e else g0[:])
 
         def scatter_scalar(nb, j0, j1):
             nc.scalar.activation(win[nb][:].indirect(offsets[:, j0 // 16 : j1 // 16]), gated[:, nb, j0:j1], ACT.Copy)
@@ -205,44 +195,43 @@ def tile_moe_adp_silu_kernel(
         halves = ((0, BANK, True), (BANK, T, True))
         last = ((0, 256, True), (256, BANK, True), (BANK, 832, True), (832, T, True))
 
-        gather_scales(0, 3, None)
-        gather_words(0, 1)
-        gather_words(1, 2)
-        gather_words(2, 4)
-        gather_words(4, CHUNKS)
-
-        hq[0] = held([P, C], U32, "hq0")
+        gather_scales(0, 2, None)
+        deal_words(0)
+        gather_words(0, 2, None)
+        deal_scales()
+        deal_words(1)
+        gather_words(2, 4, "was")
         first_layer(0, 0)
-        quantise_chunk(0)
         first_layer(1, 1)
-        gather_scales(3, 4, "hchunk0")
-        quantise_chunk(1)
-        first_layer(2, 2)
-        first_layer(3, 3)
-        first = held([P, 1, P], F32, "first")
-        second_layer(0, 0, P, 0, 1, 6, g0[:, 0:P], first[:])
-        second_layer(0, 0, P, 1, 4, 7, g0[:, 0:P])
-        nc.vector.tensor_copy(win[0][:].indirect(offsets[:, 0:LIST_COLS]), first[:, 0, :])
-        first_layer(4, 4)
-        first_layer(5, 5)
-        first_layer(6, 0)
-        second_layer(0, P, C, 0, 4, 6, g0[:, P:C])
+        gather_scales(2, 3, "wa1")
+        gather_words(4, 6, "wa_dealt0")
+        deal_words(2)
+        quantise(0, None)
+        gather_scales(3, 4, "wa2")
+        gather_words(6, 8, "hcol0")
+        for c in range(2, 6):
+            first_layer(c, c)
+        deal_words(3)
+        two_blocks(0, 0, 6)
+        two_blocks(0, 2, 7)
+        scatter_scalar(1, 0, 256)
+        scatter_vector(0, 0, 256)
+        first_layer(6, 6)
         first_layer(7, 7)
-        quantise(1, "first")
-        scatter_vector(0, 128, 256)
-        for nb in range(1, 4):
-            scatter_scalar(nb, 0, 256)
-        two_blocks(1, 0, 1)
+        quantise(1, "g0")
+        scatter_scalar(2, 0, 256)
+        scatter_scalar(3, 0, 256)
+        two_blocks(1, 0, 2)
         quantise(2, "hcol1")
-        two_blocks(1, 2, 0)
+        two_blocks(1, 2, 3)
         quantise(3, "hcol2")
         scatter_scalar(1, 256, 512)
         scatter_vector(0, 256, 512)
-        two_blocks(2, 0, 2)
-        two_blocks(3, 0, 3)
-        two_blocks(2, 2, 4)
+        two_blocks(2, 0, 4)
+        two_blocks(3, 0, 5)
+        two_blocks(2, 2, 2)
         scatter_vector(0, 512, 1024)
-        two_blocks(3, 2, 5)
+        two_blocks(3, 2, 3)
         scatter_scalar(2, 256, 640)
         scatter_scalar(3, 256, 640)
         scatter_scalar(2, 640, 1024)

@@ -28,16 +28,20 @@ def tile_moe_adp_silu_kernel(
     nc = tc.nc
     with ExitStack() as ctx:
         keep = ctx.enter_context(tc.tile_pool(name="keep", bufs=1))
+        shared = ctx.enter_context(tc.tile_pool(name="shared", bufs=1))
         psum = ctx.enter_context(tc.psum_pool(name="psum", bufs=1))
 
         def held(shape, dtype, name, tag=None):
             return keep.tile(shape, dtype, name=name, tag=tag or name, align_bytes=64)
 
+        def placed(shape, dtype, name, offset):
+            return shared.tile(shape, dtype, name=name, tag=name, align_bytes=64, offset=offset)
+
         offsets = keep.tile([P, E * C // 16], U16, name="offsets")
         nc.sync.dma_start(offsets[:], offs)
 
         xs = held([P, T], U8, "xs")
-        was = held([P, H], U8, "was")
+        was = placed([P, H], U8, "was", 4096)
         wbs = held([P, N], U8, "wbs")
         ws = held([P, N], U8, "ws")
         nc.gpsimd.memset(was[:].bitcast(I32), 0)
@@ -49,8 +53,8 @@ def tile_moe_adp_silu_kernel(
                 plane[32 * q : 32 * q + 16, :].bitcast(I32), scales[:, 0, 4 * q : 4 * q + 4, :].bitcast(I32)
             )
 
-        def load_words(src, name):
-            words = held([P, src.shape[1]], I32, name)
+        def load_words(src, name, offset=None):
+            words = held([P, src.shape[1]], I32, name) if offset is None else placed([P, src.shape[1]], I32, name, offset)
             nc.sync.dma_start(words[:], src.rearrange("p c d -> p (c d)").bitcast(I32))
             return words
 
@@ -71,7 +75,7 @@ def tile_moe_adp_silu_kernel(
         for q in range(1, 4):
             load_adapter_plane(was, wa_scales, q, nc.sync)
         wa1 = load_words(wa_words[1, 0], "wa1")
-        wa2 = load_words(wa_words[2, 0], "wa2")
+        wa2 = load_words(wa_words[2, 0], "wa2", 1024)
         wb0 = load_words(wb_words[0, 0], "wb0")
         for q in range(4):
             load_adapter_plane(wbs, wb_scales, q, nc.sync)
@@ -90,10 +94,10 @@ def tile_moe_adp_silu_kernel(
         wa_dealt = [held([P, H], I32, "wa_dealt%d" % e) for e in range(E)]
         was_dealt = held([P, H], U8, "was_dealt")
 
-        def deal_words(e):
-            nc.vector.tensor_copy(
-                wa_dealt[e][:].rearrange("p (d g m) -> p g d m", d=4, m=4),
-                wa[e].rearrange("p (g m d) -> p g d m", d=4, m=4),
+        def deal_words(e, copy):
+            copy(
+                wa_dealt[e][:].bitcast(U32).rearrange("p (d g m) -> p g d m", d=4, m=4),
+                wa[e].bitcast(U32).rearrange("p (g m d) -> p g d m", d=4, m=4),
             )
 
         def deal_scales():
@@ -112,16 +116,14 @@ def tile_moe_adp_silu_kernel(
         gated = held([P, 4, E * C], F32, "gated")
         hcol = {}
 
-        def gather_scales(e0, e1, buffer):
-            tile = held([P, (e1 - e0) * C], U8, "xsg%d" % e0, buffer)
+        def gather_scales(e0, e1, tile):
             nc.vector.tensor_copy(tile[:], xs[:].indirect(entries(e0, e1)))
             for e in range(e0, e1):
                 xsg[e] = tile[:, (e - e0) * C : (e - e0 + 1) * C]
 
-        def gather_words(c0, c1, buffer):
-            tile = held([P, (c1 - c0) * P], U32, "xg%d" % c0, buffer)
+        def gather_words(c0, c1, tile):
             nc.vector.tensor_copy(
-                tile[:], xw[:].bitcast(U32).indirect(offsets[:, c0 * LIST_COLS : c1 * LIST_COLS])
+                tile, xw[:].bitcast(U32).indirect(offsets[:, c0 * LIST_COLS : c1 * LIST_COLS])
             )
             for c in range(c0, c1):
                 xg[c] = tile[:, (c - c0) * P : (c - c0 + 1) * P]
@@ -129,7 +131,10 @@ def tile_moe_adp_silu_kernel(
         def first_layer(c, b):
             e, half = divmod(c, 2)
             if half == 0:
-                hcol[e] = held([P, 4 * C], BF16, "hcol%d" % e)
+                if e < 2:
+                    hcol[e] = placed([P, 4 * C], BF16, "hcol%d" % e, 2048 * e)
+                else:
+                    hcol[e] = held([P, 4 * C], BF16, "hcol%d" % e)
             h = hcol[e][:, half * BANK : (half + 1) * BANK]
             for d in range(4):
                 part = slice(d * P, (d + 1) * P)
@@ -144,7 +149,7 @@ def tile_moe_adp_silu_kernel(
             )
 
         def quantise(e, buffer):
-            hq[e] = held([P, C], U32, "hq%d" % e, buffer)
+            hq[e] = placed([P, C], U32, "hq2", 2048) if e == 2 else held([P, C], U32, "hq%d" % e, buffer)
             nc.vector.quantize_mx(hq[e][:].bitcast(FP8X4), hs[e][:], hcol[e][:])
 
         def second_layer(e, s0, s1, nb0, nb1, b, g, dst=None):
@@ -195,34 +200,35 @@ def tile_moe_adp_silu_kernel(
         halves = ((0, BANK, True), (BANK, T, True))
         last = ((0, 256, True), (256, BANK, True), (BANK, 832, True), (832, T, True))
 
-        gather_scales(0, 2, None)
-        deal_words(0)
-        gather_words(0, 2, None)
+        warm = held([P, 2], F32, "warm")
+        nc.vector.memset(warm[:, 0:1], 0.0)
+        nc.scalar.activation(warm[:, 1:2], warm[:, 0:1], ACT.Silu)
+        gather_scales(0, 3, held([P, 3 * C], U8, "xsg_first"))
+        for e in range(3):
+            deal_words(e, nc.scalar.copy)
+        gather_words(0, 1, held([P, P], U32, "xg_first")[:])
         deal_scales()
-        deal_words(1)
-        gather_words(2, 4, "was")
+        xg_rest = placed([P, (CHUNKS - 1) * P], U32, "xg_rest", 4096 + C)
+        for c0, c1 in ((1, 2), (2, 4), (4, 6), (6, 8)):
+            gather_words(c0, c1, xg_rest[:, (c0 - 1) * P : (c1 - 1) * P])
+        gather_scales(3, 4, placed([P, C], U8, "xsg_last", 4096))
         first_layer(0, 0)
         first_layer(1, 1)
-        gather_scales(2, 3, "wa1")
-        gather_words(4, 6, "wa_dealt0")
-        deal_words(2)
         quantise(0, None)
-        gather_scales(3, 4, "wa2")
-        gather_words(6, 8, "hcol0")
         for c in range(2, 6):
             first_layer(c, c)
-        deal_words(3)
+        deal_words(3, nc.vector.tensor_copy)
         two_blocks(0, 0, 6)
         two_blocks(0, 2, 7)
+        first_layer(6, 0)
+        first_layer(7, 1)
         scatter_scalar(1, 0, 256)
         scatter_vector(0, 0, 256)
-        first_layer(6, 6)
-        first_layer(7, 7)
         quantise(1, "g0")
         scatter_scalar(2, 0, 256)
         scatter_scalar(3, 0, 256)
         two_blocks(1, 0, 2)
-        quantise(2, "hcol1")
+        quantise(2, None)
         two_blocks(1, 2, 3)
         quantise(3, "hcol2")
         scatter_scalar(1, 256, 512)

@@ -41,7 +41,7 @@ def tile_moe_adp_silu_kernel(
         nc.sync.dma_start(offsets[:], offs)
 
         xs = held([P, T], U8, "xs")
-        was = placed([P, H], U8, "was", 4096)
+        was = held([P, H], U8, "was")
         wbs = held([P, N], U8, "wbs")
         ws = held([P, N], U8, "ws")
         nc.gpsimd.memset(was[:].bitcast(I32), 0)
@@ -74,11 +74,11 @@ def tile_moe_adp_silu_kernel(
         xw = load_words(x_words[0], "xw")
         for q in range(1, 4):
             load_adapter_plane(was, wa_scales, q, nc.sync)
-        wa1 = load_words(wa_words[1, 0], "wa1")
-        wa2 = load_words(wa_words[2, 0], "wa2", 1024)
+        wa1 = load_words(wa_words[1, 0], "wa1", 2048)
         wb0 = load_words(wb_words[0, 0], "wb0")
         for q in range(4):
             load_adapter_plane(wbs, wb_scales, q, nc.sync)
+        wa2 = load_words(wa_words[2, 0], "wa2", 6144)
         wa = [wa0[:], wa1[:], wa2[:], load_words(wa_words[3, 0], "wa3")[:]]
         g0 = held([P, C], F32, "g0")
         nc.sync.dma_start(g0[:], gate[:, 0:C])
@@ -101,9 +101,11 @@ def tile_moe_adp_silu_kernel(
             )
 
         def deal_scales():
-            nc.vector.tensor_copy(
-                was_dealt[:].rearrange("p (d m) -> p d m", d=4), was[:].rearrange("p (m d) -> p d m", d=4)
-            )
+            for d0 in (0, 2):
+                nc.gpsimd.tensor_copy(
+                    was_dealt[:].rearrange("p (d m) -> p d m", d=4)[:, d0 : d0 + 2, :],
+                    was[:].rearrange("p (m d) -> p d m", d=4)[:, d0 : d0 + 2, :],
+                )
 
         def entries(e0, e1):
             return offsets[:, e0 * C // 16 : e1 * C // 16]
@@ -132,7 +134,7 @@ def tile_moe_adp_silu_kernel(
             e, half = divmod(c, 2)
             if half == 0:
                 if e < 2:
-                    hcol[e] = placed([P, 4 * C], BF16, "hcol%d" % e, 2048 * e)
+                    hcol[e] = placed([P, 4 * C], BF16, "hcol%d" % e, (256, 3328)[e])
                 else:
                     hcol[e] = held([P, 4 * C], BF16, "hcol%d" % e)
             h = hcol[e][:, half * BANK : (half + 1) * BANK]
@@ -149,18 +151,25 @@ def tile_moe_adp_silu_kernel(
             )
 
         def quantise(e, buffer):
-            hq[e] = placed([P, C], U32, "hq2", 2048) if e == 2 else held([P, C], U32, "hq%d" % e, buffer)
+            hq[e] = placed([P, C], U32, "hq2", 3328) if e == 2 else held([P, C], U32, "hq%d" % e, buffer)
             nc.vector.quantize_mx(hq[e][:].bitcast(FP8X4), hs[e][:], hcol[e][:])
+
+        def quantise_chunk(c, codes):
+            hq[0, c] = codes
+            nc.vector.quantize_mx(
+                codes[:].bitcast(FP8X4), hs[0][:, c * P : (c + 1) * P], hcol[0][:, c * BANK : (c + 1) * BANK]
+            )
 
         def second_layer(e, s0, s1, nb0, nb1, b, g, dst=None):
             width = s1 - s0
+            codes = hq[e][:] if e else hq[0, s0 // P][:]
             if dst is None:
                 dst = gated[:, nb0:nb1, e * C + s0 : e * C + s1]
             for nb in range(nb0, nb1):
                 rows = slice(nb * P, (nb + 1) * P)
                 nc.tensor.matmul_mx(
                     banks[b][:, (nb - nb0) * width : (nb - nb0 + 1) * width], lhsT=wb[e][:, rows].bitcast(FP8X4),
-                    lhsT_scale=wbs[4 * e : P, rows], rhs=hq[e][:, s0:s1].bitcast(FP8X4), rhs_scale=hs[e][:, s0:s1],
+                    lhsT_scale=wbs[4 * e : P, rows], rhs=codes.bitcast(FP8X4), rhs_scale=hs[e][:, s0:s1],
                     start=True, stop=True,
                 )
             nc.vector.tensor_tensor(
@@ -169,7 +178,7 @@ def tile_moe_adp_silu_kernel(
             )
 
         def two_blocks(e, nb0, b):
-            second_layer(e, 0, C, nb0, nb0 + 2, b, g1[:, (e - 1) * C : e * C] if e else g0[:])
+            second_layer(e, 0, C, nb0, nb0 + 2, b, g1[:, (e - 1) * C : e * C])
 
         def scatter_scalar(nb, j0, j1):
             nc.scalar.activation(win[nb][:].indirect(offsets[:, j0 // 16 : j1 // 16]), gated[:, nb, j0:j1], ACT.Copy)
@@ -204,34 +213,39 @@ def tile_moe_adp_silu_kernel(
         nc.vector.memset(warm[:, 0:1], 0.0)
         nc.scalar.activation(warm[:, 1:2], warm[:, 0:1], ACT.Silu)
         gather_scales(0, 3, held([P, 3 * C], U8, "xsg_first"))
-        for e in range(3):
+        for e in range(2):
             deal_words(e, nc.scalar.copy)
-        gather_words(0, 1, held([P, P], U32, "xg_first")[:])
         deal_scales()
-        xg_rest = placed([P, (CHUNKS - 1) * P], U32, "xg_rest", 4096 + C)
-        for c0, c1 in ((1, 2), (2, 4), (4, 6), (6, 8)):
-            gather_words(c0, c1, xg_rest[:, (c0 - 1) * P : (c1 - 1) * P])
-        gather_scales(3, 4, placed([P, C], U8, "xsg_last", 4096))
+        for c0, c1 in ((0, 1), (1, 2), (2, 4), (4, 8)):
+            gather_words(c0, c1, held([P, (c1 - c0) * P], U32, "xg%d" % c0)[:])
+        gather_scales(3, 4, placed([P, C], U8, "xsg_last", 2304))
         first_layer(0, 0)
+        quantise_chunk(0, held([P, P], U32, "hq_first"))
         first_layer(1, 1)
-        quantise(0, None)
-        for c in range(2, 6):
-            first_layer(c, c)
+        deal_words(2, nc.vector.tensor_copy)
+        quantise_chunk(1, placed([P, P], U32, "hq_second", 6144))
         deal_words(3, nc.vector.tensor_copy)
-        two_blocks(0, 0, 6)
-        two_blocks(0, 2, 7)
+        first_layer(2, 2)
+        first_layer(3, 3)
+        first = held([P, 1, P], F32, "first")
+        second_layer(0, 0, P, 0, 1, 6, g0[:, 0:P], first[:])
+        second_layer(0, 0, P, 1, 4, 7, g0[:, 0:P])
+        nc.vector.tensor_copy(win[0][:].indirect(offsets[:, 0:LIST_COLS]), first[:, 0, :])
+        first_layer(4, 4)
+        first_layer(5, 5)
         first_layer(6, 0)
-        first_layer(7, 1)
-        scatter_scalar(1, 0, 256)
-        scatter_vector(0, 0, 256)
-        quantise(1, "g0")
+        second_layer(0, P, C, 0, 4, 6, g0[:, P:C])
+        first_layer(7, 7)
+        quantise(1, "first")
+        scatter_vector(0, 128, 256)
+        scatter_scalar(1, 0, 128)
         scatter_scalar(2, 0, 256)
-        scatter_scalar(3, 0, 256)
         two_blocks(1, 0, 2)
         quantise(2, None)
         two_blocks(1, 2, 3)
         quantise(3, "hcol2")
-        scatter_scalar(1, 256, 512)
+        scatter_scalar(1, 128, 512)
+        scatter_scalar(3, 0, 256)
         scatter_vector(0, 256, 512)
         two_blocks(2, 0, 4)
         two_blocks(3, 0, 5)

@@ -91,7 +91,7 @@ def tile_moe_adp_silu_kernel(
             nc.sync.dma_start(ws[r:P:32, :].bitcast(I32), w_scales[0, r:16:4, :].bitcast(I32))
         wb = [wb0[:], wb1[:]] + load_many(wb_words[2:E, 0], "wb_rest")
 
-        wa_dealt = [held([P, H], I32, "wa_dealt%d" % e) for e in range(E)]
+        wa_dealt = {e: held([P, H], I32, "wa_dealt%d" % e) for e in range(E - 1)}
         was_dealt = held([P, H], U8, "was_dealt")
 
         def deal_words(e, copy):
@@ -224,7 +224,8 @@ def tile_moe_adp_silu_kernel(
         first_layer(1, 1)
         deal_words(2, nc.vector.tensor_copy)
         quantise_chunk(1, placed([P, P], U32, "hq_second", 6144))
-        deal_words(3, nc.vector.tensor_copy)
+        wa_dealt[3] = placed([P, H], I32, "wa_dealt3", 256)
+        deal_words(3, nc.gpsimd.tensor_copy)
         first_layer(2, 2)
         first_layer(3, 3)
         first = held([P, 1, P], F32, "first")
@@ -233,12 +234,12 @@ def tile_moe_adp_silu_kernel(
         nc.vector.tensor_copy(win[0][:].indirect(offsets[:, 0:LIST_COLS]), first[:, 0, :])
         first_layer(4, 4)
         first_layer(5, 5)
-        first_layer(6, 0)
+        scatter_scalar(1, 0, 128)
         second_layer(0, P, C, 0, 4, 6, g0[:, P:C])
+        first_layer(6, 0)
         first_layer(7, 7)
         quantise(1, "first")
         scatter_vector(0, 128, 256)
-        scatter_scalar(1, 0, 128)
         scatter_scalar(2, 0, 256)
         two_blocks(1, 0, 2)
         quantise(2, None)

@@ -45,8 +45,6 @@ def tile_moe_adp_silu_kernel(
         wbs = held([P, N], U8, "wbs")
         ws = held([P, N], U8, "ws")
         nc.gpsimd.memset(was[:].bitcast(I32), 0)
-        nc.vector.memset(wbs[:].bitcast(I32), 0)
-        nc.vector.memset(ws[:].bitcast(I32), 0)
 
         def load_adapter_plane(plane, scales, q, queue):
             queue.dma_start(
@@ -207,7 +205,7 @@ def tile_moe_adp_silu_kernel(
 
         whole = ((0, BANK, False), (BANK, T, True))
         halves = ((0, BANK, True), (BANK, T, True))
-        last = ((0, 256, True), (256, BANK, True), (BANK, 832, True), (832, T, True))
+        last = ((0, BANK, True), (BANK, 832, True), (832, T, True))
 
         warm = held([P, 2], F32, "warm")
         nc.vector.memset(warm[:, 0:1], 0.0)

@@ -205,6 +205,7 @@ def tile_moe_adp_silu_kernel(
 
         whole = ((0, BANK, False), (BANK, T, True))
         halves = ((0, BANK, True), (BANK, T, True))
+        early_start = ((0, 256, True), (256, BANK, True), (BANK, T, True))
         last = ((0, BANK, True), (BANK, 832, True), (832, T, True))
 
         warm = held([P, 2], F32, "warm")
@@ -257,6 +258,6 @@ def tile_moe_adp_silu_kernel(
         scatter_scalar(3, 640, 1024)
         finish(0, (6, 7), whole)
         scatter_vector(1, 512, 1024)
-        finish(2, (6, 7), halves)
+        finish(2, (6, 7), early_start)
         finish(1, (0, 1), halves)
         finish(3, (6, 7), last)

from contextlib import ExitStack

import concourse.mybir as mybir

K, T, E, C, H, N = 512, 1024, 4, 256, 512, 512
FLOPS = 2 * K * N * T + 2 * K * H * E * C + 2 * H * N * E * C

F32 = mybir.dt.float32
BF16 = mybir.dt.bfloat16
I32 = mybir.dt.int32
U32 = mybir.dt.uint32
U16 = mybir.dt.uint16
U8 = mybir.dt.uint8
FP8X4 = mybir.dt.float8_e4m3fn_x4
FP4X4 = mybir.dt.float4_e2m1fn_x4
ACT = mybir.ActivationFunctionType
ALU = mybir.AluOpType

P = 128
BANK = 512
CHUNKS = E * C // P
LIST_COLS = P // 16


def tile_moe_adp_silu_kernel(
    tc, x_words, x_scales, w_words, w_scales, wa_words, wa_scales, wb_words, wb_scales, gate, offs, out
):
    nc = tc.nc
    with ExitStack() as ctx:
        keep = ctx.enter_context(tc.tile_pool(name="keep", bufs=1))
        shared = ctx.enter_context(tc.tile_pool(name="shared", bufs=1))
        psum = ctx.enter_context(tc.psum_pool(name="psum", bufs=1))

        def held(shape, dtype, name, tag=None):
            return keep.tile(shape, dtype, name=name, tag=tag or name, align_bytes=64)

        def placed(shape, dtype, name, offset):
            return shared.tile(shape, dtype, name=name, tag=name, align_bytes=64, offset=offset)

        offsets = keep.tile([P, E * C // 16], U16, name="offsets")
        nc.sync.dma_start(offsets[:], offs)

        xs = held([P, T], U8, "xs")
        was = held([P, H], U8, "was")
        wbs = held([P, N], U8, "wbs")
        ws = held([P, N], U8, "ws")
        nc.gpsimd.memset(was[:].bitcast(I32), 0)

        def load_adapter_plane(plane, scales, q, queue):
            queue.dma_start(
                plane[32 * q : 32 * q + 16, :].bitcast(I32), scales[:, 0, 4 * q : 4 * q + 4, :].bitcast(I32)
            )

        def load_words(src, name, offset=None):
            words = held([P, src.shape[1]], I32, name) if offset is None else placed([P, src.shape[1]], I32, name, offset)
            nc.sync.dma_start(words[:], src.rearrange("p c d -> p (c d)").bitcast(I32))
            return words

        def load_many(src, name):
            words = held([P, src.shape[0], src.shape[2]], I32, name)
            nc.sync.dma_start(words[:], src.rearrange("e p c d -> p e (c d)").bitcast(I32))
            return [words[:, e, :] for e in range(src.shape[0])]

        for q in range(4):
            four_rows = x_scales[0][4 * q : 4 * q + 4, :].bitcast(I32)
            (nc.scalar if q % 2 else nc.sync).dma_start(
                xs[32 * q : 32 * q + 32, :].bitcast(I32),
                four_rows.unsqueeze(0).broadcast_to([8, 4, T // 4]),
            )
        load_adapter_plane(was, wa_scales, 0, nc.scalar)
        wa0 = load_words(wa_words[0, 0], "wa0")
        xw = load_words(x_words[0], "xw")
        for q in range(1, 4):
            load_adapter_plane(was, wa_scales, q, nc.sync)
        wa1 = load_words(wa_words[1, 0], "wa1", 2048)
        wb0 = load_words(wb_words[0, 0], "wb0")
        for q in range(4):
            load_adapter_plane(wbs, wb_scales, q, nc.sync)
        wa2 = load_words(wa_words[2, 0], "wa2", 6144)
        wa = [wa0[:], wa1[:], wa2[:], load_words(wa_words[3, 0], "wa3")[:]]
        g0 = held([P, C], F32, "g0")
        nc.sync.dma_start(g0[:], gate[:, 0:C])
        g1 = held([P, (E - 1) * C], F32, "g1")
        nc.sync.dma_start(g1[:], gate[:, C : E * C])
        wb1 = load_words(wb_words[1, 0], "wb1")
        ww = held([P, 2 * N], U8, "ww")
        nc.sync.dma_start(ww[:].bitcast(I32), w_words[0].bitcast(I32))
        for r in range(4):
            nc.sync.dma_start(ws[r:P:32, :].bitcast(I32), w_scales[0, r:16:4, :].bitcast(I32))
        wb = [wb0[:], wb1[:]] + load_many(wb_words[2:E, 0], "wb_rest")

        wa_dealt = {e: held([P, H], I32, "wa_dealt%d" % e) for e in range(E - 1)}
        was_dealt = held([P, H], U8, "was_dealt")

        def deal_words(e, copy):
            copy(
                wa_dealt[e][:].bitcast(U32).rearrange("p (d g m) -> p g d m", d=4, m=4),
                wa[e].bitcast(U32).rearrange("p (g m d) -> p g d m", d=4, m=4),
            )

        def deal_scales():
            for d0 in (0, 2):
                nc.gpsimd.tensor_copy(
                    was_dealt[:].rearrange("p (d m) -> p d m", d=4)[:, d0 : d0 + 2, :],
                    was[:].rearrange("p (m d) -> p d m", d=4)[:, d0 : d0 + 2, :],
                )

        def entries(e0, e1):
            return offsets[:, e0 * C // 16 : e1 * C // 16]

        banks = [psum.tile([P, BANK], F32, name="bank%d" % b) for b in range(8)]
        xg, xsg = {}, {}
        hq = {}
        hs = [held([P, C], U8, "hs%d" % e) for e in range(E)]
        win = [held([P, T], F32, "win%d" % nb) for nb in range(4)]
        gated = held([P, 4, E * C], F32, "gated")
        hcol = {}

        def gather_scales(e0, e1, tile):
            nc.vector.tensor_copy(tile[:], xs[:].indirect(entries(e0, e1)))
            for e in range(e0, e1):
                xsg[e] = tile[:, (e - e0) * C : (e - e0 + 1) * C]

        def gather_words(c0, c1, tile):
            nc.vector.tensor_copy(
                tile, xw[:].bitcast(U32).indirect(offsets[:, c0 * LIST_COLS : c1 * LIST_COLS])
            )
            for c in range(c0, c1):
                xg[c] = tile[:, (c - c0) * P : (c - c0 + 1) * P]

        def first_layer(c, b):
            e, half = divmod(c, 2)
            if half == 0:
                if e < 2:
                    hcol[e] = placed([P, 4 * C], BF16, "hcol%d" % e, (256, 3328)[e])
                else:
                    hcol[e] = held([P, 4 * C], BF16, "hcol%d" % e)
            h = hcol[e][:, half * BANK : (half + 1) * BANK]
            for d in range(4):
                part = slice(d * P, (d + 1) * P)
                nc.tensor.matmul_mx(
                    banks[b][:, part], lhsT=wa_dealt[e][:, part].bitcast(FP8X4), lhsT_scale=was_dealt[4 * e : P, part],
                    rhs=xg[c].bitcast(FP8X4), rhs_scale=xsg[e][:, half * P : (half + 1) * P], start=True, stop=True,
                )
            nc.scalar.activation(
                h.rearrange("p (s d) -> p s d", d=4),
                banks[b][:].rearrange("p (d s) -> p s d", d=4),
                ACT.Silu,
            )

        def quantise(e, buffer):
            hq[e] = placed([P, C], U32, "hq2", 3328) if e == 2 else held([P, C], U32, "hq%d" % e, buffer)
            nc.vector.quantize_mx(hq[e][:].bitcast(FP8X4), hs[e][:], hcol[e][:])

        def quantise_chunk(c, codes):
            hq[0, c] = codes
            nc.vector.quantize_mx(
                codes[:].bitcast(FP8X4), hs[0][:, c * P : (c + 1) * P], hcol[0][:, c * BANK : (c + 1) * BANK]
            )

        def second_layer(e, s0, s1, nb0, nb1, b, g, dst=None):
            width = s1 - s0
            codes = hq[e][:] if e else hq[0, s0 // P][:]
            if dst is None:
                dst = gated[:, nb0:nb1, e * C + s0 : e * C + s1]
            for nb in range(nb0, nb1):
                rows = slice(nb * P, (nb + 1) * P)
                nc.tensor.matmul_mx(
                    banks[b][:, (nb - nb0) * width : (nb - nb0 + 1) * width], lhsT=wb[e][:, rows].bitcast(FP8X4),
                    lhsT_scale=wbs[4 * e : P, rows], rhs=codes.bitcast(FP8X4), rhs_scale=hs[e][:, s0:s1],
                    start=True, stop=True,
                )
            nc.vector.tensor_tensor(
                dst, banks[b][:, 0 : (nb1 - nb0) * width].rearrange("p (j s) -> p j s", s=width),
                g.unsqueeze(1).broadcast_to([P, nb1 - nb0, width]), ALU.mult,
            )

        def two_blocks(e, nb0, b):
            second_layer(e, 0, C, nb0, nb0 + 2, b, g1[:, (e - 1) * C : e * C])

        def scatter_scalar(nb, j0, j1):
            nc.scalar.activation(win[nb][:].indirect(offsets[:, j0 // 16 : j1 // 16]), gated[:, nb, j0:j1], ACT.Copy)

        def scatter_vector(nb, j0, j1):
            nc.vector.tensor_copy(win[nb][:].indirect(offsets[:, j0 // 16 : j1 // 16]), gated[:, nb, j0:j1])

        def finish(nb, two_banks, cuts):
            for th, b in enumerate(two_banks):
                cols = slice(th * BANK, (th + 1) * BANK)
                nc.tensor.matmul_mx(
                    banks[b][:], lhsT=ww[:, 2 * nb * P : 2 * (nb + 1) * P].bitcast(FP4X4),
                    lhsT_scale=ws[:, nb * P : (nb + 1) * P],
                    rhs=xw[:, cols].bitcast(FP8X4), rhs_scale=xs[:, cols], start=True, stop=True,
                )
            res = held([P, T], F32, "res%d" % nb)
            done = 0
            for col, end, store in cuts:
                th, off = divmod(col, BANK)
                nc.vector.tensor_tensor(
                    res[:, col:end], banks[two_banks[th]][:, off : off + end - col], win[nb][:, col:end], ALU.add
                )
                if store:
                    nc.sync.dma_start(out[nb * P : (nb + 1) * P, done:end], res[:, done:end])
                    done = end

        whole = ((0, BANK, False), (BANK, T, True))
        halves = ((0, BANK, True), (BANK, T, True))
        early_start = ((0, 256, True), (256, BANK, True), (BANK, T, True))
        last = ((0, BANK, True), (BANK, 832, True), (832, T, True))

        warm = held([P, 2], F32, "warm")
        nc.vector.memset(warm[:, 0:1], 0.0)
        nc.scalar.activation(warm[:, 1:2], warm[:, 0:1], ACT.Silu)
        gather_scales(0, 3, held([P, 3 * C], U8, "xsg_first"))
        for e in range(2):
            deal_words(e, nc.scalar.copy)
        deal_scales()
        for c0, c1 in ((0, 1), (1, 2), (2, 4), (4, 8)):
            gather_words(c0, c1, held([P, (c1 - c0) * P], U32, "xg%d" % c0)[:])
        gather_scales(3, 4, placed([P, C], U8, "xsg_last", 2304))
        first_layer(0, 0)
        quantise_chunk(0, held([P, P], U32, "hq_first"))
        first_layer(1, 1)
        deal_words(2, nc.vector.tensor_copy)
        quantise_chunk(1, placed([P, P], U32, "hq_second", 6144))
        wa_dealt[3] = placed([P, H], I32, "wa_dealt3", 256)
        deal_words(3, nc.gpsimd.tensor_copy)
        first_layer(2, 2)
        first_layer(3, 3)
        first = held([P, 1, P], F32, "first")
        second_layer(0, 0, P, 0, 1, 6, g0[:, 0:P], first[:])
        second_layer(0, 0, P, 1, 4, 7, g0[:, 0:P])
        nc.vector.tensor_copy(win[0][:].indirect(offsets[:, 0:LIST_COLS]), first[:, 0, :])
        first_layer(4, 4)
        first_layer(5, 5)
        scatter_scalar(1, 0, 128)
        second_layer(0, P, C, 0, 4, 6, g0[:, P:C])
        first_layer(6, 0)
        first_layer(7, 7)
        quantise(1, "first")
        scatter_vector(0, 128, 256)
        scatter_scalar(2, 0, 256)
        two_blocks(1, 0, 2)
        quantise(2, None)
        two_blocks(1, 2, 3)
        quantise(3, "hcol2")
        scatter_scalar(1, 128, 512)
        scatter_scalar(3, 0, 256)
        scatter_vector(0, 256, 512)
        two_blocks(2, 0, 4)
        two_blocks(3, 0, 5)
        two_blocks(2, 2, 2)
        scatter_vector(0, 512, 1024)
        two_blocks(3, 2, 3)
        scatter_scalar(2, 256, 640)
        scatter_scalar(3, 256, 640)
        scatter_scalar(2, 640, 1024)
        scatter_scalar(3, 640, 1024)
        finish(0, (6, 7), whole)
        scatter_vector(1, 512, 1024)
        finish(2, (6, 7), early_start)
        finish(1, (0, 1), halves)
        finish(3, (6, 7), last)
